import numpy as np, ml_dtypes
CORES = [2,6,10,14,18,22,26,30]
N = 8
BF = ml_dtypes.bfloat16
def gentries(a):
    return np.ascontiguousarray(a.reshape(8, 16, -1).transpose(0, 2, 1)).reshape(8, -1)
def gtable(e):
    e = np.asarray(e); return np.ascontiguousarray(e.reshape(8, -1, 16).transpose(0, 2, 1)).reshape(128, -1).astype(np.int32)
V, P, T, TL, Q, M = 2560, 192, 4, 2, 8, 4096
def money(rng, base):
    v = base + rng.integers(-3, 4, base.shape[:2] + (16, base.shape[-1]))
    return np.clip(np.floor(v), 0, 15).astype(np.int64)
def parts(rng):
    x = money(rng, 16 * rng.random((N, 8, 1, V)) ** rng.choice(np.array([2.0, 3.0, 5.0]), (N, 8, 1, 1)))
    price = money(rng, 16 * rng.random((N, 8, 1, P)))
    pool = rng.integers(0, V, (N, 8, 64))
    pop = np.take_along_axis(pool, rng.integers(0, 64, (N, 8, 16 * V)), 2).reshape(N, 8, 16, V)
    kin = np.where(rng.random((N, 8, 16, V)) < 0.15, pop, rng.integers(0, V, (N, 8, 16, V)))
    few = np.take_along_axis(pool, rng.integers(0, 48, (N, 8, P)), 2)
    own = np.where(rng.random((N, 8, P)) < 0.5, few, rng.integers(0, V, (N, 8, P)))
    hold = rng.integers(0, V, (N, 8, P)); wall = rng.integers(0, 2, (N, 8, P)); wt = rng.integers(0, 256, (N, 8, 16))
    return x, kin, own, hold, wall, price, wt
def pack(x, kin, own, hold, wall, price, wt):
    return {"x": np.ascontiguousarray(x.reshape(N, 128, V)).astype(np.float32).astype(BF), "kin": np.ascontiguousarray(kin.reshape(N, 128, V)).astype(np.int32),
            "own": np.stack([gtable(a) for a in own]), "hold": np.stack([gtable(a) for a in hold]), "wall": np.stack([gtable(a) for a in wall]),
            "price": np.ascontiguousarray(price.reshape(N, 128, P)).astype(np.float32).astype(BF), "wt": np.ascontiguousarray(wt.reshape(N, 128, 1)).astype(np.int32)}
def setup_inputs(rng):
    return pack(*parts(rng))
def setup_inputs_alike(rng):
    x, kin, own, hold, wall, price, wt = parts(rng)
    kin[:, 0] = kin[:, 0, :, :1].copy()
    kin[:, 1] = kin[:, 1, :1, :].copy()
    own[:, 2] = own[:, 2, :1].copy()
    kin[:, 3] = rng.integers(0, V, (N, 1, 1))
    own[:, 4] = np.take_along_axis(rng.integers(0, V, (N, 3)), rng.integers(0, 3, (N, P)), 1)
    own[:, 5] = np.argsort(rng.random((N, V)), axis=-1)[:, :P]; price[:, 5] = 15; x[:, 5] = 0; x[:, 5, 3] = rng.integers(0, 2, (N, V))
    own[1::2, 5, P - 1] = own[1::2, 5, 0]; price[1::2, 5, 3, P - 1] = 0
    x[:, 6] = x[:, 6, :, :1].copy(); hold[:, 6] = hold[:, 6, :1].copy()
    kin[:, 7] = rng.choice(np.array([0, 1, V - 2, V - 1]), (N, 16, V)); own[:, 7] = rng.choice(np.array([0, V - 1]), (N, P))
    return pack(x, kin, own, hold, wall, price, wt)
def setup_inputs_corners(rng):
    x, kin, own, hold, wall, price, wt = parts(rng); q = rng.permutation(8); a = np.arange(V)
    for r in range(N):
        g = q[0]; x[r, g] = 0; price[r, g] = 15; kin[r, g] = np.minimum(a + 1, V - 1); own[r, g, ::8] = V - 1; own[r, g, 1::8] = 0; own[r, g, 2::8] = V - 2
        g = q[1]; kin[r, g] = a; own[r, g, :2] = 0; own[r, g, P - 2:] = V - 1
        g = q[2]; price[r, g] = 0; wt[r, g] = 255 * (r % 2)
        g = q[3]; x[r, g] = 15; price[r, g] = 15; wt[r, g] = 255; wall[r, g] = 1; hold[r, g, ::2] = V - 1; hold[r, g, 1::4] = 0
        kin[r, g, 0] = rng.permutation(V); own[r, g] = rng.permutation(V)[:P]
        if r % 2 == 1: own[r, g, P - 1] = own[r, g, 0]; price[r, g, :, P - 1] = 7
        g = q[4 + r % 4]; kin[r, g] = rng.integers(0, 2, (16, V)) * (V - 1); own[r, g] = rng.integers(0, 2, P) * (V - 1)
        g = q[4 + (r + 1) % 4]; wall[r, g] = 0; wt[r, g] = 0
        g = q[4 + (r + 2) % 4]; x[r, g] = 0; x[r, g, :, 0] = 15; price[r, g] = 15; kin[r, g] = np.maximum(a - 1, 0); own[r, g] = rng.integers(0, 2 * T, P)
        g = q[4 + (r + 3) % 4]; wall[r, g] = 1; hold[r, g] = rng.integers(0, 2, P) * (V - 1); kin[r, g, :, V - 1] = 0; kin[r, g, :, 0] = V - 1
    return pack(x, kin, own, hold, wall, price, wt)
def setup_inputs_ends(rng):
    def rec(n):
        k = rng.random((N, 8, 1, n)); el = rng.integers(0, 2, (N, 8, 16, n))
        return 15 * np.where(k < 0.35, 0, np.where(k < 0.7, 1, el))
    x = rec(V); price = rec(P)
    kin = np.where(rng.random((N, 8, 1, V)) < 0.7, rng.integers(0, 2, (N, 8, 16, V)) * (V - 1), rng.integers(0, V, (N, 8, 16, V)))
    own = np.where(rng.random((N, 8, P)) < 0.7, rng.integers(0, 2, (N, 8, P)) * (V - 1), rng.integers(0, V, (N, 8, P)))
    hold = np.where(rng.random((N, 8, P)) < 0.75, rng.integers(0, 2, (N, 8, P)) * (V - 1), rng.integers(0, V, (N, 8, P)))
    wall = rng.integers(0, 2, (N, 8, P)); wt = 255 * rng.integers(0, 2, (N, 8, 16)); wt[N - 1, 7] = 255; wt[N - 1, 0, 0] = 0
    for g in range(8):
        x[:, g, :, 0] = (0, 15, 0, 15)[g % 4]; x[:, g, :, V - 1] = (15, 0, 0, 15)[g % 4]
    x[:, 7, :, 0] = 0; x[:, 7, :, 4] = 0; x[:, 7, :, V - 1] = 15
    kin[:, 7, :, V - 1] = V - 1; kin[:, 7, :, 0] = 0; kin[:, 7, 0::2, 2] = 4; kin[:, 7, 1::2, 2] = 0
    own[:, 7, 0] = V - 1; price[:, 7, :, 0] = 0; wall[:, 7, 0] = 0
    own[:, 7, P - 8:] = V - 1; hold[:, 7, P - 8:] = V - 1; wall[:, 7, P - 8:] = 1
    own[:, 7, P - 16:P - 8] = 0; own[:, 7, P - 24:P - 16] = 2; price[:, 7, :, P - 24:] = 15
    x[:, 5, :, V - 2] = 0; kin[:, 5, :, V - 2] = V - 2; own[:, 5, P - 2:] = V - 2; wall[:, 5, P - 2:] = 0; price[:, 5, :, P - 2:] = 15
    y = 15 >> (T // TL); s = [a for a in range(V, 61201, M) if a % y == 0][0] // y
    for r in range(N):
        wt[r, 5] = rng.permutation(np.array([255] * (s // 255) + [s % 255] + [0] * (15 - s // 255)))
    return pack(x, kin, own, hold, wall, price, wt)
def setup_inputs_spread(rng):
    def skew(top, p, *shape):
        return np.minimum(np.floor(top * rng.random(shape) ** p), top - 1).astype(np.int64)
    x = skew(16, np.exp2(rng.integers(-2, 4, (N, 8, 1, V)) + rng.integers(0, 2, (N, 8, 16, 1))), N, 8, 16, V)
    price = skew(16, np.exp2(rng.integers(-3, 3, (N, 8, 1, P)) + rng.integers(0, 2, (N, 8, 16, 1))), N, 8, 16, P)
    kin = skew(V, np.exp2(rng.integers(-1, 4, (N, 8, 16, 1))), N, 8, 16, V)
    own = skew(V, np.exp2(rng.integers(-2, 4, (N, 8, 1))), N, 8, P); hold = skew(V, np.exp2(rng.integers(-3, 4, (N, 8, 1))), N, 8, P)
    wall = (rng.random((N, 8, P)) < rng.choice(np.array([0.1, 0.5, 0.9]), (N, 8, 1))).astype(np.int64)
    wt = np.minimum(np.floor(np.exp2(8.02 * rng.random((N, 8, 16)))).astype(np.int64) - 1, 255)
    return pack(x, kin, own, hold, wall, price, wt)
def setup_inputs_ties(rng):
    x, kin, own, hold, wall, price, wt = parts(rng)
    n = Q - 2 + rng.integers(0, 2, (N, 8, 1, V)) + (rng.random((N, 8, 1, V)) < 0.03) + (np.arange(8) % 2).reshape(1, 8, 1, 1)
    x = 6 + (np.argsort(rng.random((N, 8, 16, V)), axis=2) < n).astype(np.int64)
    price = np.broadcast_to(rng.choice(np.array([6, 7, 7, 7, 7, 7, 7, 8]), (N, 8, 1, P)), (N, 8, 16, P)).copy()
    i = int(rng.integers(0, 16)); x[:, 6, :, V - 1] = 11; x[:, 6, i, V - 1] = 1
    k6 = kin[:, 6]; k6[k6 == V - 1] = V - 2; kin[:, 6, :, V - 1] = V - 1
    o6 = own[:, 6]; o6[o6 == V - 1] = 0; own[:, 6, P - 2:] = V - 1; wall[:, 6] = 0; price[:, 6, :, P - 2:] = 15
    ya, yz = 15, 15
    for _ in range(T // TL):
        ya, yz = (ya + 11) >> 1, (yz + 1) >> 1
    for r in range(N):
        s = 32768 if r % 2 == 0 else 7 * M
        c = [a for a in range(256) if (s - yz * a) % ya == 0][0]; rest = (s - yz * c) // ya
        wt[r, 6] = np.insert(rng.permutation(np.array([255] * (rest // 255) + [rest % 255] + [0] * (14 - rest // 255))), i, c)
    return pack(x, kin, own, hold, wall, price, wt)
def check_inputs(d):
    bad = []
    for k, hi in (("x", 15), ("kin", V - 1), ("own", V - 1), ("hold", V - 1), ("wall", 1), ("price", 15), ("wt", 255)):
        a = np.asarray(d[k]).astype(np.float64)
        if not (np.min(a) >= 0 and np.max(a) <= hi): bad.append("range of " + k)
        elif np.any(a != np.floor(a)): bad.append("whole numbers in " + k)
    return bad
def reference(x, kin, own, hold, wall, price, wt):
    X = x.astype(np.float32).astype(np.int32).reshape(N, 8, 16, V); K = kin.astype(np.int64).reshape(N, 8, 16, V)
    heir = np.tile(np.arange(V), (N, 8, 1)); lane = np.arange(P)
    e = np.stack([gentries(a) for a in own]).astype(np.int64); h = np.stack([gentries(a) for a in hold]).astype(np.int64); wl = np.stack([gentries(a) for a in wall])
    y = price.astype(np.float32).astype(np.int32).reshape(N, 8, 16, P); w = wt.astype(np.int64).reshape(N, 8, 16, 1)
    for t in range(T):
        for r in range(N):
            s = (r + t) % N; XS, KS, HS, ys, hs, es = X[s], K[s], heir[s], y[r], h[r], e[r].copy()
            c = np.take_along_axis(KS, es[:, None, :], 2)
            d = np.take_along_axis(XS, c.reshape(8, 1, 16 * P), 2).reshape(8, 16, 16, P) - ys[:, :, None, :]
            solvent = np.add.reduce((d >= 0).astype(np.int32), axis=1) >= Q; score = np.add.reduce(np.abs(d), axis=1)
            offers = np.any(solvent, axis=1)
            k = np.where(offers, np.argmax(solvent, axis=1), np.argmin(score, axis=1))
            b = np.take_along_axis(c, k[:, None, :], 1)[:, 0]
            key = np.where(offers, b, V + es)
            first = np.argmax(key[:, :, None] == key[:, None, :], axis=2) == lane
            fg, fp = np.nonzero(first & ~offers); ef, f = es[fg, fp], b[fg, fp]
            KS[fg, 1::2, ef] = KS[fg, 1::2, f]
            HS[fg, ef] = f
            wg, wp = np.nonzero(first & offers); cw = b[wg, wp]
            XS[wg, :, cw] = np.maximum(XS[wg, :, cw] - (ys[wg, :, wp] >> 2), 0)
            ys[wg, :, wp] = np.minimum(ys[wg, :, wp] + 1, 15); hs[wg, wp] = cw
            es = np.take_along_axis(HS, es, 1)
            if t % TL == TL - 1:
                es = np.where(wl[r] == 1, hs, es)
                y[r] = (ys + np.take_along_axis(XS, es[:, None, :], 2)) >> 1
                u = np.add.reduce(w[s] * y[r], axis=1) & (M - 1)
                h[r] = np.where(u >= V, u - V, u)
            e[r] = es
    yk = np.add.reduce(K * np.arange(1, 17).reshape(1, 1, 16, 1), axis=2)
    return {"yx": X.reshape(N, 128, V).astype(np.float32).astype(BF), "yk": yk.astype(np.float32), "yh": heir.astype(np.float32), "yo": e.astype(np.float32), "yt": h.astype(np.float32)}

@@ -1,0 +1,523 @@
+from concourse.mybir import dt, AluOpType, AxisListType, ActivationFunctionType
+
+V, P, NS, FB = 2560, 192, 4, 2752
+W = V + P
+CH = [(0, 7), (7, 12), (12, 15), (15, 16)]
+C0 = 7
+SG = [(0, 1, None, None, None), (1, 3, 0, 0, None), (3, 7, 3, None, 3), (7, 10, 7, None, None), (10, 12, 10, None, 7),
+      (12, 15, 12, None, 12), (15, 16, 15, None, 15)]
+BIG, LOW = 2.0 ** 21, 2.0 ** 23
+A = AluOpType
+F = ActivationFunctionType
+
+SCRATCH = {}
+
+
+def _b(name, cols, d, where="sbuf"):
+    SCRATCH[name] = (where, [128] + (cols if isinstance(cols, list) else [cols]), d)
+
+
+for _n, _c in (("Kw", W), ("Hw", W), ("Yw", W), ("ramp", 5312), ("cb", 224), ("tr", 416), ("cTf", 192), ("colj", 16),
+               ("jlrow", 192), ("C3", 192), ("c3t", 192), ("sc3", 192), ("IDF", 128), ("mrow", 128),
+               ("K4", 192), ("K4c", 192), ("keys", 192), ("t1", 192), ("sc", 192), ("bF", 192), ("Fo", 192), ("ce", 192),
+               ("hm", 192), ("DUM", 24), ("bxk", 24), ("dm0", 12), ("cols", 16), ("eF", 12), ("eB", 12), ("fe", 12),
+               ("dk", 12), ("dkB", 12), ("ek", 12), ("bx", 12), ("oX", 12), ("bk", 12), ("oK", 12), ("wF", 12), ("th", 12), ("hW", 12),
+               ("Aw", 12), ("nw", 12), ("m12", 12), ("eh", 12), ("fin", 24), ("rfin", 24), ("outf", 384), ("WKB", 128),
+               ("yv2", 192), ("yv3", 192), ("gg", 12)):
+    _b(_n, _c, "float32")
+for _n, _c in (("Xw", W), ("d", 3072), ("aa", 1344), ("sg", 1344), ("as", 3456), ("KZ", 216), ("eq", [12, 192]), ("LA", 2048), ("LB", 2048), ("lv", 128), ("BO", 128),
+               ("U", 128), ("BW", 128), ("grow", 128), ("irow", 128), ("gt", 128), ("KC", 192), ("zero", 192), ("q", 192), ("ID", 128),
+               ("NID", 128), ("ZB", 96), ("Xb", 192), ("xr", 192), ("pw", 192), ("pj", 192), ("wb", 192), ("ph", 192)):
+    _b(_n, _c, "bfloat16")
+for _n, _c in (("ki", V), ("own_s", 12), ("hold_s", 12), ("wall_s", 12), ("wt_s", 1), ("ci", 4), ("kI", 12), ("jI", 12),
+               ("KEY", 12), ("bI", 12), ("sI", 12), ("uI", 12)):
+    _b(_n, _c, "int32")
+for _n, _c in (("SELu", 12), ("cTu", 192), ("bU", 12), ("dkU", 12), ("dkf", 192), ("of0", 24), ("of1", 24), ("wU", 12), ("rU", 24)):
+    _b(_n, _c, "uint16")
+for _t in range(NS):
+    _b("E%d" % _t, 12, "uint16")
+    _b("EO%d" % _t, 12, "uint16")
+    _b("PR%d" % _t, 768, "bfloat16")
+    _b("PO%d" % _t, 192, "bfloat16")
+    _b("HW%d" % _t, 48, "float32")
+for _n, _c in (("Z0", 512), ("Z1", 512), ("Z2", 512), ("CN", 512), ("SS", 512), ("XB", 512), ("Y0", 512), ("Y1", 512)):
+    _b(_n, _c, "float32", "psum")
+
+SEMAPHORES = ["qV", "qS", "qT", "qG", "ls"] + ["dm%d" % i for i in range(24)] + ["r%s%d" % (a, t) for a in "eph" for t in range(1, NS)] + ["rf", "ro1"]
+
+
+def rank_program(g, core, T, topo):
+    rank = T.rank_of(core)
+    if rank is None:
+        return
+    cores = T.cores
+    n = len(cores)
+    eng = {"V": g.vector, "S": g.scalar, "T": g.tensor, "G": g, "Y": g.sync}
+    cnt = {"V": 0, "S": 0, "T": 0, "G": 0}
+    log = {}
+    known = {q: {} for q in "VSTGY"}
+    clock = {}
+    ndma = [0]
+    psum = ("Z0", "Z1", "Z2", "CN", "SS", "XB", "Y0", "Y1")
+
+    def B(name, lo=0, hi=None, step=1, parts=None):
+        t = T[name]
+        if hi is None:
+            hi = SCRATCH[name][1][1]
+        if parts is None:
+            ap = t[:, lo:hi] if step == 1 else t[:, lo:hi:step]
+        else:
+            ap = t[parts[0]:parts[1]:parts[2], lo:hi]
+        return (ap, [(name, lo, hi)], [])
+
+    def IND(win, off):
+        return (win[0].indirect(off[0]), win[1], off[1])
+
+    def ext(ap):
+        return (ap, [], [])
+
+    def need(q, reads, writes, acc):
+        want = {}
+        for regs, wr in ((reads, False), (writes, True)):
+            for nm, lo, hi in regs:
+                if nm in psum:
+                    lo, hi = 0, 512
+                for e in log.get(nm, []):
+                    if e[0] < hi and lo < e[1] and (wr or e[3]):
+                        if e[4] == q and (not e[3] or acc):
+                            continue
+                        s, v = e[2]
+                        if want.get(s, 0) < v:
+                            want[s] = v
+        for s in sorted(want):
+            v = want[s]
+            if known[q].get(s, 0) >= v:
+                continue
+            eng[q].wait_ge(T.sem[s], v)
+            for k, w in clock.get((s, v), {}).items():
+                if known[q].get(k, 0) < w:
+                    known[q][k] = w
+            known[q][s] = max(known[q].get(s, 0), v)
+
+    def note(q, tok, reads, writes):
+        clock[tok] = dict(known[q])
+        for regs, wr in ((reads, False), (writes, True)):
+            for nm, lo, hi in regs:
+                if nm in psum:
+                    lo, hi = 0, 512
+                lst = log.get(nm, [])
+                if wr:
+                    lst = [e for e in lst if not (lo <= e[0] and e[1] <= hi)]
+                else:
+                    lst = [e for e in lst if not (e[4] == q and not e[3] and lo <= e[0] and e[1] <= hi)]
+                lst.append([lo, hi, tok, wr, q])
+                log[nm] = lst
+
+    def op(q, fn, out, ins, acc=False, done=True):
+        reads = list(out[2])
+        for i in ins:
+            reads += i[1] + i[2]
+        need(q, reads, out[1], acc)
+        inst = fn()
+        s = "q" + q
+        if done:
+            cnt[q] += 1
+            inst.then_inc(T.sem[s], 1)
+            note(q, (s, cnt[q]), reads, out[1])
+        else:
+            note(q, (s, cnt[q] + 1), reads, out[1])
+
+    def dma(q, out, in_):
+        need(q, in_[1], out[1], False)
+        s = "dm%d" % ndma[0]
+        ndma[0] += 1
+        eng[q].dma_start(out[0], in_[0]).then_inc(T.sem[s], 16)
+        known[s] = dict(known[q])
+        note(s, (s, 16), in_[1], out[1])
+
+    sent = [0]
+
+    def send(dst, out, in_, sem, ne):
+        need("G", in_[1], [], False)
+        rid, pid, _ = topo.addr(dst)
+        es = topo.engines(core, dst)[:ne]
+        g.remote_dma(out[0], in_[0], T.sem[sem], T.sem["ls"], pid, rid, sum(1 << e for e in es))
+        sent[0] += len(es)
+
+    def arrive(name, lo, hi, src, sem, ne):
+        v = len(topo.engines(src, core)[:ne])
+        known[sem] = {}
+        note(sem, (sem, v), [], [(name, lo, hi)])
+
+    def val(x):
+        return x[0] if isinstance(x, tuple) else x
+
+    def opnds(*xs):
+        return [x for x in xs if isinstance(x, tuple)]
+
+    def tcopy(out, in_):
+        op("V", lambda: g.vector.tensor_copy(out[0], in_[0]), out, [in_])
+
+    def tt(out, a, b, o):
+        op("V", lambda: g.vector.tensor_tensor(out[0], a[0], b[0], o), out, [a, b])
+
+    def ts(out, a, s1, o1, s2=None, o2=None):
+        if o2 is None:
+            op("V", lambda: g.vector.tensor_scalar(out[0], a[0], val(s1), None, o1), out, [a] + opnds(s1))
+        else:
+            op("V", lambda: g.vector.tensor_scalar(out[0], a[0], val(s1), val(s2), o1, o2), out, [a] + opnds(s1, s2))
+
+    def scan(out, a, b, o1, o2):
+        op("V", lambda: g.vector.tensor_tensor_scan(out[0], a[0], b[0], 0.0, o1, o2), out, [a, b])
+
+    def fill(out, c):
+        op("V", lambda: g.vector.memset(out[0], c), out, [])
+
+    def act(out, in_, f, bias=0.0, scale=1.0):
+        op("S", lambda: g.scalar.activation(out[0], in_[0], f, bias=val(bias), scale=val(scale)), out, [in_] + opnds(bias, scale))
+
+    def mm(out, l, r, st, sp):
+        op("T", lambda: g.tensor.matmul(out[0], l[0], r[0], st, sp), out, [l, r], acc=not st, done=sp)
+
+    def iota(out, pat, base, cm):
+        op("G", lambda: g.iota(out[0], pat, base, cm, allow_small_or_imprecise_dtypes=True), out, [])
+
+    def col(i):
+        return B("cols", i, i + 1)
+
+    H = V // 2
+    dma("Y", B("own_s"), ext(T.own[:]))
+    dma("Y", B("ki"), ext(T.kin[:]))
+    dma("Y", B("PR0", 0, P), ext(T.price[:]))
+    dma("Y", B("Xw", 0, V), ext(T.x[:]))
+    dma("Y", B("hold_s"), ext(T.hold[:]))
+    dma("Y", B("wall_s"), ext(T.wall[:]))
+    dma("Y", B("wt_s"), ext(T.wt[:]))
+
+    iota(B("cols", 9, 10), [[0, 1]], 0, 1)
+    iota(B("dm0"), [[16, 12]], V, 1)
+    iota(B("grow"), [[1, 8], [0, 16]], 0, 0)
+    iota(B("irow"), [[0, 8], [1, 16]], 0, 0)
+    iota(B("K4"), [[4096, 16], [0, 12]], -65536, 0)
+    iota(B("mrow"), [[1, 128]], 0, 0)
+    iota(B("jlrow"), [[0, 12], [1, 16]], 0, 0)
+    iota(B("lv"), [[1, 8], [16, 16]], 0, 0)
+    iota(B("colj"), [[16, 16]], 0, 0)
+    RB = 1328
+    iota(B("ramp", 0, RB), [[1, RB]], 0, 0)
+    act(B("ramp", RB, 2 * RB), B("ramp", 0, RB), F.Identity, bias=float(RB))
+    act(B("ramp", 2 * RB, 4 * RB), B("ramp", 0, 2 * RB), F.Identity, bias=float(2 * RB))
+    ci = lambda i: B("ci", i, i + 1)
+    fill(B("cb"), 0.0)
+    fill(B("zero"), 0.0)
+    fill(B("ZB"), -128.0)
+    tcopy(ci(0), col(9))
+    ts(ci(1), ci(0), 4, A.logical_shift_right)
+    ts(ci(2), ci(0), 1, A.bitwise_and)
+    ts(ci(3), ci(0), 4, A.logical_shift_right, 1, A.bitwise_and)
+    ts(ci(0), ci(0), 15, A.bitwise_and)
+    tcopy(B("cols", 0, 3), B("ci", 0, 3))
+    tcopy(col(6), ci(3))
+    ts(col(3), col(2), -1.0, A.mult, 1.0, A.add)
+    ts(col(4), col(1), -16.0, A.mult)
+    ts(col(5), col(0), 1.0, A.add)
+    ts(B("DUM", 0, 12), B("dm0"), col(4), A.add)
+    ts(B("DUM", 12, 24), B("dm0"), col(4), A.add)
+    ts(B("m12"), B("DUM", 0, 12), -float(V), A.add)
+    ts(B("kI"), B("m12"), 1.0 / 12.0, A.mult, -11.0 / 24.0, A.add)
+    ts(B("eh"), B("kI"), -12.0, A.mult)
+    tt(B("eh"), B("eh"), B("m12"), A.add)
+    ts(B("jI"), B("eh"), col(6), A.add)
+    ts(B("jI"), B("jI"), 1, A.bitwise_and)
+    ts(B("bx"), B("jI"), 208.0, A.mult)
+    ts(B("bk"), B("eh"), 16.0, A.mult)
+    tt(B("bk"), B("bk"), B("kI"), A.add)
+    tt(B("bk"), B("bk"), B("bx"), A.add)
+    tcopy(B("SELu"), B("bk"))
+    ts(B("BO"), B("grow"), col(1), A.is_equal, 8192.0, A.mult)
+    ts(B("gt"), B("irow"), col(0), A.is_gt)
+    tt(B("U"), B("BO"), B("gt"), A.mult)
+    ts(B("KC"), B("K4"), 1.0 / 131072.0, A.mult)
+    fill(B("KZ"), -2176.0)
+    for a, b in CH[1:]:
+        o = 24 * (a - C0)
+        tcopy(B("KZ", o, o + 12 * (b - a)), B("KC", 12 * a, 12 * b))
+    tcopy(B("XB", 192, 384), B("K4"))
+    ts(B("IDF"), B("mrow"), col(9), A.is_equal)
+    ts(B("ID"), B("mrow"), col(9), A.is_equal)
+    ts(B("NID"), B("ID"), -1.0, A.mult)
+    ts(B("c3t"), B("jlrow"), col(0), A.is_lt, -LOW, A.mult)
+    ts(B("C3"), B("jlrow"), col(0), A.is_equal, BIG, A.mult)
+    tt(B("C3"), B("C3"), B("c3t"), A.add)
+    ts(col(8), col(0), 0.0, A.is_equal, -LOW, A.mult)
+    ts(B("c3t"), B("jlrow"), 15.0, A.is_equal, col(8), A.mult)
+    tt(B("C3"), B("C3"), B("c3t"), A.add)
+    ts(col(11), col(8), -1.0, A.mult, -BIG, A.add)
+    ts(B("colj"), B("colj"), col(1), A.add)
+    for j in range(16):
+        ts(B("LA", 128 * j, 128 * j + 128), B("lv"), B("colj", j, j + 1), A.is_equal, 65536.0, A.mult)
+    ts(B("LB"), B("LA"), 512.0, A.mult)
+    ts(B("WKB"), B("grow"), col(1), A.is_equal, col(5), A.mult)
+    tcopy(B("E0"), B("own_s"))
+
+    DIAG = (T.eq[:, :, 0:16], [("eq", 0, 192)], [])
+    nxt = cores[(rank + 1) % n]
+    prv = cores[(rank - 1) % n]
+    NE, NP = 16, 16
+    late = []
+
+    def absd(a, b, sign=False):
+        if a < C0:
+            return B("aa", a * P, b * P)
+        ca, cb = [c for c in CH if c[0] <= a < c[1]][0]
+        o = 2 * (ca - C0) + (a - ca) + (cb - ca if sign else 0)
+        return B("as", o * P, (o + b - a) * P)
+
+    def sums(i):
+        y = "Y%d" % (i % 2)
+        mm(B(y, 0, 512), B("WKB"), B("Kw", 512 * i, 512 * i + 512), True, True)
+
+    def sums_out(i):
+        y = "Y%d" % (i % 2)
+        act(B("Yw", 512 * i, 512 * i + 512), B(y, 0, 512), F.Copy)
+
+    for t in range(NS):
+        jub = t % 2 == 1
+        EU, PR, HW, OF = "E%d" % t, "PR%d" % t, "HW%d" % t, "of%d" % (t % 2)
+        OX, OK = B(OF, 0, 12), B(OF, 12, 24)
+        EO, PO, HN = "EO%d" % t, "PO%d" % t, "HW%d" % (t + 1)
+        if t:
+            arrive(EU, 0, 12, prv, "re%d" % t, NE)
+            arrive(PR, 0, P, prv, "rp%d" % t, NP)
+            arrive(HW, 0, 36 if t == 3 else 24, prv, "rh%d" % t, NE)
+            if t == 1:
+                arrive(HW, 24, 36, prv, "ro1", NE)
+        tcopy(B("cb", 16, 208), IND(B("Kw" if t else "ki", 0, V), B(EU)))
+        op("V", lambda: g.vector.transpose(T.tr[:, 0:192], T.cb[:, 16:208]), B("tr", 0, 192), [B("cb", 16, 208)])
+        op("V", lambda: g.vector.transpose(T.tr[:, 192:416], T.cb[:, 0:224]), B("tr", 192, 416), [B("cb")])
+        tcopy(B("cTu"), IND(B("tr"), B("SELu")))
+        act(B("cTf"), IND(B("tr"), B("SELu")), F.Copy)
+        if t == 0:
+            tcopy(B("Kw", 0, H), B("ki", 0, H))
+            late = [lambda: tcopy(B("HW0", 0, 12), B("hold_s")),
+                    lambda: tcopy(B("HW0", 12, 24), B("wall_s")),
+                    lambda: send(nxt, B("HW1", 0, 24), B("HW0", 0, 24), "rh1", NE),
+                    lambda: tcopy(col(7), B("wt_s")),
+                    lambda: ts(B("BW"), B("grow"), col(1), A.is_equal, col(7), A.mult)]
+        if t == 2:
+            late.pop(0)()
+            sums(0)
+            sums(1)
+        if t == 1:
+            mm(B("SS", 0, 16), B("BW"), B("ZB", 0, 16), True, True)
+            late = [lambda: ts(col(12), B("SS", 0, 1), 130.0 / 128.0, A.mult, col(11), A.add)]
+        act(B(PR, 192, 384), B(PR, 0, 192), F.Copy)
+        act(B(PR, 384, 768), B(PR, 0, 384), F.Copy)
+        side = []
+
+        def fillers():
+            if side:
+                side.pop(0)()
+        for a, b, ab, sn, iv in SG:
+            tt(B("d", a * P, b * P), IND(B("Xw", 0, V), B("cTu", 12 * a, 12 * b)), B(PR, 0, (b - a) * P), A.subtract)
+            if a == 0:
+                tt(B("K4c"), B("XB", 192, 384), B("cTf"), A.add)
+            if ab is not None:
+                act(absd(ab, b), B("d", ab * P, b * P), F.Abs)
+            if sn is not None:
+                act(B("sg", sn * P, b * P), B("d", sn * P, b * P), F.Sign, bias=-0.5, scale=-1.0)
+            if iv is not None and iv < C0:
+                ts(B("sg", iv * P, b * P), B("d", iv * P, b * P), 0.0, A.is_lt, -0.5, A.add)
+            elif iv is not None:
+                ts(absd(iv, b, True), B("d", iv * P, b * P), 0.0, A.is_lt, 512.0, A.mult)
+        act(B("q"), B(PR, 0, P), F.Identity, bias=129.625, scale=0.25)
+        if t == 0:
+            act(B("Hw", 0, V), B("ramp", 0, V), F.Copy)
+        for c, (a, b) in enumerate(CH):
+            z = ("Z0", "Z1", "Z2", "CN")[c]
+            w = 12 * (b - a)
+            zb = w if c else 128
+            if c == 0:
+                mm(B(z, 0, w), B("BO"), B("KC", 0, w), True, False)
+                mm(B(z, 0, w), B("IDF"), B("cTf", 0, w), False, False)
+                for j in range(16):
+                    mm(B(z, 0, w), B("LA", 128 * j, 128 * j + 128), B("aa", j, b * P, 16), False, j == 15)
+                mm(B(z, 128, 128 + w), B("BO"), B("ZB", 0, w), True, False)
+                for j in range(16):
+                    mm(B(z, 128, 128 + w), B("LB", 128 * j, 128 * j + 128), B("sg", j, b * P, 16), False, j == 15)
+            else:
+                lo, hi = 2 * (a - C0), 2 * (b - C0)
+                mm(B(z, 0, 2 * w), B("BO"), B("KZ", 12 * lo, 12 * hi), True, False)
+                mm(B(z, 0, w), B("IDF"), B("cTf", 12 * a, 12 * b), False, False)
+                for j in range(16):
+                    mm(B(z, 0, 2 * w), B("LA", 128 * j, 128 * j + 128), B("as", lo * P + j, hi * P, 16), False, j == 15)
+            if c == 0:
+                side = [lambda: ts(B("eF"), B(EU), float(FB), A.add),
+                        lambda: ts(B("eB"), B(EU), col(11), A.add)]
+                if t == 0:
+                    side = [lambda: tcopy(B("Kw", H, V), B("ki", H, V))] + side
+                if jub:
+                    side += [lambda: ts(B("wF"), B(HW, 24, 36), float(V), A.is_lt),
+                             lambda: tt(B("th"), B(HW, 24, 36), B(HW, 0, 12), A.subtract),
+                             lambda: ts(B("nw"), B(HW, 12, 24), -1.0, A.mult, 1.0, A.add),
+                             lambda: tt(B("th"), B("th"), B("wF"), A.mult),
+                             lambda: ts(B("Aw"), B("nw"), col(11), A.mult),
+                             lambda: tt(B(HW, 0, 12), B("th"), B(HW, 0, 12), A.add),
+                             lambda: tt(B("hW"), B(HW, 0, 12), B(HW, 12, 24), A.mult),
+                             lambda: tt(B("hW"), B("hW"), B("Aw"), A.add)]
+                side += late
+                late = []
+            if c == 3:
+                while side:
+                    fillers()
+                if t == 2:
+                    sums_out(0)
+                    sums_out(1)
+                    sums(2)
+            tt(B("t1", 12 * a, 12 * b), B(z, zb, zb + w), B("K4c", 12 * a, 12 * b), A.max)
+            if c == 3:
+                tt(B("t1", 180, 192), B("t1", 180, 192), B("keys", 168, 180), A.min)
+                tt(B("KEY"), B(z, 0, w), B("t1", 180, 192), A.min)
+                break
+            fillers()
+            if c == 2:
+                tt(B("t1", 144, 180), B("t1", 144, 180), B("keys", 0, 36), A.min)
+                fillers()
+            tt(B("keys", 12 * a, 12 * b), B(z, 0, w), B("t1", 12 * a, 12 * b), A.min)
+            fillers()
+            if c == 1:
+                tt(B("keys", 0, 72), B("keys", 0, 72), B("keys", 72, 144), A.min)
+                fillers()
+                tt(B("keys", 0, 36), B("keys", 0, 36), B("keys", 36, 72), A.min)
+                fillers()
+            if c == 2:
+                tt(B("keys", 144, 156), B("keys", 144, 156), B("keys", 156, 168), A.min)
+                fillers()
+                tt(B("keys", 168, 180), B("keys", 144, 156), B("keys", 168, 180), A.min)
+        ts(B("bI"), B("KEY"), 4095, A.bitwise_and)
+        tt(B("fe"), B("KEY"), B("eF"), A.min)
+        tcopy(B("bU"), B("bI"))
+        tt(B("dk"), B("fe"), B("bI"), A.max)
+        ts(B("ek"), B("KEY"), 0.0, A.is_lt, 8192.0, A.mult)
+        tcopy(B("dkU"), B("dk"))
+        ts(B("dkB"), B("dk"), col(11), A.add)
+        tcopy(B("dkf"), IND(B("ramp"), B("dkU")))
+        act(B("bF"), IND(B("ramp", 0, V), B("bU")), F.Copy)
+        act(B("Xb"), IND(B("Xw", 0, V), B("bU")), F.Copy)
+        act(B("Fo"), IND(B("Kw", 0, V), B("bU")), F.Identity, scale=col(2))
+        act(B("ce"), B("cb", 16, 208), F.Identity, scale=col(3))
+        mm(B("CN", 0, P), B("BO"), B("zero"), True, False)
+        for j in range(12):
+            w = P - 16 * j
+            op("V", lambda: g.vector.tensor_scalar(T.eq[:, j, 0:w], T.dkf[:, 16 * j:P], T.dk[:, j:j + 1], None, A.is_equal),
+               (None, [("eq", 16 * j, 16 * j + 16)], []), [B("dkf"), B("dk")])
+            if j < 11:
+                mm(B("CN", 16 * j + 16, P), B("BO"), (T.eq[:, j, 16:w], [("eq", 16 * j, 16 * j + 16)], []), False, False)
+        mm(B("CN", 0, P), B("U"), DIAG, False, True)
+        mm(B("XB", 0, P), B("ID"), B("Xb"), True, False)
+        mm(B("XB", 0, P), B("NID"), B("q"), False, True)
+        if t == 2:
+            sums_out(2)
+            sums(3)
+            sums(4)
+        act(B("xr"), B("XB", 0, P), F.Relu, bias=130.0)
+        tt(B("ek"), B("ek"), B("eB"), A.add)
+        if jub:
+            tt(B("th"), B("bI"), B(HW, 0, 12), A.subtract)
+        scan(B("sc3"), B("CN", 0, P), B("C3"), A.max, A.add)
+        oX = B(HW, 24, 36)
+        tt(B("bxk", 12, 24), B("sc3", 15, P, 16), B("ek"), A.add)
+        tt(B("bxk", 0, 12), B("sc3", 15, P, 16), B("dkB"), A.add)
+        if jub:
+            tt(B("th"), B("th"), B(HW, 12, 24), A.mult)
+        tt(B(HW, 24, 48), B("bxk"), B("DUM"), A.min)
+        tcopy(B(OF), B(HW, 24, 48))
+        ts(B("wU"), oX, float(V), A.is_lt)
+        tcopy(IND(B("Hw"), OK), B("bF"))
+        act(B("hm"), IND(B("Hw", 0, V), B(EU)), F.Copy)
+        if t == NS - 1:
+            dma("Y", ext(T.yh[:]), B("Hw", 0, V, parts=(0, 128, 16)))
+        if t == 2:
+            sums_out(3)
+            sums_out(4)
+        if t == NS - 1:
+            tcopy(IND(B("Xw"), OX), B("xr"))
+            dma("Y", ext(T.yx[:]), B("Xw", 0, V))
+        if jub:
+            act(B("wb"), IND(B("ramp", 0, 16), B("wU")), F.Copy)
+            mm(B("Z2", 0, P), B("ID"), B("wb"), True, False)
+            mm(B("Z2", 0, P), B("ID"), B(PR, 0, P), False, True)
+            act(B("pj"), B("Z2", 0, P), F.Relu, bias=15.0, scale=-1.0)
+            act(B("pw"), B("pj"), F.Identity, bias=15.0, scale=-1.0)
+            ts(B("wF"), oX, float(V), A.is_lt)
+            tt(B("th"), B("th"), B("wF"), A.mult)
+            tt(B("Aw"), B("th"), B("hW"), A.add)
+        else:
+            tt(B("pj"), IND(B("ramp", 0, 16), B("wU")), B(PR, 0, P), A.add)
+        if t >= 2:
+            yv = "yv%d" % t
+            mm(B("Y1", 0, P), B("WKB"), B("Fo"), True, False)
+            mm(B("Y1", 0, P), B("WKB"), B("ce"), False, True)
+            act(B(yv), B("Y1", 0, P), F.Copy)
+        scan(B("sc"), B("hm"), B("C3"), A.max, A.add)
+        el = B("sc", 15, 192, 16)
+        if jub:
+            tt(B("eh"), el, B("nw"), A.mult)
+            tt(B("fin", 0, 12), B("eh"), B("Aw"), A.add)
+            tcopy(B(EO), B("fin", 0, 12))
+        else:
+            ts(B(EO), el, col(11), A.add)
+        if t < NS - 1:
+            send(nxt, B("E%d" % (t + 1)), B(EO), "re%d" % (t + 1), NE)
+        if not jub:
+            ts(B(PO), B("pj"), 15.0, A.min)
+            send(nxt, B("PR%d" % (t + 1), 0, P), B(PO), "rp%d" % (t + 1), NP)
+            if t == 0:
+                send(nxt, B(HN, 24, 36), B(HW, 24, 36), "ro1", NE)
+            else:
+                send(nxt, B(HN, 0, 36), B(HW, 0, 36), "rh%d" % (t + 1), NE)
+            tt(IND(B("Kw"), OK), B("Fo"), B("ce"), A.add)
+        if t < NS - 1:
+            tcopy(IND(B("Xw"), OX), B("xr"))
+        if jub:
+            tt(B("pj"), IND(B("Xw", 0, V), B(EO)), B("pw"), A.add)
+            ts(B("ph"), B("pj"), 0.5, A.mult, 129.75, A.add)
+            mm(B("SS", 0, P), B("BW"), B("ph"), True, True)
+            if t < NS - 1:
+                ts(B(PO), B("ph"), -130.0, A.add)
+                send(nxt, B("PR%d" % (t + 1), 0, P), B(PO), "rp%d" % (t + 1), NP)
+                tt(IND(B("Kw"), OK), B("Fo"), B("ce"), A.add)
+
+            def holders(t=t, HW=HW, HN=HN):
+                def home():
+                    if t < NS - 1:
+                        tt(B(HW, 0, 12), B("uI"), B("gg"), A.add)
+                        send(nxt, B(HN, 0, 24), B(HW, 0, 24), "rh%d" % (t + 1), NE)
+                    else:
+                        tt(B("fin", 12, 24), B("uI"), B("gg"), A.add)
+                        send(cores[(rank - t) % n], B("rfin"), B("fin"), "rf", NE)
+                return [lambda: scan(B("sc3"), B("SS", 0, P), B("C3"), A.max, A.add),
+                        lambda: ts(B("sI"), B("sc3", 15, P, 16), col(12), A.add),
+                        lambda: ts(B("uI"), B("sI"), 4095, A.bitwise_and),
+                        lambda: ts(B("gg"), B("uI"), float(V), A.is_ge, -float(V), A.mult),
+                        home]
+            if t == NS - 1:
+                for f in holders():
+                    f()
+            else:
+                late = holders()
+    tcopy(IND(B("Yw"), B("of0", 12, 24)), B("yv2"))
+    tcopy(IND(B("Yw"), B("of1", 12, 24)), B("yv3"))
+    dma("Y", ext(T.yk[:]), B("Yw", 0, V, parts=(0, 128, 16)))
+    arrive("rfin", 0, 24, cores[(rank + NS - 1) % n], "rf", NE)
+    tcopy(B("rU"), B("rfin"))
+    tcopy(B("outf", 0, P), IND(B("ramp", 0, V), B("rU", 0, 12)))
+    act(B("outf", P, 2 * P), IND(B("ramp", 0, V), B("rU", 12, 24)), F.Copy)
+    dma("Y", ext(T.yo[:]), B("outf", 0, P, parts=(0, 128, 16)))
+    dma("S", ext(T.yt[:]), B("outf", P, 2 * P, parts=(0, 128, 16)))
+    g.wait_ge(T.sem["ls"], sent[0])
+    for i in range(ndma[0]):
+        g.wait_ge(T.sem["dm%d" % i], 16)
+    for q in "VST":
+        g.wait_ge(T.sem["q" + q], cnt[q])
+    g.wait_ge(T.sem["qG"], cnt["G"])

@@ -1,12 +1,11 @@
 from concourse.mybir import dt, AluOpType, AxisListType, ActivationFunctionType
 
-V, P, NS, FB = 2560, 192, 4, 2752
-W = V + P
-CH = [(0, 7), (7, 12), (12, 15), (15, 16)]
-C0 = 7
-SG = [(0, 1, None, None, None), (1, 3, 0, 0, None), (3, 7, 3, None, 3), (7, 10, 7, None, None), (10, 12, 10, None, 7),
-      (12, 15, 12, None, 12), (15, 16, 15, None, 15)]
+V, P, NS = 2560, 192, 4
+W = 2 * V + P
 BIG, LOW = 2.0 ** 21, 2.0 ** 23
+OFF = 240.0 * 65536
+RND = 1.5 * 2.0 ** 39
+NV = 2
 A = AluOpType
 F = ActivationFunctionType
 
@@ -17,33 +16,37 @@ def _b(name, cols, d, where="sbuf"):
     SCRATCH[name] = (where, [128] + (cols if isinstance(cols, list) else [cols]), d)
 
 
-for _n, _c in (("Kw", W), ("Hw", W), ("Yw", W), ("ramp", 5312), ("cb", 224), ("tr", 416), ("cTf", 192), ("colj", 16),
-               ("jlrow", 192), ("C3", 192), ("c3t", 192), ("sc3", 192), ("IDF", 128), ("mrow", 128),
-               ("K4", 192), ("K4c", 192), ("keys", 192), ("t1", 192), ("sc", 192), ("bF", 192), ("Fo", 192), ("ce", 192),
-               ("hm", 192), ("DUM", 24), ("bxk", 24), ("dm0", 12), ("cols", 16), ("eF", 12), ("eB", 12), ("fe", 12),
-               ("dk", 12), ("dkB", 12), ("ek", 12), ("bx", 12), ("oX", 12), ("bk", 12), ("oK", 12), ("wF", 12), ("th", 12), ("hW", 12),
-               ("Aw", 12), ("nw", 12), ("m12", 12), ("eh", 12), ("fin", 24), ("rfin", 24), ("outf", 384), ("WKB", 128),
-               ("yv2", 192), ("yv3", 192), ("gg", 12)):
+for _n, _c in (("Kw", W), ("Hw", W), ("Yw", W), ("ramp", 2 * V), ("cb", 224), ("tr", 416), ("jlrow", 192), ("C3", 192),
+               ("c3t", 192), ("sc3", 192), ("K0", 192), ("keys", 192), ("rA", 192), ("RST", 192), ("sk", 192), ("sc", 192),
+               ("bF", 192), ("Fo", 192), ("ce", 192), ("hm", 192), ("DUM", 12), ("dm0", 12), ("cols", 16), ("eF", 12), ("fe", 12),
+               ("fo", 12), ("dk", 12), ("ox", 12), ("oy", 12), ("wF", 12), ("th", 12), ("hW", 12), ("Aw", 12), ("nw", 12), ("eh", 12),
+               ("fin", 12), ("hh", 12), ("rh", 12), ("outf", 192), ("WKB", 128), ("yv2", 192), ("yv3", 192), ("gg", 12),
+               ("s2", 12), ("s3", 12)):
     _b(_n, _c, "float32")
-for _n, _c in (("Xw", W), ("d", 3072), ("aa", 1344), ("sg", 1344), ("as", 3456), ("KZ", 216), ("eq", [12, 192]), ("LA", 2048), ("LB", 2048), ("lv", 128), ("BO", 128),
-               ("U", 128), ("BW", 128), ("grow", 128), ("irow", 128), ("gt", 128), ("KC", 192), ("zero", 192), ("q", 192), ("ID", 128),
-               ("NID", 128), ("ZB", 96), ("Xb", 192), ("xr", 192), ("pw", 192), ("pj", 192), ("wb", 192), ("ph", 192)):
+for _n, _c in (("Xw", W), ("wk", [12, 256]), ("eq", [12, 192]), ("crow", 288), ("L32", 288), ("Lw", 288), ("BO", 128),
+               ("U", 128), ("grow", 128), ("irow", 128), ("mrow", 128), ("gt", 128), ("zero", 192), ("q", 192), ("ID", 128), ("ID2", 128),
+               ("NID", 128), ("C16", 64), ("Cm", 192), ("C130", 16), ("Xb", 192), ("xr", 192), ("pw", 192), ("pj", 192), ("wb", 192),
+               ("ph", 192)):
     _b(_n, _c, "bfloat16")
-for _n, _c in (("ki", V), ("own_s", 12), ("hold_s", 12), ("wall_s", 12), ("wt_s", 1), ("ci", 4), ("kI", 12), ("jI", 12),
-               ("KEY", 12), ("bI", 12), ("sI", 12), ("uI", 12)):
+for _n, _c in (("tk", [12, 256]), ("L64", 288)):
+    _b(_n, _c, "float16")
+for _n, _c in (("ki", V), ("own_s", 12), ("hold_s", 12), ("wall_s", 12), ("wt_s", 1), ("ci", 8), ("KEY", 12), ("bI", 12), ("sI", 12),
+               ("uI", 12)):
     _b(_n, _c, "int32")
-for _n, _c in (("SELu", 12), ("cTu", 192), ("bU", 12), ("dkU", 12), ("dkf", 192), ("of0", 24), ("of1", 24), ("wU", 12), ("rU", 24)):
+for _n, _c in (("SELk", 12), ("cbu", 192), ("bU", 12), ("dkU", 12), ("dkf", 192), ("of0", 12), ("of1", 12),
+               ("wU", 12), ("rE", 12)):
     _b(_n, _c, "uint16")
 for _t in range(NS):
     _b("E%d" % _t, 12, "uint16")
     _b("EO%d" % _t, 12, "uint16")
-    _b("PR%d" % _t, 768, "bfloat16")
+    _b("PR%d" % _t, 192, "bfloat16")
     _b("PO%d" % _t, 192, "bfloat16")
-    _b("HW%d" % _t, 48, "float32")
-for _n, _c in (("Z0", 512), ("Z1", 512), ("Z2", 512), ("CN", 512), ("SS", 512), ("XB", 512), ("Y0", 512), ("Y1", 512)):
-    _b(_n, _c, "float32", "psum")
+    _b("HW%d" % _t, 24, "float32")
+for _n in ("ZA", "ZB", "ZC", "PP", "CN", "XB", "Y0", "Y1"):
+    _b(_n, 512, "float32", "psum")
 
-SEMAPHORES = ["qV", "qS", "qT", "qG", "ls"] + ["dm%d" % i for i in range(24)] + ["r%s%d" % (a, t) for a in "eph" for t in range(1, NS)] + ["rf", "ro1"]
+SEMAPHORES = (["qV", "qS", "qT", "qG", "ls"] + ["dm%d" % i for i in range(16)]
+              + ["r%s%d" % (a, t) for a in "eph" for t in range(1, NS)] + ["rf", "rg", "rw1"])
 
 
 def rank_program(g, core, T, topo):
@@ -58,7 +61,7 @@ def rank_program(g, core, T, topo):
     known = {q: {} for q in "VSTGY"}
     clock = {}
     ndma = [0]
-    psum = ("Z0", "Z1", "Z2", "CN", "SS", "XB", "Y0", "Y1")
+    psum = ("ZA", "ZB", "ZC", "PP", "CN", "XB", "Y0", "Y1")
 
     def B(name, lo=0, hi=None, step=1, parts=None):
         t = T[name]
@@ -68,6 +71,9 @@ def rank_program(g, core, T, topo):
             ap = t[:, lo:hi] if step == 1 else t[:, lo:hi:step]
         else:
             ap = t[parts[0]:parts[1]:parts[2], lo:hi]
+        return (ap, [(name, lo, hi)], [])
+
+    def R(name, ap, lo=0, hi=16):
         return (ap, [(name, lo, hi)], [])
 
     def IND(win, off):
@@ -80,11 +86,9 @@ def rank_program(g, core, T, topo):
         want = {}
         for regs, wr in ((reads, False), (writes, True)):
             for nm, lo, hi in regs:
-                if nm in psum:
-                    lo, hi = 0, 512
                 for e in log.get(nm, []):
-                    if e[0] < hi and lo < e[1] and (wr or e[3]):
-                        if e[4] == q and (not e[3] or acc):
+                    if (e[0] < hi and lo < e[1] and (wr or e[3])) or (nm in psum and e[4] != q):
+                        if e[4] == q and acc:
                             continue
                         s, v = e[2]
                         if want.get(s, 0) < v:
@@ -103,8 +107,6 @@ def rank_program(g, core, T, topo):
         clock[tok] = dict(known[q])
         for regs, wr in ((reads, False), (writes, True)):
             for nm, lo, hi in regs:
-                if nm in psum:
-                    lo, hi = 0, 512
                 lst = log.get(nm, [])
                 if wr:
                     lst = [e for e in lst if not (lo <= e[0] and e[1] <= hi)]
@@ -137,17 +139,15 @@ def rank_program(g, core, T, topo):
 
     sent = [0]
 
-    def send(dst, out, in_, sem, ne):
+    def send(dst, out, in_, sem):
         need("G", in_[1], [], False)
         rid, pid, _ = topo.addr(dst)
-        es = topo.engines(core, dst)[:ne]
-        g.remote_dma(out[0], in_[0], T.sem[sem], T.sem["ls"], pid, rid, sum(1 << e for e in es))
-        sent[0] += len(es)
+        g.remote_dma(out[0], in_[0], T.sem[sem], T.sem["ls"], pid, rid, topo.mask(core, dst))
+        sent[0] += len(topo.engines(core, dst))
 
-    def arrive(name, lo, hi, src, sem, ne):
-        v = len(topo.engines(src, core)[:ne])
+    def arrive(name, lo, hi, src, sem):
         known[sem] = {}
-        note(sem, (sem, v), [], [(name, lo, hi)])
+        note(sem, (sem, len(topo.engines(src, core))), [], [(name, lo, hi)])
 
     def val(x):
         return x[0] if isinstance(x, tuple) else x
@@ -185,227 +185,201 @@ def rank_program(g, core, T, topo):
     def col(i):
         return B("cols", i, i + 1)
 
-    H = V // 2
+    def ci(i):
+        return B("ci", i, i + 1)
+
+    def L(name, j):
+        o = 15 - j if j % 2 else 144 + 16 - j
+        return B(name, o, o + 128)
+
     dma("Y", B("own_s"), ext(T.own[:]))
     dma("Y", B("ki"), ext(T.kin[:]))
-    dma("Y", B("PR0", 0, P), ext(T.price[:]))
     dma("Y", B("Xw", 0, V), ext(T.x[:]))
-    dma("Y", B("hold_s"), ext(T.hold[:]))
+    dma("Y", B("PR0"), ext(T.price[:]))
     dma("Y", B("wall_s"), ext(T.wall[:]))
+    dma("Y", B("hold_s"), ext(T.hold[:]))
     dma("Y", B("wt_s"), ext(T.wt[:]))
 
-    iota(B("cols", 9, 10), [[0, 1]], 0, 1)
-    iota(B("dm0"), [[16, 12]], V, 1)
-    iota(B("grow"), [[1, 8], [0, 16]], 0, 0)
-    iota(B("irow"), [[0, 8], [1, 16]], 0, 0)
-    iota(B("K4"), [[4096, 16], [0, 12]], -65536, 0)
+    RB = V // 4
+    iota(col(9), [[0, 1]], 0, 1)
+    iota(B("ramp", 0, RB), [[1, RB]], 0, 0)
+    iota(B("s2"), [[32, 6], [16, 2]], 0, 0)
+    iota(B("s3"), [[0, 6], [1, 2]], 0, 0)
+    iota(B("crow"), [[-1, 2], [1, 144]], 0, 0)
     iota(B("mrow"), [[1, 128]], 0, 0)
     iota(B("jlrow"), [[0, 12], [1, 16]], 0, 0)
-    iota(B("lv"), [[1, 8], [16, 16]], 0, 0)
-    iota(B("colj"), [[16, 16]], 0, 0)
-    RB = 1328
-    iota(B("ramp", 0, RB), [[1, RB]], 0, 0)
-    act(B("ramp", RB, 2 * RB), B("ramp", 0, RB), F.Identity, bias=float(RB))
-    act(B("ramp", 2 * RB, 4 * RB), B("ramp", 0, 2 * RB), F.Identity, bias=float(2 * RB))
-    ci = lambda i: B("ci", i, i + 1)
+    iota(B("grow"), [[1, 8], [0, 16]], 0, 0)
+    iota(B("irow"), [[0, 8], [1, 16]], 0, 0)
+    iota(B("dm0"), [[16, 12]], 2 * V, 0)
+    iota(B("Hw", V, 2 * V), [[1, V]], 0, 0)
+    for a in (RB, 2 * RB, 4 * RB):
+        act(B("ramp", a, 2 * a), B("ramp", 0, a), F.Identity, bias=float(a))
     fill(B("cb"), 0.0)
+    tcopy(ci(6), col(9))
     fill(B("zero"), 0.0)
-    fill(B("ZB"), -128.0)
-    tcopy(ci(0), col(9))
-    ts(ci(1), ci(0), 4, A.logical_shift_right)
-    ts(ci(2), ci(0), 1, A.bitwise_and)
-    ts(ci(3), ci(0), 4, A.logical_shift_right, 1, A.bitwise_and)
-    ts(ci(0), ci(0), 15, A.bitwise_and)
-    tcopy(B("cols", 0, 3), B("ci", 0, 3))
-    tcopy(col(6), ci(3))
-    ts(col(3), col(2), -1.0, A.mult, 1.0, A.add)
-    ts(col(4), col(1), -16.0, A.mult)
-    ts(col(5), col(0), 1.0, A.add)
-    ts(B("DUM", 0, 12), B("dm0"), col(4), A.add)
-    ts(B("DUM", 12, 24), B("dm0"), col(4), A.add)
-    ts(B("m12"), B("DUM", 0, 12), -float(V), A.add)
-    ts(B("kI"), B("m12"), 1.0 / 12.0, A.mult, -11.0 / 24.0, A.add)
-    ts(B("eh"), B("kI"), -12.0, A.mult)
-    tt(B("eh"), B("eh"), B("m12"), A.add)
-    ts(B("jI"), B("eh"), col(6), A.add)
-    ts(B("jI"), B("jI"), 1, A.bitwise_and)
-    ts(B("bx"), B("jI"), 208.0, A.mult)
-    ts(B("bk"), B("eh"), 16.0, A.mult)
-    tt(B("bk"), B("bk"), B("kI"), A.add)
-    tt(B("bk"), B("bk"), B("bx"), A.add)
-    tcopy(B("SELu"), B("bk"))
-    ts(B("BO"), B("grow"), col(1), A.is_equal, 8192.0, A.mult)
-    ts(B("gt"), B("irow"), col(0), A.is_gt)
-    tt(B("U"), B("BO"), B("gt"), A.mult)
-    ts(B("KC"), B("K4"), 1.0 / 131072.0, A.mult)
-    fill(B("KZ"), -2176.0)
-    for a, b in CH[1:]:
-        o = 24 * (a - C0)
-        tcopy(B("KZ", o, o + 12 * (b - a)), B("KC", 12 * a, 12 * b))
-    tcopy(B("XB", 192, 384), B("K4"))
-    ts(B("IDF"), B("mrow"), col(9), A.is_equal)
+    fill(B("C16"), 16384.0)
+    ts(ci(0), ci(6), 15, A.bitwise_and)
+    ts(ci(1), ci(6), 4, A.logical_shift_right)
+    ts(ci(2), ci(6), 1, A.bitwise_and)
+    ts(ci(3), ci(6), 4, A.logical_shift_right, 1, A.bitwise_and)
+    fill(B("Cm"), -32.0)
+    tcopy(B("cols", 0, 4), B("ci", 0, 4))
+    fill(B("C130"), -130.0)
+    ts(col(6), col(2), -1.0, A.mult, 1.0, A.add)
+    ts(col(10), col(3), -416.0, A.mult, 208.0, A.add)
+    ts(col(12), col(3), 208.0, A.mult, col(0), A.add)
+    ts(col(13), col(1), 16.0, A.mult, 15.0, A.add)
+    ts(col(15), col(0), 1.0, A.add)
+    ts(B("s3"), B("s3"), col(10), A.mult, col(12), A.add)
+    ts(B("L64"), B("crow"), col(13), A.is_equal, 64.0, A.mult)
+    tt(B("s2"), B("s2"), B("s3"), A.add)
+    ts(B("L32"), B("crow"), col(13), A.is_equal, -32.0, A.mult)
     ts(B("ID"), B("mrow"), col(9), A.is_equal)
-    ts(B("NID"), B("ID"), -1.0, A.mult)
+    tcopy(B("SELk"), B("s2"))
+    ts(B("ID2"), B("mrow"), col(9), A.is_equal, 2048.0, A.mult)
+    ts(B("NID"), B("mrow"), col(9), A.is_equal, -1.0, A.mult)
+    tcopy(B("E0"), B("own_s"))
+    ts(B("RST"), B("jlrow"), 0.0, A.is_equal, 2.0 ** 26, A.mult)
     ts(B("c3t"), B("jlrow"), col(0), A.is_lt, -LOW, A.mult)
     ts(B("C3"), B("jlrow"), col(0), A.is_equal, BIG, A.mult)
-    tt(B("C3"), B("C3"), B("c3t"), A.add)
     ts(col(8), col(0), 0.0, A.is_equal, -LOW, A.mult)
-    ts(B("c3t"), B("jlrow"), 15.0, A.is_equal, col(8), A.mult)
+    ts(B("RST"), B("RST"), -4096.0, A.add)
     tt(B("C3"), B("C3"), B("c3t"), A.add)
     ts(col(11), col(8), -1.0, A.mult, -BIG, A.add)
-    ts(B("colj"), B("colj"), col(1), A.add)
-    for j in range(16):
-        ts(B("LA", 128 * j, 128 * j + 128), B("lv"), B("colj", j, j + 1), A.is_equal, 65536.0, A.mult)
-    ts(B("LB"), B("LA"), 512.0, A.mult)
-    ts(B("WKB"), B("grow"), col(1), A.is_equal, col(5), A.mult)
-    tcopy(B("E0"), B("own_s"))
+    ts(B("BO"), B("grow"), col(1), A.is_equal, 8192.0, A.mult)
+    ts(B("C3", 15, P, 16), B("C3", 15, P, 16), col(8), A.add)
+    ts(B("gt"), B("irow"), col(0), A.is_gt)
+    ts(B("WKB"), B("grow"), col(1), A.is_equal, col(15), A.mult)
+    ts(B("DUM"), B("dm0"), col(0), A.add, col(11), A.subtract)
+    tt(B("U"), B("BO"), B("gt"), A.mult)
 
     DIAG = (T.eq[:, :, 0:16], [("eq", 0, 192)], [])
     nxt = cores[(rank + 1) % n]
     prv = cores[(rank - 1) % n]
-    NE, NP = 16, 16
-    late = []
-
-    def absd(a, b, sign=False):
-        if a < C0:
-            return B("aa", a * P, b * P)
-        ca, cb = [c for c in CH if c[0] <= a < c[1]][0]
-        o = 2 * (ca - C0) + (a - ca) + (cb - ca if sign else 0)
-        return B("as", o * P, (o + b - a) * P)
+    home = cores[(rank - (NS - 1)) % n]
+    away = cores[(rank + NS - 1) % n]
+    XW, KW, HS = B("Xw", 0, V), B("Kw", V, 2 * V), B("Hw", V, 2 * V)
 
     def sums(i):
-        y = "Y%d" % (i % 2)
-        mm(B(y, 0, 512), B("WKB"), B("Kw", 512 * i, 512 * i + 512), True, True)
+        mm(B("Y%d" % (i % 2)), B("WKB"), B("Kw", V + 512 * i, V + 512 * i + 512), True, True)
 
     def sums_out(i):
-        y = "Y%d" % (i % 2)
-        act(B("Yw", 512 * i, 512 * i + 512), B(y, 0, 512), F.Copy)
+        act(B("Yw", V + 512 * i, V + 512 * i + 512), B("Y%d" % (i % 2)), F.Copy)
+
+    def moving(c, buf, j):
+        return R(buf, T[buf][:, 4 * c:4 * c + 4, 16 * j:16 * j + 16], 16 * c, 16 * c + 16)
+
+    def part(name, c):
+        return B(name, 64 * c, 64 * c + 64)
+
+    def Z(c, i):
+        return part(("ZA", "ZB", "ZC")[c], i)
+
+    def linear(c):
+        mm(Z(c, 0), B("ID"), B("C16"), True, False)
+        for j in range(16):
+            mm(Z(c, 0), L("L32", j), moving(c, "wk", j), False, False)
+
+    def maxima(c):
+        for j in range(16):
+            mm(Z(c, 0), L("L64", j), moving(c, "tk", j), False, j == 15)
+
+    def decode(c):
+        return [lambda: ts(part("rA", c), Z(c, 0), RND, A.add, RND, A.subtract),
+                lambda: tt(Z(c, 1), Z(c, 0), part("rA", c), A.is_lt),
+                lambda: tt(Z(c, 2), Z(c, 1), part("rA", c), A.mult)]
+
+    def key(c):
+        tt(part("keys", c), Z(c, 2), part("K0", c), A.add)
 
     for t in range(NS):
         jub = t % 2 == 1
-        EU, PR, HW, OF = "E%d" % t, "PR%d" % t, "HW%d" % t, "of%d" % (t % 2)
-        OX, OK = B(OF, 0, 12), B(OF, 12, 24)
+        last = t == NS - 1
+        EU, PR, HW, OF = "E%d" % t, "PR%d" % t, "HW%d" % t, B("of%d" % (t % 2))
         EO, PO, HN = "EO%d" % t, "PO%d" % t, "HW%d" % (t + 1)
+        hh, wall = B(HW, 0, 12), B(HW, 12, 24)
         if t:
-            arrive(EU, 0, 12, prv, "re%d" % t, NE)
-            arrive(PR, 0, P, prv, "rp%d" % t, NP)
-            arrive(HW, 0, 36 if t == 3 else 24, prv, "rh%d" % t, NE)
+            arrive(EU, 0, 12, prv, "re%d" % t)
+            arrive(PR, 0, P, prv, "rp%d" % t)
+            arrive(HW, 0, 12 if t == 1 else 24, prv, "rh%d" % t)
             if t == 1:
-                arrive(HW, 24, 36, prv, "ro1", NE)
-        tcopy(B("cb", 16, 208), IND(B("Kw" if t else "ki", 0, V), B(EU)))
-        op("V", lambda: g.vector.transpose(T.tr[:, 0:192], T.cb[:, 16:208]), B("tr", 0, 192), [B("cb", 16, 208)])
-        op("V", lambda: g.vector.transpose(T.tr[:, 192:416], T.cb[:, 0:224]), B("tr", 192, 416), [B("cb")])
-        tcopy(B("cTu"), IND(B("tr"), B("SELu")))
-        act(B("cTf"), IND(B("tr"), B("SELu")), F.Copy)
+                arrive(HW, 12, 24, prv, "rw1")
+        kw = KW if t else B("ki")
+        tcopy(B("cbu", 0, 64), IND(kw, B(EU, 0, 4)))
+        tcopy(B("cbu", 64, P), IND(kw, B(EU, 4, 12)))
+        ts(B("eF"), B(EU), V - OFF, A.add)
+        blocks = [(R("wk", T.wk[:, a, :], 4 * a, 4 * a + 4), IND(XW, B("cbu", 16 * a, 16 * a + 16))) for a in range(12)]
+        for o, i in blocks[:8 - NV] + blocks[8:]:
+            act(o, i, F.Identity, scale=2048.0)
+        tcopy(B("cb", 16, 208), B("cbu"))
         if t == 0:
-            tcopy(B("Kw", 0, H), B("ki", 0, H))
-            late = [lambda: tcopy(B("HW0", 0, 12), B("hold_s")),
-                    lambda: tcopy(B("HW0", 12, 24), B("wall_s")),
-                    lambda: send(nxt, B("HW1", 0, 24), B("HW0", 0, 24), "rh1", NE),
-                    lambda: tcopy(col(7), B("wt_s")),
-                    lambda: ts(B("BW"), B("grow"), col(1), A.is_equal, col(7), A.mult)]
-        if t == 2:
-            late.pop(0)()
-            sums(0)
-            sums(1)
-        if t == 1:
-            mm(B("SS", 0, 16), B("BW"), B("ZB", 0, 16), True, True)
-            late = [lambda: ts(col(12), B("SS", 0, 1), 130.0 / 128.0, A.mult, col(11), A.add)]
-        act(B(PR, 192, 384), B(PR, 0, 192), F.Copy)
-        act(B(PR, 384, 768), B(PR, 0, 384), F.Copy)
+            tcopy(KW, B("ki"))
+        for o, i in blocks[8 - NV:8]:
+            ts(o, i, 2048.0, A.mult)
+        mm(B("PP", 0, P), B("ID"), B("Cm"), True, False)
+        mm(B("PP", 0, P), B("ID2"), B(PR), False, True)
         side = []
+        if t == 0:
+            side = [lambda: tcopy(B(HW, 12, 24), B("wall_s")),
+                    lambda: tcopy(B(HW, 0, 12), B("hold_s")),
+                    lambda: send(nxt, B(HN, 12, 24), wall, "rw1"),
+                    lambda: tcopy(col(7), B("wt_s")),
+                    lambda: None,
+                    lambda: ts(B("Lw"), B("crow"), col(13), A.is_equal, col(7), A.mult)]
+        if jub:
+            side = [lambda: ts(B("nw"), wall, -1.0, A.mult, 1.0, A.add),
+                    lambda: tt(B("hW"), hh, wall, A.mult),
+                    lambda: ts(B("Aw"), B("nw"), col(11), A.mult),
+                    lambda: None,
+                    lambda: tt(B("hW"), B("hW"), B("Aw"), A.add)]
 
         def fillers():
             if side:
                 side.pop(0)()
-        for a, b, ab, sn, iv in SG:
-            tt(B("d", a * P, b * P), IND(B("Xw", 0, V), B("cTu", 12 * a, 12 * b)), B(PR, 0, (b - a) * P), A.subtract)
-            if a == 0:
-                tt(B("K4c"), B("XB", 192, 384), B("cTf"), A.add)
-            if ab is not None:
-                act(absd(ab, b), B("d", ab * P, b * P), F.Abs)
-            if sn is not None:
-                act(B("sg", sn * P, b * P), B("d", sn * P, b * P), F.Sign, bias=-0.5, scale=-1.0)
-            if iv is not None and iv < C0:
-                ts(B("sg", iv * P, b * P), B("d", iv * P, b * P), 0.0, A.is_lt, -0.5, A.add)
-            elif iv is not None:
-                ts(absd(iv, b, True), B("d", iv * P, b * P), 0.0, A.is_lt, 512.0, A.mult)
-        act(B("q"), B(PR, 0, P), F.Identity, bias=129.625, scale=0.25)
-        if t == 0:
-            act(B("Hw", 0, V), B("ramp", 0, V), F.Copy)
-        for c, (a, b) in enumerate(CH):
-            z = ("Z0", "Z1", "Z2", "CN")[c]
-            w = 12 * (b - a)
-            zb = w if c else 128
+        for c in range(3):
+            linear(c)
+            for k in range(16):
+                tt(R("tk", T.tk[:, 4 * c:4 * c + 4, k::16], 16 * c + k, 16 * c + k + 1),
+                   R("wk", T.wk[:, 4 * c:4 * c + 4, k::16], 16 * c, 16 * c + 16), B("PP", 64 * c, 64 * c + 64), A.max)
+                if c == 1 and k >= 10 and k % 2:
+                    fillers()
+            maxima(c)
             if c == 0:
-                mm(B(z, 0, w), B("BO"), B("KC", 0, w), True, False)
-                mm(B(z, 0, w), B("IDF"), B("cTf", 0, w), False, False)
-                for j in range(16):
-                    mm(B(z, 0, w), B("LA", 128 * j, 128 * j + 128), B("aa", j, b * P, 16), False, j == 15)
-                mm(B(z, 128, 128 + w), B("BO"), B("ZB", 0, w), True, False)
-                for j in range(16):
-                    mm(B(z, 128, 128 + w), B("LB", 128 * j, 128 * j + 128), B("sg", j, b * P, 16), False, j == 15)
-            else:
-                lo, hi = 2 * (a - C0), 2 * (b - C0)
-                mm(B(z, 0, 2 * w), B("BO"), B("KZ", 12 * lo, 12 * hi), True, False)
-                mm(B(z, 0, w), B("IDF"), B("cTf", 12 * a, 12 * b), False, False)
-                for j in range(16):
-                    mm(B(z, 0, 2 * w), B("LA", 128 * j, 128 * j + 128), B("as", lo * P + j, hi * P, 16), False, j == 15)
-            if c == 0:
-                side = [lambda: ts(B("eF"), B(EU), float(FB), A.add),
-                        lambda: ts(B("eB"), B(EU), col(11), A.add)]
-                if t == 0:
-                    side = [lambda: tcopy(B("Kw", H, V), B("ki", H, V))] + side
-                if jub:
-                    side += [lambda: ts(B("wF"), B(HW, 24, 36), float(V), A.is_lt),
-                             lambda: tt(B("th"), B(HW, 24, 36), B(HW, 0, 12), A.subtract),
-                             lambda: ts(B("nw"), B(HW, 12, 24), -1.0, A.mult, 1.0, A.add),
-                             lambda: tt(B("th"), B("th"), B("wF"), A.mult),
-                             lambda: ts(B("Aw"), B("nw"), col(11), A.mult),
-                             lambda: tt(B(HW, 0, 12), B("th"), B(HW, 0, 12), A.add),
-                             lambda: tt(B("hW"), B(HW, 0, 12), B(HW, 12, 24), A.mult),
-                             lambda: tt(B("hW"), B("hW"), B("Aw"), A.add)]
-                side += late
-                late = []
-            if c == 3:
+                side = decode(0) + side
+            if c == 1:
+                op("V", lambda: g.vector.transpose(T.tr[:, 0:192], T.cb[:, 16:208]), B("tr", 0, 192), [B("cb", 16, 208)])
+                op("V", lambda: g.vector.transpose(T.tr[:, 192:416], T.cb[:, 0:224]), B("tr", 192, 416), [B("cb")])
+                act(B("K0"), IND(B("tr"), B("SELk")), F.Identity, bias=-OFF)
+                act(B("q"), B(PR), F.Identity, bias=129.625, scale=0.25)
+                act(B("ce"), B("cb", 16, 208), F.Identity, scale=col(6))
                 while side:
                     fillers()
-                if t == 2:
-                    sums_out(0)
-                    sums_out(1)
-                    sums(2)
-            tt(B("t1", 12 * a, 12 * b), B(z, zb, zb + w), B("K4c", 12 * a, 12 * b), A.max)
-            if c == 3:
-                tt(B("t1", 180, 192), B("t1", 180, 192), B("keys", 168, 180), A.min)
-                tt(B("KEY"), B(z, 0, w), B("t1", 180, 192), A.min)
-                break
-            fillers()
-            if c == 2:
-                tt(B("t1", 144, 180), B("t1", 144, 180), B("keys", 0, 36), A.min)
-                fillers()
-            tt(B("keys", 12 * a, 12 * b), B(z, 0, w), B("t1", 12 * a, 12 * b), A.min)
-            fillers()
-            if c == 1:
-                tt(B("keys", 0, 72), B("keys", 0, 72), B("keys", 72, 144), A.min)
-                fillers()
-                tt(B("keys", 0, 36), B("keys", 0, 36), B("keys", 36, 72), A.min)
-                fillers()
-            if c == 2:
-                tt(B("keys", 144, 156), B("keys", 144, 156), B("keys", 156, 168), A.min)
-                fillers()
-                tt(B("keys", 168, 180), B("keys", 144, 156), B("keys", 168, 180), A.min)
+        if t >= 2:
+            sums(3 * (t - 2))
+            sums(3 * (t - 2) + 1)
+        d1 = decode(1)
+        d1[0]()
+        key(0)
+        d1[1]()
+        d1[2]()
+        key(1)
+        for f in decode(2):
+            f()
+        key(2)
+        scan(B("sk"), B("RST"), B("keys"), A.add, A.min)
+        sv = B("sk", 15, P, 16)
+        tcopy(B("KEY"), sv)
+        tt(B("fo"), sv, B("eF"), A.min)
         ts(B("bI"), B("KEY"), 4095, A.bitwise_and)
-        tt(B("fe"), B("KEY"), B("eF"), A.min)
-        tcopy(B("bU"), B("bI"))
+        ts(B("fe"), B("fo"), OFF, A.add)
         tt(B("dk"), B("fe"), B("bI"), A.max)
-        ts(B("ek"), B("KEY"), 0.0, A.is_lt, 8192.0, A.mult)
+        tcopy(B("bU"), B("bI"))
         tcopy(B("dkU"), B("dk"))
-        ts(B("dkB"), B("dk"), col(11), A.add)
+        tt(B("th"), B("bI"), hh, A.subtract)
         tcopy(B("dkf"), IND(B("ramp"), B("dkU")))
         act(B("bF"), IND(B("ramp", 0, V), B("bU")), F.Copy)
-        act(B("Xb"), IND(B("Xw", 0, V), B("bU")), F.Copy)
-        act(B("Fo"), IND(B("Kw", 0, V), B("bU")), F.Identity, scale=col(2))
-        act(B("ce"), B("cb", 16, 208), F.Identity, scale=col(3))
+        act(B("Xb"), IND(XW, B("bU")), F.Copy)
+        act(B("Fo"), IND(KW, B("bU")), F.Identity, scale=col(2))
         mm(B("CN", 0, P), B("BO"), B("zero"), True, False)
         for j in range(12):
             w = P - 16 * j
@@ -416,105 +390,96 @@ def rank_program(g, core, T, topo):
         mm(B("CN", 0, P), B("U"), DIAG, False, True)
         mm(B("XB", 0, P), B("ID"), B("Xb"), True, False)
         mm(B("XB", 0, P), B("NID"), B("q"), False, True)
-        if t == 2:
-            sums_out(2)
-            sums(3)
-            sums(4)
         act(B("xr"), B("XB", 0, P), F.Relu, bias=130.0)
-        tt(B("ek"), B("ek"), B("eB"), A.add)
+        if t >= 2:
+            sums_out(3 * (t - 2))
+            sums_out(3 * (t - 2) + 1)
         if jub:
-            tt(B("th"), B("bI"), B(HW, 0, 12), A.subtract)
+            tt(B("th"), B("th"), wall, A.mult)
         scan(B("sc3"), B("CN", 0, P), B("C3"), A.max, A.add)
-        oX = B(HW, 24, 36)
-        tt(B("bxk", 12, 24), B("sc3", 15, P, 16), B("ek"), A.add)
-        tt(B("bxk", 0, 12), B("sc3", 15, P, 16), B("dkB"), A.add)
-        if jub:
-            tt(B("th"), B("th"), B(HW, 12, 24), A.mult)
-        tt(B(HW, 24, 48), B("bxk"), B("DUM"), A.min)
-        tcopy(B(OF), B(HW, 24, 48))
-        ts(B("wU"), oX, float(V), A.is_lt)
-        tcopy(IND(B("Hw"), OK), B("bF"))
-        act(B("hm"), IND(B("Hw", 0, V), B(EU)), F.Copy)
-        if t == NS - 1:
-            dma("Y", ext(T.yh[:]), B("Hw", 0, V, parts=(0, 128, 16)))
-        if t == 2:
-            sums_out(3)
-            sums_out(4)
-        if t == NS - 1:
-            tcopy(IND(B("Xw"), OX), B("xr"))
-            dma("Y", ext(T.yx[:]), B("Xw", 0, V))
+        tt(B("ox"), B("sc3", 15, P, 16), B("dk"), A.add)
+        tt(B("oy"), B("ox"), B("DUM"), A.min)
+        ts(OF, B("oy"), col(11), A.add)
+        ts(B("wU"), B("oy"), col(11), A.add, float(V), A.is_lt)
+        tcopy(IND(B("Hw"), OF), B("bF"))
+        act(B("hm"), IND(HS, B(EU)), F.Copy)
+        if last:
+            dma("Y", ext(T.yh[:]), B("Hw", V, 2 * V, parts=(0, 128, 16)))
+        ts(B("wF"), B("oy"), col(11), A.add, float(V), A.is_lt)
         if jub:
             act(B("wb"), IND(B("ramp", 0, 16), B("wU")), F.Copy)
-            mm(B("Z2", 0, P), B("ID"), B("wb"), True, False)
-            mm(B("Z2", 0, P), B("ID"), B(PR, 0, P), False, True)
-            act(B("pj"), B("Z2", 0, P), F.Relu, bias=15.0, scale=-1.0)
+            mm(B("PP", 0, P), B("ID"), B("wb"), True, False)
+            mm(B("PP", 0, P), B("ID"), B(PR), False, True)
+            act(B("pj"), B("PP", 0, P), F.Relu, bias=15.0, scale=-1.0)
             act(B("pw"), B("pj"), F.Identity, bias=15.0, scale=-1.0)
-            ts(B("wF"), oX, float(V), A.is_lt)
             tt(B("th"), B("th"), B("wF"), A.mult)
+            tcopy(IND(B("Xw"), OF), B("xr"))
+            if last:
+                dma("Y", ext(T.yx[:]), XW)
             tt(B("Aw"), B("th"), B("hW"), A.add)
+            for j in range(16):
+                mm(B("ZC", 0, 12), L("Lw", j), B("C130", 0, 12), j == 0, False)
         else:
-            tt(B("pj"), IND(B("ramp", 0, 16), B("wU")), B(PR, 0, P), A.add)
+            tt(B("pj"), IND(B("ramp", 0, 16), B("wU")), B(PR), A.add)
         if t >= 2:
             yv = "yv%d" % t
-            mm(B("Y1", 0, P), B("WKB"), B("Fo"), True, False)
-            mm(B("Y1", 0, P), B("WKB"), B("ce"), False, True)
-            act(B(yv), B("Y1", 0, P), F.Copy)
+            mm(B("XB", 0, P), B("WKB"), B("Fo"), True, False)
+            mm(B("XB", 0, P), B("WKB"), B("ce"), False, True)
+            act(B(yv), B("XB", 0, P), F.Copy)
+        if t == 2:
+            sums(2)
+            sums_out(2)
         scan(B("sc"), B("hm"), B("C3"), A.max, A.add)
         el = B("sc", 15, 192, 16)
         if jub:
             tt(B("eh"), el, B("nw"), A.mult)
-            tt(B("fin", 0, 12), B("eh"), B("Aw"), A.add)
-            tcopy(B(EO), B("fin", 0, 12))
+            tt(B("fin"), B("eh"), B("Aw"), A.add)
+            tcopy(B(EO), B("fin"))
         else:
-            ts(B(EO), el, col(11), A.add)
-        if t < NS - 1:
-            send(nxt, B("E%d" % (t + 1)), B(EO), "re%d" % (t + 1), NE)
-        if not jub:
             ts(B(PO), B("pj"), 15.0, A.min)
-            send(nxt, B("PR%d" % (t + 1), 0, P), B(PO), "rp%d" % (t + 1), NP)
+            ts(B(EO), el, col(11), A.add)
+        if last:
+            send(home, B("rE"), B(EO), "rg")
+        else:
+            send(nxt, B("E%d" % (t + 1)), B(EO), "re%d" % (t + 1))
+        if not jub:
+            send(nxt, B("PR%d" % (t + 1)), B(PO), "rp%d" % (t + 1))
+            tt(B("th"), B("th"), B("wF"), A.mult)
+            tt(IND(B("Kw"), OF), B("Fo"), B("ce"), A.add)
+            tt(hh, B("th"), hh, A.add)
+            tcopy(IND(B("Xw"), OF), B("xr"))
             if t == 0:
-                send(nxt, B(HN, 24, 36), B(HW, 24, 36), "ro1", NE)
+                send(nxt, B(HN, 0, 12), hh, "rh1")
             else:
-                send(nxt, B(HN, 0, 36), B(HW, 0, 36), "rh%d" % (t + 1), NE)
-            tt(IND(B("Kw"), OK), B("Fo"), B("ce"), A.add)
-        if t < NS - 1:
-            tcopy(IND(B("Xw"), OX), B("xr"))
-        if jub:
-            tt(B("pj"), IND(B("Xw", 0, V), B(EO)), B("pw"), A.add)
+                send(nxt, B(HN), B(HW), "rh%d" % (t + 1))
+                tcopy(IND(B("Yw"), OF), B("yv2"))
+        else:
+            tt(B("pj"), IND(XW, B(EO)), B("pw"), A.add)
             ts(B("ph"), B("pj"), 0.5, A.mult, 129.75, A.add)
-            mm(B("SS", 0, P), B("BW"), B("ph"), True, True)
-            if t < NS - 1:
-                ts(B(PO), B("ph"), -130.0, A.add)
-                send(nxt, B("PR%d" % (t + 1), 0, P), B(PO), "rp%d" % (t + 1), NP)
-                tt(IND(B("Kw"), OK), B("Fo"), B("ce"), A.add)
-
-            def holders(t=t, HW=HW, HN=HN):
-                def home():
-                    if t < NS - 1:
-                        tt(B(HW, 0, 12), B("uI"), B("gg"), A.add)
-                        send(nxt, B(HN, 0, 24), B(HW, 0, 24), "rh%d" % (t + 1), NE)
-                    else:
-                        tt(B("fin", 12, 24), B("uI"), B("gg"), A.add)
-                        send(cores[(rank - t) % n], B("rfin"), B("fin"), "rf", NE)
-                return [lambda: scan(B("sc3"), B("SS", 0, P), B("C3"), A.max, A.add),
-                        lambda: ts(B("sI"), B("sc3", 15, P, 16), col(12), A.add),
-                        lambda: ts(B("uI"), B("sI"), 4095, A.bitwise_and),
-                        lambda: ts(B("gg"), B("uI"), float(V), A.is_ge, -float(V), A.mult),
-                        home]
-            if t == NS - 1:
-                for f in holders():
-                    f()
+            for j in range(16):
+                rhs = B("ph", 12 * j, 12 * j + 12) if last else B("ph", j, P, 16)
+                mm(B("ZC", 0, 12), L("Lw", j), rhs, False, j == 15)
+            if last:
+                tcopy(IND(B("Yw"), OF), B("yv3"))
+                dma("Y", ext(T.yk[:]), B("Yw", V, 2 * V, parts=(0, 128, 16)))
             else:
-                late = holders()
-    tcopy(IND(B("Yw"), B("of0", 12, 24)), B("yv2"))
-    tcopy(IND(B("Yw"), B("of1", 12, 24)), B("yv3"))
-    dma("Y", ext(T.yk[:]), B("Yw", 0, V, parts=(0, 128, 16)))
-    arrive("rfin", 0, 24, cores[(rank + NS - 1) % n], "rf", NE)
-    tcopy(B("rU"), B("rfin"))
-    tcopy(B("outf", 0, P), IND(B("ramp", 0, V), B("rU", 0, 12)))
-    act(B("outf", P, 2 * P), IND(B("ramp", 0, V), B("rU", 12, 24)), F.Copy)
-    dma("Y", ext(T.yo[:]), B("outf", 0, P, parts=(0, 128, 16)))
-    dma("S", ext(T.yt[:]), B("outf", P, 2 * P, parts=(0, 128, 16)))
+                ts(B(PO), B("ph"), -130.0, A.add)
+                send(nxt, B("PR%d" % (t + 1)), B(PO), "rp%d" % (t + 1))
+                tt(IND(B("Kw"), OF), B("Fo"), B("ce"), A.add)
+            tcopy(B("sI"), B("ZC", 0, 12))
+            ts(B("uI"), B("sI"), 4095, A.bitwise_and)
+            ts(B("gg"), B("uI"), float(V), A.is_ge, -float(V), A.mult)
+            if last:
+                tt(B("hh"), B("uI"), B("gg"), A.add)
+                send(home, B("rh"), B("hh"), "rf")
+            else:
+                tt(hh, B("uI"), B("gg"), A.add)
+                send(nxt, B(HN), B(HW), "rh%d" % (t + 1))
+    arrive("rE", 0, 12, away, "rg")
+    act(B("outf"), IND(B("ramp", 0, V), B("rE")), F.Copy)
+    dma("S", ext(T.yo[:]), B("outf", 0, P, parts=(0, 128, 16)))
+    arrive("rh", 0, 12, away, "rf")
+    dma("Y", ext(T.yt[:]), B("rh"))
     g.wait_ge(T.sem["ls"], sent[0])
     for i in range(ndma[0]):
         g.wait_ge(T.sem["dm%d" % i], 16)

@@ -5,7 +5,8 @@ W = 2 * V + P
 BIG, LOW = 2.0 ** 21, 2.0 ** 23
 OFF = 240.0 * 65536
 RND = 1.5 * 2.0 ** 39
-NV = 2
+NV = 4
+HALF = V // 2
 A = AluOpType
 F = ActivationFunctionType
 
@@ -16,22 +17,22 @@ def _b(name, cols, d, where="sbuf"):
     SCRATCH[name] = (where, [128] + (cols if isinstance(cols, list) else [cols]), d)
 
 
-for _n, _c in (("Kw", W), ("Hw", W), ("Yw", W), ("ramp", 2 * V), ("cb", 224), ("tr", 416), ("jlrow", 192), ("C3", 192),
-               ("c3t", 192), ("sc3", 192), ("K0", 192), ("keys", 192), ("rA", 192), ("RST", 192), ("sk", 192), ("sc", 192),
-               ("bF", 192), ("Fo", 192), ("ce", 192), ("hm", 192), ("DUM", 12), ("dm0", 12), ("cols", 16), ("eF", 12), ("fe", 12),
-               ("fo", 12), ("dk", 12), ("ox", 12), ("oy", 12), ("wF", 12), ("th", 12), ("hW", 12), ("Aw", 12), ("nw", 12), ("eh", 12),
-               ("fin", 12), ("hh", 12), ("rh", 12), ("outf", 192), ("WKB", 128), ("yv2", 192), ("yv3", 192), ("gg", 12),
+for _n, _c in (("Kw", W), ("Hw", W), ("Yw", W), ("ramp", 2 * V), ("cb", 224), ("tr", 416), ("sc3", 192), ("K0", 192), ("keys", 192),
+               ("rA", 192), ("RST", 192), ("sk", 192), ("sc", 192), ("bF", 192), ("dkF", 192), ("pw", 192), ("IDF", 128),
+               ("Fo", 192), ("ce", 192), ("hm", 192), ("DUM", 12), ("dm0", 12), ("cols", 16), ("eF", 12), ("fe", 12),
+               ("fo", 12), ("dk", 12), ("oy", 12), ("wF", 12), ("th", 12), ("hW", 12), ("Aw", 12), ("nw", 12), ("eh", 12),
+               ("fin", 12), ("hh", 12), ("rh", 12), ("outf", 192), ("WKB", 128), ("yv2", 192), ("yv3", 192),
                ("s2", 12), ("s3", 12)):
     _b(_n, _c, "float32")
 for _n, _c in (("Xw", W), ("wk", [12, 256]), ("eq", [12, 192]), ("crow", 288), ("L32", 288), ("Lw", 288), ("BO", 128),
-               ("U", 128), ("grow", 128), ("irow", 128), ("mrow", 128), ("gt", 128), ("zero", 192), ("q", 192), ("ID", 128), ("ID2", 128),
-               ("NID", 128), ("C16", 64), ("Cm", 192), ("C130", 16), ("Xb", 192), ("xr", 192), ("pw", 192), ("pj", 192), ("wb", 192),
-               ("ph", 192)):
+               ("U", 128), ("grow", 128), ("mrow", 128), ("zero", 192), ("q", 192), ("ID", 128), ("ID2", 128),
+               ("NID", 128), ("C16", 64), ("Cm", 192), ("C260", 16), ("Xb", 192), ("xr", 192), ("p15", 192), ("wb", 192),
+               ("ph", 192), ("jlrow", 192), ("C3", 192), ("c3t", 192)):
     _b(_n, _c, "bfloat16")
 for _n, _c in (("tk", [12, 256]), ("L64", 288)):
     _b(_n, _c, "float16")
-for _n, _c in (("ki", V), ("own_s", 12), ("hold_s", 12), ("wall_s", 12), ("wt_s", 1), ("ci", 8), ("KEY", 12), ("bI", 12), ("sI", 12),
-               ("uI", 12)):
+for _n, _c in (("ki", V), ("own_s", 12), ("hold_s", 12), ("wall_s", 12), ("wt_s", 1), ("ci", 8), ("KEY", 12), ("bI", 12), ("sI", 24),
+               ("uI", 24)):
     _b(_n, _c, "int32")
 for _n, _c in (("SELk", 12), ("cbu", 192), ("bU", 12), ("dkU", 12), ("dkf", 192), ("of0", 12), ("of1", 12),
                ("wU", 12), ("rE", 12)):
@@ -73,7 +74,7 @@ def rank_program(g, core, T, topo):
             ap = t[parts[0]:parts[1]:parts[2], lo:hi]
         return (ap, [(name, lo, hi)], [])
 
-    def R(name, ap, lo=0, hi=16):
+    def R(name, ap, lo, hi):
         return (ap, [(name, lo, hi)], [])
 
     def IND(win, off):
@@ -192,8 +193,9 @@ def rank_program(g, core, T, topo):
         o = 15 - j if j % 2 else 144 + 16 - j
         return B(name, o, o + 128)
 
+    dma("Y", B("ki", 0, HALF), ext(T.kin[:, 0:HALF]))
     dma("Y", B("own_s"), ext(T.own[:]))
-    dma("Y", B("ki"), ext(T.kin[:]))
+    dma("Y", B("ki", HALF, V), ext(T.kin[:, HALF:V]))
     dma("Y", B("Xw", 0, V), ext(T.x[:]))
     dma("Y", B("PR0"), ext(T.price[:]))
     dma("Y", B("wall_s"), ext(T.wall[:]))
@@ -201,57 +203,57 @@ def rank_program(g, core, T, topo):
     dma("Y", B("wt_s"), ext(T.wt[:]))
 
     RB = V // 4
-    iota(col(9), [[0, 1]], 0, 1)
-    iota(B("ramp", 0, RB), [[1, RB]], 0, 0)
-    iota(B("s2"), [[32, 6], [16, 2]], 0, 0)
-    iota(B("s3"), [[0, 6], [1, 2]], 0, 0)
+    iota(ci(6), [[0, 1]], 0, 1)
     iota(B("crow"), [[-1, 2], [1, 144]], 0, 0)
+    iota(B("ramp", 0, RB), [[1, RB]], 0, 0)
     iota(B("mrow"), [[1, 128]], 0, 0)
     iota(B("jlrow"), [[0, 12], [1, 16]], 0, 0)
     iota(B("grow"), [[1, 8], [0, 16]], 0, 0)
-    iota(B("irow"), [[0, 8], [1, 16]], 0, 0)
+    iota(B("s2"), [[32, 6], [16, 2]], 0, 0)
+    iota(B("s3"), [[0, 6], [1, 2]], 0, 0)
     iota(B("dm0"), [[16, 12]], 2 * V, 0)
-    iota(B("Hw", V, 2 * V), [[1, V]], 0, 0)
     for a in (RB, 2 * RB, 4 * RB):
         act(B("ramp", a, 2 * a), B("ramp", 0, a), F.Identity, bias=float(a))
     fill(B("cb"), 0.0)
-    tcopy(ci(6), col(9))
-    fill(B("zero"), 0.0)
-    fill(B("C16"), 16384.0)
     ts(ci(0), ci(6), 15, A.bitwise_and)
     ts(ci(1), ci(6), 4, A.logical_shift_right)
     ts(ci(2), ci(6), 1, A.bitwise_and)
     ts(ci(3), ci(6), 4, A.logical_shift_right, 1, A.bitwise_and)
-    fill(B("Cm"), -32.0)
+    tcopy(col(9), ci(6))
+    fill(B("RST"), -4096.0)
     tcopy(B("cols", 0, 4), B("ci", 0, 4))
-    fill(B("C130"), -130.0)
+    fill(B("zero"), 0.0)
+    fill(B("C16"), 16384.0)
+    ts(col(13), col(1), 16.0, A.mult, 15.0, A.add)
+    ts(col(8), col(0), 0.0, A.is_equal, -LOW, A.mult)
     ts(col(6), col(2), -1.0, A.mult, 1.0, A.add)
     ts(col(10), col(3), -416.0, A.mult, 208.0, A.add)
     ts(col(12), col(3), 208.0, A.mult, col(0), A.add)
-    ts(col(13), col(1), 16.0, A.mult, 15.0, A.add)
     ts(col(15), col(0), 1.0, A.add)
-    ts(B("s3"), B("s3"), col(10), A.mult, col(12), A.add)
+    ts(col(11), col(8), -1.0, A.mult, -BIG, A.add)
+    fill(B("RST", 0, P, 16), 2.0 ** 26)
+    fill(B("Cm"), -32.0)
+    fill(B("C260"), -260.0)
     ts(B("L64"), B("crow"), col(13), A.is_equal, 64.0, A.mult)
-    tt(B("s2"), B("s2"), B("s3"), A.add)
     ts(B("L32"), B("crow"), col(13), A.is_equal, -32.0, A.mult)
+    tcopy(B("Kw", V, V + HALF), B("ki", 0, HALF))
     ts(B("ID"), B("mrow"), col(9), A.is_equal)
-    tcopy(B("SELk"), B("s2"))
     ts(B("ID2"), B("mrow"), col(9), A.is_equal, 2048.0, A.mult)
     ts(B("NID"), B("mrow"), col(9), A.is_equal, -1.0, A.mult)
+    ts(B("IDF"), B("mrow"), col(9), A.is_equal)
     tcopy(B("E0"), B("own_s"))
-    ts(B("RST"), B("jlrow"), 0.0, A.is_equal, 2.0 ** 26, A.mult)
     ts(B("c3t"), B("jlrow"), col(0), A.is_lt, -LOW, A.mult)
     ts(B("C3"), B("jlrow"), col(0), A.is_equal, BIG, A.mult)
-    ts(col(8), col(0), 0.0, A.is_equal, -LOW, A.mult)
-    ts(B("RST"), B("RST"), -4096.0, A.add)
-    tt(B("C3"), B("C3"), B("c3t"), A.add)
-    ts(col(11), col(8), -1.0, A.mult, -BIG, A.add)
     ts(B("BO"), B("grow"), col(1), A.is_equal, 8192.0, A.mult)
-    ts(B("C3", 15, P, 16), B("C3", 15, P, 16), col(8), A.add)
-    ts(B("gt"), B("irow"), col(0), A.is_gt)
+    tt(B("C3"), B("C3"), B("c3t"), A.add)
     ts(B("WKB"), B("grow"), col(1), A.is_equal, col(15), A.mult)
+    ts(B("C3", 15, P, 16), B("C3", 15, P, 16), col(8), A.add)
+    ts(B("s3"), B("s3"), col(10), A.mult, col(12), A.add)
     ts(B("DUM"), B("dm0"), col(0), A.add, col(11), A.subtract)
-    tt(B("U"), B("BO"), B("gt"), A.mult)
+    tt(B("s2"), B("s2"), B("s3"), A.add)
+    op("G", lambda: g.affine_select(T.U[:], T.BO[:], [[1, 128]], A.is_gt, 0.0, 0, -1), B("U"), [B("BO")])
+    iota(B("Hw", V, 2 * V), [[1, V]], 0, 0)
+    tcopy(B("SELk"), B("s2"))
 
     DIAG = (T.eq[:, :, 0:16], [("eq", 0, 192)], [])
     nxt = cores[(rank + 1) % n]
@@ -260,11 +262,13 @@ def rank_program(g, core, T, topo):
     away = cores[(rank + NS - 1) % n]
     XW, KW, HS = B("Xw", 0, V), B("Kw", V, 2 * V), B("Hw", V, 2 * V)
 
+    YB = ("Y0", "Y1", "ZA", "Y0", "Y1")
+
     def sums(i):
-        mm(B("Y%d" % (i % 2)), B("WKB"), B("Kw", V + 512 * i, V + 512 * i + 512), True, True)
+        mm(B(YB[i]), B("WKB"), B("Kw", V + 512 * i, V + 512 * i + 512), True, True)
 
     def sums_out(i):
-        act(B("Yw", V + 512 * i, V + 512 * i + 512), B("Y%d" % (i % 2)), F.Copy)
+        act(B("Yw", V + 512 * i, V + 512 * i + 512), B(YB[i]), F.Copy)
 
     def moving(c, buf, j):
         return R(buf, T[buf][:, 4 * c:4 * c + 4, 16 * j:16 * j + 16], 16 * c, 16 * c + 16)
@@ -280,6 +284,11 @@ def rank_program(g, core, T, topo):
         for j in range(16):
             mm(Z(c, 0), L("L32", j), moving(c, "wk", j), False, False)
 
+    def greater(c):
+        for k in range(16):
+            tt(R("tk", T.tk[:, 4 * c:4 * c + 4, k::16], 16 * c + k, 16 * c + k + 1),
+               R("wk", T.wk[:, 4 * c:4 * c + 4, k::16], 16 * c, 16 * c + 16), B("PP", 64 * c, 64 * c + 64), A.max)
+
     def maxima(c):
         for j in range(16):
             mm(Z(c, 0), L("L64", j), moving(c, "tk", j), False, j == 15)
@@ -287,11 +296,10 @@ def rank_program(g, core, T, topo):
     def decode(c):
         return [lambda: ts(part("rA", c), Z(c, 0), RND, A.add, RND, A.subtract),
                 lambda: tt(Z(c, 1), Z(c, 0), part("rA", c), A.is_lt),
-                lambda: tt(Z(c, 2), Z(c, 1), part("rA", c), A.mult)]
+                lambda: tt(Z(c, 2), Z(c, 1), part("rA", c), A.mult),
+                lambda: tt(part("keys", c), Z(c, 2), part("K0", c), A.add)]
 
-    def key(c):
-        tt(part("keys", c), Z(c, 2), part("K0", c), A.add)
-
+    late = []
     for t in range(NS):
         jub = t % 2 == 1
         last = t == NS - 1
@@ -308,79 +316,72 @@ def rank_program(g, core, T, topo):
         tcopy(B("cbu", 0, 64), IND(kw, B(EU, 0, 4)))
         tcopy(B("cbu", 64, P), IND(kw, B(EU, 4, 12)))
         ts(B("eF"), B(EU), V - OFF, A.add)
+        if t == 0:
+            tcopy(B("Kw", V + HALF, 2 * V), B("ki", HALF, V))
         blocks = [(R("wk", T.wk[:, a, :], 4 * a, 4 * a + 4), IND(XW, B("cbu", 16 * a, 16 * a + 16))) for a in range(12)]
         for o, i in blocks[:8 - NV] + blocks[8:]:
             act(o, i, F.Identity, scale=2048.0)
-        tcopy(B("cb", 16, 208), B("cbu"))
-        if t == 0:
-            tcopy(KW, B("ki"))
+        act(B("cb", 16, 208), IND(KW, B(EU)), F.Copy)
         for o, i in blocks[8 - NV:8]:
             ts(o, i, 2048.0, A.mult)
         mm(B("PP", 0, P), B("ID"), B("Cm"), True, False)
         mm(B("PP", 0, P), B("ID2"), B(PR), False, True)
-        side = []
+        linear(0)
+        linear(1)
+        greater(0)
+        maxima(0)
+        greater(1)
+        linear(2)
+        maxima(1)
+        greater(2)
+        maxima(2)
+        if t >= 2:
+            sums(3 * (t - 2))
+            sums(3 * (t - 2) + 1)
+        act(B("q"), B(PR), F.Identity, bias=129.625, scale=0.25)
+        act(B("ce"), B("cb", 16, 208), F.Identity, scale=col(6))
+        op("V", lambda: g.vector.transpose(T.tr[:, 0:192], T.cb[:, 16:208]), B("tr", 0, 192), [B("cb", 16, 208)])
+        op("V", lambda: g.vector.transpose(T.tr[:, 192:416], T.cb[:, 0:224]), B("tr", 192, 416), [B("cb")])
+        act(B("K0"), IND(B("tr"), B("SELk")), F.Identity, bias=-OFF)
+        d0, d1, d2 = decode(0), decode(1), decode(2)
+        for f in (d0[0], d1[0], d0[1], d1[1], d2[0], d0[2], d1[2], d2[1], d0[3], d2[2], d1[3], d2[3]):
+            f()
+        side = late
+        late = []
         if t == 0:
-            side = [lambda: tcopy(B(HW, 12, 24), B("wall_s")),
-                    lambda: tcopy(B(HW, 0, 12), B("hold_s")),
-                    lambda: send(nxt, B(HN, 12, 24), wall, "rw1"),
-                    lambda: tcopy(col(7), B("wt_s")),
-                    lambda: None,
-                    lambda: ts(B("Lw"), B("crow"), col(13), A.is_equal, col(7), A.mult)]
+            side += [lambda: tcopy(B(HW, 12, 24), B("wall_s")),
+                     lambda: tcopy(B(HW, 0, 12), B("hold_s")),
+                     lambda: (send(nxt, B(HN, 12, 24), wall, "rw1"), tcopy(col(7), B("wt_s")))]
         if jub:
-            side = [lambda: ts(B("nw"), wall, -1.0, A.mult, 1.0, A.add),
-                    lambda: tt(B("hW"), hh, wall, A.mult),
-                    lambda: ts(B("Aw"), B("nw"), col(11), A.mult),
-                    lambda: None,
-                    lambda: tt(B("hW"), B("hW"), B("Aw"), A.add)]
+            side += [lambda: ts(B("nw"), wall, -1.0, A.mult, 1.0, A.add),
+                     lambda: tt(B("hW"), hh, wall, A.mult),
+                     lambda: ts(B("Aw"), B("nw"), col(11), A.mult),
+                     lambda: tt(B("hW"), B("hW"), B("Aw"), A.add)]
 
         def fillers():
             if side:
                 side.pop(0)()
-        for c in range(3):
-            linear(c)
-            for k in range(16):
-                tt(R("tk", T.tk[:, 4 * c:4 * c + 4, k::16], 16 * c + k, 16 * c + k + 1),
-                   R("wk", T.wk[:, 4 * c:4 * c + 4, k::16], 16 * c, 16 * c + 16), B("PP", 64 * c, 64 * c + 64), A.max)
-                if c == 1 and k >= 10 and k % 2:
-                    fillers()
-            maxima(c)
-            if c == 0:
-                side = decode(0) + side
-            if c == 1:
-                op("V", lambda: g.vector.transpose(T.tr[:, 0:192], T.cb[:, 16:208]), B("tr", 0, 192), [B("cb", 16, 208)])
-                op("V", lambda: g.vector.transpose(T.tr[:, 192:416], T.cb[:, 0:224]), B("tr", 192, 416), [B("cb")])
-                act(B("K0"), IND(B("tr"), B("SELk")), F.Identity, bias=-OFF)
-                act(B("q"), B(PR), F.Identity, bias=129.625, scale=0.25)
-                act(B("ce"), B("cb", 16, 208), F.Identity, scale=col(6))
-                while side:
-                    fillers()
-        if t >= 2:
-            sums(3 * (t - 2))
-            sums(3 * (t - 2) + 1)
-        d1 = decode(1)
-        d1[0]()
-        key(0)
-        d1[1]()
-        d1[2]()
-        key(1)
-        for f in decode(2):
-            f()
-        key(2)
+        fillers()
         scan(B("sk"), B("RST"), B("keys"), A.add, A.min)
         sv = B("sk", 15, P, 16)
+        fillers()
         tcopy(B("KEY"), sv)
         tt(B("fo"), sv, B("eF"), A.min)
         ts(B("bI"), B("KEY"), 4095, A.bitwise_and)
         ts(B("fe"), B("fo"), OFF, A.add)
+        fillers()
         tt(B("dk"), B("fe"), B("bI"), A.max)
         tcopy(B("bU"), B("bI"))
         tcopy(B("dkU"), B("dk"))
-        tt(B("th"), B("bI"), hh, A.subtract)
+        fillers()
         tcopy(B("dkf"), IND(B("ramp"), B("dkU")))
-        act(B("bF"), IND(B("ramp", 0, V), B("bU")), F.Copy)
+        fillers()
+        act(B("dkF"), IND(B("ramp"), B("dkU")), F.Copy)
         act(B("Xb"), IND(XW, B("bU")), F.Copy)
+        act(B("bF"), IND(B("ramp", 0, V), B("bU")), F.Copy)
         act(B("Fo"), IND(KW, B("bU")), F.Identity, scale=col(2))
         mm(B("CN", 0, P), B("BO"), B("zero"), True, False)
+        mm(B("CN", 0, P), B("IDF"), B("dkF"), False, False)
         for j in range(12):
             w = P - 16 * j
             op("V", lambda: g.vector.tensor_scalar(T.eq[:, j, 0:w], T.dkf[:, 16 * j:P], T.dk[:, j:j + 1], None, A.is_equal),
@@ -391,43 +392,47 @@ def rank_program(g, core, T, topo):
         mm(B("XB", 0, P), B("ID"), B("Xb"), True, False)
         mm(B("XB", 0, P), B("NID"), B("q"), False, True)
         act(B("xr"), B("XB", 0, P), F.Relu, bias=130.0)
+        if t == 2:
+            sums(2)
         if t >= 2:
             sums_out(3 * (t - 2))
-            sums_out(3 * (t - 2) + 1)
+        while side:
+            fillers()
+        if jub:
+            tt(B("th"), B("bI"), hh, A.subtract)
+        if t == 0:
+            ts(B("Lw"), B("crow"), col(13), A.is_equal, col(7), A.mult)
+        scan(B("sc3"), B("CN", 0, P), B("C3"), A.max, A.add)
         if jub:
             tt(B("th"), B("th"), wall, A.mult)
-        scan(B("sc3"), B("CN", 0, P), B("C3"), A.max, A.add)
-        tt(B("ox"), B("sc3", 15, P, 16), B("dk"), A.add)
-        tt(B("oy"), B("ox"), B("DUM"), A.min)
+        tt(B("oy"), B("sc3", 15, P, 16), B("DUM"), A.min)
         ts(OF, B("oy"), col(11), A.add)
         ts(B("wU"), B("oy"), col(11), A.add, float(V), A.is_lt)
         tcopy(IND(B("Hw"), OF), B("bF"))
+        act(B("wb"), IND(B("ramp", 0, 16), B("wU")), F.Copy)
         act(B("hm"), IND(HS, B(EU)), F.Copy)
         if last:
             dma("Y", ext(T.yh[:]), B("Hw", V, 2 * V, parts=(0, 128, 16)))
         ts(B("wF"), B("oy"), col(11), A.add, float(V), A.is_lt)
+        mm(B("PP", 0, P), B("ID"), B("wb"), True, False)
+        mm(B("PP", 0, P), B("ID"), B(PR), False, True)
+        act(B("p15"), B("PP", 0, P), F.Relu, bias=15.0, scale=-1.0)
+        act(B("pw" if jub else PO), B("p15"), F.Identity, bias=274.5 if jub else 15.0, scale=-1.0)
         if jub:
-            act(B("wb"), IND(B("ramp", 0, 16), B("wU")), F.Copy)
-            mm(B("PP", 0, P), B("ID"), B("wb"), True, False)
-            mm(B("PP", 0, P), B("ID"), B(PR), False, True)
-            act(B("pj"), B("PP", 0, P), F.Relu, bias=15.0, scale=-1.0)
-            act(B("pw"), B("pj"), F.Identity, bias=15.0, scale=-1.0)
             tt(B("th"), B("th"), B("wF"), A.mult)
-            tcopy(IND(B("Xw"), OF), B("xr"))
             if last:
+                tcopy(IND(B("Xw"), OF), B("xr"))
                 dma("Y", ext(T.yx[:]), XW)
             tt(B("Aw"), B("th"), B("hW"), A.add)
             for j in range(16):
-                mm(B("ZC", 0, 12), L("Lw", j), B("C130", 0, 12), j == 0, False)
-        else:
-            tt(B("pj"), IND(B("ramp", 0, 16), B("wU")), B(PR), A.add)
+                mm(B("ZC", 0, 12), L("Lw", j), B("C260", 0, 12), j == 0, False)
         if t >= 2:
             yv = "yv%d" % t
+            sums_out(3 * (t - 2) + 1)
             mm(B("XB", 0, P), B("WKB"), B("Fo"), True, False)
             mm(B("XB", 0, P), B("WKB"), B("ce"), False, True)
             act(B(yv), B("XB", 0, P), F.Copy)
         if t == 2:
-            sums(2)
             sums_out(2)
         scan(B("sc"), B("hm"), B("C3"), A.max, A.add)
         el = B("sc", 15, 192, 16)
@@ -436,7 +441,6 @@ def rank_program(g, core, T, topo):
             tt(B("fin"), B("eh"), B("Aw"), A.add)
             tcopy(B(EO), B("fin"))
         else:
-            ts(B(PO), B("pj"), 15.0, A.min)
             ts(B(EO), el, col(11), A.add)
         if last:
             send(home, B("rE"), B(EO), "rg")
@@ -444,37 +448,38 @@ def rank_program(g, core, T, topo):
             send(nxt, B("E%d" % (t + 1)), B(EO), "re%d" % (t + 1))
         if not jub:
             send(nxt, B("PR%d" % (t + 1)), B(PO), "rp%d" % (t + 1))
-            tt(B("th"), B("th"), B("wF"), A.mult)
             tt(IND(B("Kw"), OF), B("Fo"), B("ce"), A.add)
-            tt(hh, B("th"), hh, A.add)
+            tt(B("th"), B("bI"), hh, A.subtract)
             tcopy(IND(B("Xw"), OF), B("xr"))
+            tt(B("th"), B("th"), B("wF"), A.mult)
+            tt(hh, B("th"), hh, A.add)
             if t == 0:
                 send(nxt, B(HN, 0, 12), hh, "rh1")
             else:
                 send(nxt, B(HN), B(HW), "rh%d" % (t + 1))
-                tcopy(IND(B("Yw"), OF), B("yv2"))
         else:
-            tt(B("pj"), IND(XW, B(EO)), B("pw"), A.add)
-            ts(B("ph"), B("pj"), 0.5, A.mult, 129.75, A.add)
+            if not last:
+                tcopy(IND(B("Xw"), OF), B("xr"))
+            tt(B("ph"), IND(XW, B(EO)), B("pw"), A.add)
             for j in range(16):
                 rhs = B("ph", 12 * j, 12 * j + 12) if last else B("ph", j, P, 16)
                 mm(B("ZC", 0, 12), L("Lw", j), rhs, False, j == 15)
+            if not last:
+                ts(B(PO), B("ph"), -260.0, A.add, 0.5, A.mult)
+                send(nxt, B("PR%d" % (t + 1)), B(PO), "rp%d" % (t + 1))
+                tt(IND(B("Kw"), OF), B("Fo"), B("ce"), A.add)
+            ts(B("sI", 0, 12), B("ZC", 0, 12), 0.5, A.mult)
+            ts(B("sI", 12, 24), B("ZC", 0, 12), 0.5, A.mult, -float(V), A.add)
+            late = [lambda: ts(B("uI"), B("sI"), 4095, A.bitwise_and)]
             if last:
+                late.pop()()
+                tt(B("hh"), B("uI", 0, 12), B("uI", 12, 24), A.min)
+                send(home, B("rh"), B("hh"), "rf")
+                tcopy(IND(B("Yw"), B("of0")), B("yv2"))
                 tcopy(IND(B("Yw"), OF), B("yv3"))
                 dma("Y", ext(T.yk[:]), B("Yw", V, 2 * V, parts=(0, 128, 16)))
             else:
-                ts(B(PO), B("ph"), -130.0, A.add)
-                send(nxt, B("PR%d" % (t + 1)), B(PO), "rp%d" % (t + 1))
-                tt(IND(B("Kw"), OF), B("Fo"), B("ce"), A.add)
-            tcopy(B("sI"), B("ZC", 0, 12))
-            ts(B("uI"), B("sI"), 4095, A.bitwise_and)
-            ts(B("gg"), B("uI"), float(V), A.is_ge, -float(V), A.mult)
-            if last:
-                tt(B("hh"), B("uI"), B("gg"), A.add)
-                send(home, B("rh"), B("hh"), "rf")
-            else:
-                tt(hh, B("uI"), B("gg"), A.add)
-                send(nxt, B(HN), B(HW), "rh%d" % (t + 1))
+                late += [lambda hh=hh, HN=HN, HW=HW: (tt(hh, B("uI", 0, 12), B("uI", 12, 24), A.min), send(nxt, B(HN), B(HW), "rh2"))]
     arrive("rE", 0, 12, away, "rg")
     act(B("outf"), IND(B("ramp", 0, V), B("rE")), F.Copy)
     dma("S", ext(T.yo[:]), B("outf", 0, P, parts=(0, 128, 16)))

@@ -7,6 +7,8 @@ OFF = 240.0 * 65536
 RND = 1.5 * 2.0 ** 39
 NV = 4
 HALF = V // 2
+EARLY = HALF + 256
+XH = 6
 A = AluOpType
 F = ActivationFunctionType
 
@@ -17,25 +19,24 @@ def _b(name, cols, d, where="sbuf"):
     SCRATCH[name] = (where, [128] + (cols if isinstance(cols, list) else [cols]), d)
 
 
-for _n, _c in (("Kw", W), ("Hw", W), ("Yw", W), ("ramp", 2 * V), ("cb", 224), ("tr", 416), ("sc3", 192), ("K0", 192), ("keys", 192),
-               ("rA", 192), ("RST", 192), ("sk", 192), ("sc", 192), ("bF", 192), ("dkF", 192), ("pw", 192), ("IDF", 128),
-               ("Fo", 192), ("ce", 192), ("hm", 192), ("DUM", 12), ("dm0", 12), ("cols", 16), ("eF", 12), ("fe", 12),
-               ("fo", 12), ("dk", 12), ("oy", 12), ("wF", 12), ("th", 12), ("hW", 12), ("Aw", 12), ("nw", 12), ("eh", 12),
-               ("fin", 12), ("hh", 12), ("rh", 12), ("outf", 192), ("WKB", 128), ("yv2", 192), ("yv3", 192),
-               ("s2", 12), ("s3", 12)):
+for _n, _c in (("Kw", W), ("Hw", W + 16), ("Yw", W), ("ramp", 2 * V), ("cb", 224), ("tr", 416), ("sc3", 192), ("K0", 192), ("keys", 192),
+               ("rA", 192), ("RST", 192), ("RS2", 192), ("sk", 192), ("sz", 192), ("sc", 192), ("bF", 192), ("dkF", 192), ("pw", 192),
+               ("IDF", 128), ("Fo", 192), ("ce", 192), ("hm", 192), ("DUM", 12), ("dm0", 12), ("cols", 16), ("eF", 12),
+               ("dk", 12), ("oy", 12), ("wF", 12), ("th", 12), ("hW", 12), ("Aw", 12), ("nw", 12),
+               ("fin", 12), ("hh", 12), ("outf", 192), ("WKB", 128), ("yv2", 192), ("yv3", 192), ("s2", 12), ("s3", 12)):
     _b(_n, _c, "float32")
 for _n, _c in (("Xw", W), ("wk", [12, 256]), ("eq", [12, 192]), ("crow", 288), ("L32", 288), ("Lw", 288), ("BO", 128),
-               ("U", 128), ("grow", 128), ("mrow", 128), ("zero", 192), ("q", 192), ("ID", 128), ("ID2", 128),
+               ("U", 128), ("grow", 128), ("mrow", 128), ("q", 192), ("ID", 128), ("ID2", 128),
                ("NID", 128), ("C16", 64), ("Cm", 192), ("C260", 16), ("Xb", 192), ("xr", 192), ("p15", 192), ("wb", 192),
                ("ph", 192), ("jlrow", 192), ("C3", 192), ("c3t", 192)):
     _b(_n, _c, "bfloat16")
 for _n, _c in (("tk", [12, 256]), ("L64", 288)):
     _b(_n, _c, "float16")
-for _n, _c in (("ki", V), ("own_s", 12), ("hold_s", 12), ("wall_s", 12), ("wt_s", 1), ("ci", 8), ("KEY", 12), ("bI", 12), ("sI", 24),
-               ("uI", 24)):
+for _n, _c in (("ki", V), ("own_s", 12), ("hold_s", 12), ("wall_s", 12), ("wt_s", 1), ("ci", 8), ("KEY", 12), ("zI", 12), ("bI", 12),
+               ("sI", 24), ("uI", 24)):
     _b(_n, _c, "int32")
 for _n, _c in (("SELk", 12), ("cbu", 192), ("bU", 12), ("dkU", 12), ("dkf", 192), ("of0", 12), ("of1", 12),
-               ("wU", 12), ("rE", 12)):
+               ("wU", 12), ("EW", 12), ("rE", 12)):
     _b(_n, _c, "uint16")
 for _t in range(NS):
     _b("E%d" % _t, 12, "uint16")
@@ -43,10 +44,11 @@ for _t in range(NS):
     _b("PR%d" % _t, 192, "bfloat16")
     _b("PO%d" % _t, 192, "bfloat16")
     _b("HW%d" % _t, 24, "float32")
+_b("rh", 12, "float32", "dram")
 for _n in ("ZA", "ZB", "ZC", "PP", "CN", "XB", "Y0", "Y1"):
     _b(_n, 512, "float32", "psum")
 
-SEMAPHORES = (["qV", "qS", "qT", "qG", "ls"] + ["dm%d" % i for i in range(16)]
+SEMAPHORES = (["qV", "qS", "qT", "qG", "ls"] + ["dm%d" % i for i in range(18)]
               + ["r%s%d" % (a, t) for a in "eph" for t in range(1, NS)] + ["rf", "rg", "rw1"])
 
 
@@ -205,63 +207,67 @@ def rank_program(g, core, T, topo):
     RB = V // 4
     iota(ci(6), [[0, 1]], 0, 1)
     iota(B("crow"), [[-1, 2], [1, 144]], 0, 0)
-    iota(B("ramp", 0, RB), [[1, RB]], 0, 0)
     iota(B("mrow"), [[1, 128]], 0, 0)
-    iota(B("jlrow"), [[0, 12], [1, 16]], 0, 0)
+    iota(B("ramp", 0, RB), [[1, RB]], 0, 0)
     iota(B("grow"), [[1, 8], [0, 16]], 0, 0)
+    iota(B("jlrow"), [[0, 12], [1, 16]], 0, 0)
     iota(B("s2"), [[32, 6], [16, 2]], 0, 0)
     iota(B("s3"), [[0, 6], [1, 2]], 0, 0)
     iota(B("dm0"), [[16, 12]], 2 * V, 0)
-    for a in (RB, 2 * RB, 4 * RB):
-        act(B("ramp", a, 2 * a), B("ramp", 0, a), F.Identity, bias=float(a))
-    fill(B("cb"), 0.0)
+    fill(B("cb", 0, 16), 0.0)
+    fill(B("cb", 208, 224), 0.0)
     ts(ci(0), ci(6), 15, A.bitwise_and)
     ts(ci(1), ci(6), 4, A.logical_shift_right)
     ts(ci(2), ci(6), 1, A.bitwise_and)
     ts(ci(3), ci(6), 4, A.logical_shift_right, 1, A.bitwise_and)
     tcopy(col(9), ci(6))
-    fill(B("RST"), -4096.0)
+    fill(B("Cm"), -32.0)
     tcopy(B("cols", 0, 4), B("ci", 0, 4))
-    fill(B("zero"), 0.0)
     fill(B("C16"), 16384.0)
+    fill(B("C260"), -260.0)
     ts(col(13), col(1), 16.0, A.mult, 15.0, A.add)
     ts(col(8), col(0), 0.0, A.is_equal, -LOW, A.mult)
     ts(col(6), col(2), -1.0, A.mult, 1.0, A.add)
     ts(col(10), col(3), -416.0, A.mult, 208.0, A.add)
     ts(col(12), col(3), 208.0, A.mult, col(0), A.add)
-    ts(col(15), col(0), 1.0, A.add)
+    ts(col(15), col(0), 1.0, A.add, 1.0 / 8192, A.mult)
     ts(col(11), col(8), -1.0, A.mult, -BIG, A.add)
-    fill(B("RST", 0, P, 16), 2.0 ** 26)
-    fill(B("Cm"), -32.0)
-    fill(B("C260"), -260.0)
     ts(B("L64"), B("crow"), col(13), A.is_equal, 64.0, A.mult)
     ts(B("L32"), B("crow"), col(13), A.is_equal, -32.0, A.mult)
-    tcopy(B("Kw", V, V + HALF), B("ki", 0, HALF))
     ts(B("ID"), B("mrow"), col(9), A.is_equal)
-    ts(B("ID2"), B("mrow"), col(9), A.is_equal, 2048.0, A.mult)
-    ts(B("NID"), B("mrow"), col(9), A.is_equal, -1.0, A.mult)
-    ts(B("IDF"), B("mrow"), col(9), A.is_equal)
+    fill(B("RST"), -4096.0)
+    act(B("ID2"), B("ID"), F.Identity, scale=2048.0)
+    act(B("NID"), B("ID"), F.Identity, scale=-1.0)
+    act(B("IDF"), B("ID"), F.Copy)
+    fill(B("RST", 0, P, 16), 2.0 ** 26)
+    act(B("RS2"), B("RST"), F.Identity, scale=2.0)
+    for a in (RB, 2 * RB):
+        act(B("ramp", a, 2 * a), B("ramp", 0, a), F.Identity, bias=float(a))
+    tcopy(B("Kw", V, V + HALF), B("ki", 0, HALF))
     tcopy(B("E0"), B("own_s"))
-    ts(B("c3t"), B("jlrow"), col(0), A.is_lt, -LOW, A.mult)
-    ts(B("C3"), B("jlrow"), col(0), A.is_equal, BIG, A.mult)
     ts(B("BO"), B("grow"), col(1), A.is_equal, 8192.0, A.mult)
-    tt(B("C3"), B("C3"), B("c3t"), A.add)
-    ts(B("WKB"), B("grow"), col(1), A.is_equal, col(15), A.mult)
-    ts(B("C3", 15, P, 16), B("C3", 15, P, 16), col(8), A.add)
+    act(B("WKB"), B("BO"), F.Identity, scale=col(15))
+    ts(B("c3t"), B("jlrow"), col(0), A.is_lt, -LOW, A.mult)
+    ts(B("PP", 0, P), B("jlrow"), col(0), A.is_equal, BIG, A.mult)
     ts(B("s3"), B("s3"), col(10), A.mult, col(12), A.add)
-    ts(B("DUM"), B("dm0"), col(0), A.add, col(11), A.subtract)
+    tt(B("C3"), B("PP", 0, P), B("c3t"), A.add)
     tt(B("s2"), B("s2"), B("s3"), A.add)
-    op("G", lambda: g.affine_select(T.U[:], T.BO[:], [[1, 128]], A.is_gt, 0.0, 0, -1), B("U"), [B("BO")])
-    iota(B("Hw", V, 2 * V), [[1, V]], 0, 0)
+    ts(B("C3", 15, P, 16), B("C3", 15, P, 16), col(8), A.add)
+    ts(B("DUM"), B("dm0"), col(0), A.add, col(11), A.subtract)
     tcopy(B("SELk"), B("s2"))
+    op("G", lambda: g.affine_select(T.U[:], T.BO[:], [[1, 128]], A.is_gt, 0.0, 0, -1), B("U"), [B("BO")])
+    iota(B("ramp", V, 2 * V), [[1, V]], V, 0)
+    iota(B("Hw", 2 * V, W + 16), [[0, P + 16]], 0, 0)
+    need("Y", B("wt_s")[1], [], False)
+    dma("Y", B("Hw", V, 2 * V), B("ramp", 0, V))
 
-    DIAG = (T.eq[:, :, 0:16], [("eq", 0, 192)], [])
     nxt = cores[(rank + 1) % n]
     prv = cores[(rank - 1) % n]
     home = cores[(rank - (NS - 1)) % n]
     away = cores[(rank + NS - 1) % n]
-    XW, KW, HS = B("Xw", 0, V), B("Kw", V, 2 * V), B("Hw", V, 2 * V)
+    XW, KW, HS = B("Xw", 0, V), B("Kw", V, 2 * V), B("Hw", V, W + 16)
 
+    SS = "CN"
     YB = ("Y0", "Y1", "ZA", "Y0", "Y1")
 
     def sums(i):
@@ -303,7 +309,8 @@ def rank_program(g, core, T, topo):
     for t in range(NS):
         jub = t % 2 == 1
         last = t == NS - 1
-        EU, PR, HW, OF = "E%d" % t, "PR%d" % t, "HW%d" % t, B("of%d" % (t % 2))
+        ofn = "of%d" % (t % 2)
+        EU, PR, HW, OF = "E%d" % t, "PR%d" % t, "HW%d" % t, B(ofn)
         EO, PO, HN = "EO%d" % t, "PO%d" % t, "HW%d" % (t + 1)
         hh, wall = B(HW, 0, 12), B(HW, 12, 24)
         if t:
@@ -316,21 +323,30 @@ def rank_program(g, core, T, topo):
         tcopy(B("cbu", 0, 64), IND(kw, B(EU, 0, 4)))
         tcopy(B("cbu", 64, P), IND(kw, B(EU, 4, 12)))
         ts(B("eF"), B(EU), V - OFF, A.add)
-        if t == 0:
-            tcopy(B("Kw", V + HALF, 2 * V), B("ki", HALF, V))
         blocks = [(R("wk", T.wk[:, a, :], 4 * a, 4 * a + 4), IND(XW, B("cbu", 16 * a, 16 * a + 16))) for a in range(12)]
         for o, i in blocks[:8 - NV] + blocks[8:]:
             act(o, i, F.Identity, scale=2048.0)
-        act(B("cb", 16, 208), IND(KW, B(EU)), F.Copy)
+        if t:
+            act(B("cb", 16, 208), IND(KW, B(EU)), F.Copy)
+        else:
+            tcopy(B("cb", 16, 208), B("cbu"))
+            tcopy(B("Kw", V + HALF, V + EARLY), B("ki", HALF, EARLY))
+            late = [lambda: tcopy(wall, B("wall_s")), lambda: send(nxt, B(HN, 12, 24), wall, "rw1")]
         for o, i in blocks[8 - NV:8]:
             ts(o, i, 2048.0, A.mult)
         mm(B("PP", 0, P), B("ID"), B("Cm"), True, False)
         mm(B("PP", 0, P), B("ID2"), B(PR), False, True)
         linear(0)
         linear(1)
+        for f in late[:2]:
+            f()
         greater(0)
+        for f in late[2:3]:
+            f()
         maxima(0)
         greater(1)
+        for f in late[3:]:
+            f()
         linear(2)
         maxima(1)
         greater(2)
@@ -346,49 +362,48 @@ def rank_program(g, core, T, topo):
         d0, d1, d2 = decode(0), decode(1), decode(2)
         for f in (d0[0], d1[0], d0[1], d1[1], d2[0], d0[2], d1[2], d2[1], d0[3], d2[2], d1[3], d2[3]):
             f()
-        side = late
+        side = []
         late = []
         if t == 0:
-            side += [lambda: tcopy(B(HW, 12, 24), B("wall_s")),
-                     lambda: tcopy(B(HW, 0, 12), B("hold_s")),
-                     lambda: (send(nxt, B(HN, 12, 24), wall, "rw1"), tcopy(col(7), B("wt_s")))]
+            side = [lambda: tcopy(hh, B("hold_s")), lambda: ts(col(7), B("wt_s"), -1.0 / 32, A.mult)]
+            side += [lambda a=a: tcopy(B("Kw", V + a, V + a + 128), B("ki", a, a + 128)) for a in range(EARLY, V, 128)]
         if jub:
-            side += [lambda: ts(B("nw"), wall, -1.0, A.mult, 1.0, A.add),
-                     lambda: tt(B("hW"), hh, wall, A.mult),
-                     lambda: ts(B("Aw"), B("nw"), col(11), A.mult),
-                     lambda: tt(B("hW"), B("hW"), B("Aw"), A.add)]
+            side = [lambda: ts(B("nw"), wall, 2.0 * V + P, A.mult, -OFF, A.add),
+                    lambda: tt(B("hW"), hh, wall, A.mult),
+                    lambda: tt(B("nw"), B("nw"), B("eF"), A.max),
+                    lambda: ts(B("hW"), B("hW"), col(11), A.add),
+                    lambda: ts(B("EW"), B("nw"), OFF - V, A.add)]
 
         def fillers():
             if side:
                 side.pop(0)()
         fillers()
+        scan(B("sz"), B("RS2"), B("keys"), A.add, A.min)
         scan(B("sk"), B("RST"), B("keys"), A.add, A.min)
-        sv = B("sk", 15, P, 16)
-        fillers()
-        tcopy(B("KEY"), sv)
-        tt(B("fo"), sv, B("eF"), A.min)
+        tt(B("zI"), B("sz", 15, P, 16), B("eF"), A.min)
+        tcopy(B("KEY"), B("sk", 15, P, 16))
+        ts(B("zI"), B("zI"), 8191, A.bitwise_and)
         ts(B("bI"), B("KEY"), 4095, A.bitwise_and)
-        ts(B("fe"), B("fo"), OFF, A.add)
-        fillers()
-        tt(B("dk"), B("fe"), B("bI"), A.max)
+        tcopy(B("dkU"), B("zI"))
+        tcopy(B("dk"), B("zI"))
         tcopy(B("bU"), B("bI"))
-        tcopy(B("dkU"), B("dk"))
-        fillers()
         tcopy(B("dkf"), IND(B("ramp"), B("dkU")))
         fillers()
         act(B("dkF"), IND(B("ramp"), B("dkU")), F.Copy)
         act(B("Xb"), IND(XW, B("bU")), F.Copy)
         act(B("bF"), IND(B("ramp", 0, V), B("bU")), F.Copy)
-        act(B("Fo"), IND(KW, B("bU")), F.Identity, scale=col(2))
-        mm(B("CN", 0, P), B("BO"), B("zero"), True, False)
-        mm(B("CN", 0, P), B("IDF"), B("dkF"), False, False)
+        if t:
+            act(B("Fo"), IND(KW, B("bU")), F.Identity, scale=col(2))
+        mm(B("CN", 0, P), B("IDF"), B("dkF"), True, False)
         for j in range(12):
             w = P - 16 * j
             op("V", lambda: g.vector.tensor_scalar(T.eq[:, j, 0:w], T.dkf[:, 16 * j:P], T.dk[:, j:j + 1], None, A.is_equal),
                (None, [("eq", 16 * j, 16 * j + 16)], []), [B("dkf"), B("dk")])
             if j < 11:
-                mm(B("CN", 16 * j + 16, P), B("BO"), (T.eq[:, j, 16:w], [("eq", 16 * j, 16 * j + 16)], []), False, False)
-        mm(B("CN", 0, P), B("U"), DIAG, False, True)
+                mm(B("CN", 16 * j + 16, P), B("BO"), R("eq", T.eq[:, j, 16:w], 16 * j, 16 * j + 16), False, False)
+            if j == 7:
+                mm(B("CN", 0, 128), B("U"), R("eq", T.eq[:, 0:8, 0:16], 0, 128), False, False)
+        mm(B("CN", 128, P), B("U"), R("eq", T.eq[:, 8:12, 0:16], 128, P), False, True)
         mm(B("XB", 0, P), B("ID"), B("Xb"), True, False)
         mm(B("XB", 0, P), B("NID"), B("q"), False, True)
         act(B("xr"), B("XB", 0, P), F.Relu, bias=130.0)
@@ -396,36 +411,34 @@ def rank_program(g, core, T, topo):
             sums(2)
         if t >= 2:
             sums_out(3 * (t - 2))
-        while side:
-            fillers()
-        if jub:
-            tt(B("th"), B("bI"), hh, A.subtract)
+        fillers()
+        tt(B("th"), B("bI"), hh, A.subtract)
         if t == 0:
-            ts(B("Lw"), B("crow"), col(13), A.is_equal, col(7), A.mult)
+            act(B("Lw"), B("L32"), F.Identity, scale=col(7))
         scan(B("sc3"), B("CN", 0, P), B("C3"), A.max, A.add)
         if jub:
             tt(B("th"), B("th"), wall, A.mult)
+        fillers()
         tt(B("oy"), B("sc3", 15, P, 16), B("DUM"), A.min)
+        fillers()
         ts(OF, B("oy"), col(11), A.add)
         ts(B("wU"), B("oy"), col(11), A.add, float(V), A.is_lt)
-        tcopy(IND(B("Hw"), OF), B("bF"))
+        tcopy(IND(B("Hw", 0, W), OF), B("bF"))
         act(B("wb"), IND(B("ramp", 0, 16), B("wU")), F.Copy)
-        act(B("hm"), IND(HS, B(EU)), F.Copy)
+        act(B("hm"), IND(HS, B("EW" if jub else EU)), F.Copy)
         if last:
             dma("Y", ext(T.yh[:]), B("Hw", V, 2 * V, parts=(0, 128, 16)))
         ts(B("wF"), B("oy"), col(11), A.add, float(V), A.is_lt)
         mm(B("PP", 0, P), B("ID"), B("wb"), True, False)
         mm(B("PP", 0, P), B("ID"), B(PR), False, True)
         act(B("p15"), B("PP", 0, P), F.Relu, bias=15.0, scale=-1.0)
-        act(B("pw" if jub else PO), B("p15"), F.Identity, bias=274.5 if jub else 15.0, scale=-1.0)
+        if t != 1:
+            act(B("pw" if jub else PO), B("p15"), F.Identity, bias=274.5 if jub else 15.0, scale=-1.0)
+        tcopy(IND(B("Xw"), B(ofn, 0, XH)), B("xr", 0, 16 * XH))
+        tt(B("th"), B("th"), B("wF"), A.mult)
         if jub:
-            tt(B("th"), B("th"), B("wF"), A.mult)
-            if last:
-                tcopy(IND(B("Xw"), OF), B("xr"))
-                dma("Y", ext(T.yx[:]), XW)
-            tt(B("Aw"), B("th"), B("hW"), A.add)
             for j in range(16):
-                mm(B("ZC", 0, 12), L("Lw", j), B("C260", 0, 12), j == 0, False)
+                mm(B(SS, 0, 12), L("Lw", j), B("C260", 0, 12), j == 0, False)
         if t >= 2:
             yv = "yv%d" % t
             sums_out(3 * (t - 2) + 1)
@@ -437,44 +450,62 @@ def rank_program(g, core, T, topo):
         scan(B("sc"), B("hm"), B("C3"), A.max, A.add)
         el = B("sc", 15, 192, 16)
         if jub:
-            tt(B("eh"), el, B("nw"), A.mult)
-            tt(B("fin"), B("eh"), B("Aw"), A.add)
+            tt(B("Aw"), B("th"), B("hW"), A.add)
+            tt(B("fin"), el, B("Aw"), A.add)
             tcopy(B(EO), B("fin"))
         else:
+            tt(hh, B("th"), hh, A.add)
+            fillers()
             ts(B(EO), el, col(11), A.add)
         if last:
             send(home, B("rE"), B(EO), "rg")
         else:
             send(nxt, B("E%d" % (t + 1)), B(EO), "re%d" % (t + 1))
+
+        def wealth():
+            tcopy(IND(B("Xw"), B(ofn, XH, 12)), B("xr", 16 * XH, P))
+
+        def kin():
+            tt(IND(B("Kw"), OF), B("Fo"), B("ce"), A.add)
         if not jub:
             send(nxt, B("PR%d" % (t + 1)), B(PO), "rp%d" % (t + 1))
-            tt(IND(B("Kw"), OF), B("Fo"), B("ce"), A.add)
-            tt(B("th"), B("bI"), hh, A.subtract)
-            tcopy(IND(B("Xw"), OF), B("xr"))
-            tt(B("th"), B("th"), B("wF"), A.mult)
-            tt(hh, B("th"), hh, A.add)
             if t == 0:
+                while side:
+                    fillers()
+                act(B("Fo"), IND(KW, B("bU")), F.Identity, scale=col(2))
+                wealth()
+                kin()
                 send(nxt, B(HN, 0, 12), hh, "rh1")
             else:
+                kin()
+                wealth()
                 send(nxt, B(HN), B(HW), "rh%d" % (t + 1))
         else:
-            if not last:
-                tcopy(IND(B("Xw"), OF), B("xr"))
-            tt(B("ph"), IND(XW, B(EO)), B("pw"), A.add)
+            wealth()
+            if last:
+                dma("Y", ext(T.yx[:, 0:HALF]), B("Xw", 0, HALF))
+                tt(B("ph"), IND(XW, B(EO)), B("pw"), A.add)
+            else:
+                kin()
+                act(B("Xb"), IND(XW, B(EO)), F.Copy)
+                mm(B("XB", 0, P), B("NID"), B("p15"), True, False)
+                mm(B("XB", 0, P), B("ID"), B("Xb"), False, True)
+                act(B("ph"), B("XB", 0, P), F.Identity, bias=274.5)
+                act(B(PO), B("ph"), F.Identity, bias=-130.0, scale=0.5)
+                send(nxt, B("PR%d" % (t + 1)), B(PO), "rp%d" % (t + 1))
             for j in range(16):
                 rhs = B("ph", 12 * j, 12 * j + 12) if last else B("ph", j, P, 16)
-                mm(B("ZC", 0, 12), L("Lw", j), rhs, False, j == 15)
-            if not last:
-                ts(B(PO), B("ph"), -260.0, A.add, 0.5, A.mult)
-                send(nxt, B("PR%d" % (t + 1)), B(PO), "rp%d" % (t + 1))
-                tt(IND(B("Kw"), OF), B("Fo"), B("ce"), A.add)
-            ts(B("sI", 0, 12), B("ZC", 0, 12), 0.5, A.mult)
-            ts(B("sI", 12, 24), B("ZC", 0, 12), 0.5, A.mult, -float(V), A.add)
-            late = [lambda: ts(B("uI"), B("sI"), 4095, A.bitwise_and)]
+                mm(B(SS, 0, 12), L("Lw", j), rhs, False, j == 15)
+            late = [lambda: ts(B("sI", 0, 12), B(SS, 0, 12), 0.5, A.mult),
+                    lambda: ts(B("sI", 12, 24), B(SS, 0, 12), 0.5, A.mult, -float(V), A.add),
+                    lambda: ts(B("uI"), B("sI"), 4095, A.bitwise_and)]
             if last:
-                late.pop()()
+                for f in late:
+                    f()
                 tt(B("hh"), B("uI", 0, 12), B("uI", 12, 24), A.min)
                 send(home, B("rh"), B("hh"), "rf")
+                need("Y", B("hh")[1], [], False)
+                dma("Y", ext(T.yx[:, HALF:V]), B("Xw", HALF, V))
                 tcopy(IND(B("Yw"), B("of0")), B("yv2"))
                 tcopy(IND(B("Yw"), OF), B("yv3"))
                 dma("Y", ext(T.yk[:]), B("Yw", V, 2 * V, parts=(0, 128, 16)))

@@ -2,12 +2,13 @@ from concourse.mybir import dt, AluOpType, AxisListType, ActivationFunctionType
 
 V, P, NS = 2560, 192, 4
 W = 2 * V + P
+Q = 12 * 17
 BIG, LOW = 2.0 ** 21, 2.0 ** 23
 OFF = 240.0 * 65536
 RND = 1.5 * 2.0 ** 39
-NV = 4
 HALF = V // 2
-EARLY = HALF + 256
+NJ = 8
+EARLY = HALF + 512
 XH = 6
 A = AluOpType
 F = ActivationFunctionType
@@ -19,37 +20,37 @@ def _b(name, cols, d, where="sbuf"):
     SCRATCH[name] = (where, [128] + (cols if isinstance(cols, list) else [cols]), d)
 
 
-for _n, _c in (("Kw", W), ("Hw", W + 16), ("Yw", W), ("ramp", 2 * V), ("cb", 224), ("tr", 416), ("sc3", 192), ("K0", 192), ("keys", 192),
-               ("rA", 192), ("RST", 192), ("RS2", 192), ("sk", 192), ("sz", 192), ("sc", 192), ("bF", 192), ("dkF", 192), ("pw", 192),
-               ("IDF", 128), ("Fo", 192), ("ce", 192), ("hm", 192), ("DUM", 12), ("dm0", 12), ("cols", 16), ("eF", 12),
-               ("dk", 12), ("oy", 12), ("wF", 12), ("th", 12), ("hW", 12), ("Aw", 12), ("nw", 12),
-               ("fin", 12), ("hh", 12), ("outf", 192), ("WKB", 128), ("yv2", 192), ("yv3", 192), ("s2", 12), ("s3", 12)):
+for _n, _c in (("Kw", W), ("Hw", W + 16), ("Yw", W), ("ramp", 2 * V), ("cb", 224), ("tr", 432), ("K0", 208), ("K1", Q), ("keys", Q),
+               ("rA", Q), ("RST", Q), ("sk", Q), ("sz", Q), ("z0", Q), ("z1", Q), ("C3", Q), ("sc3", Q), ("C4", P), ("sc", P),
+               ("bF", P), ("pw", P), ("Fo", P), ("ce", P), ("hm", P), ("outf", P), ("yv2", P), ("yv3", P), ("WKB", 128), ("cols", 16),
+               ("cA", 12), ("cB", 12), ("c15", 12), ("dm0", 12), ("wF", 12), ("th", 12), ("hW", 12), ("nw", 12), ("hh", P // NJ),
+               ("s1", 13), ("s2", 13), ("s3", 13), ("s4", 13)):
     _b(_n, _c, "float32")
-for _n, _c in (("Xw", W), ("wk", [12, 256]), ("eq", [12, 192]), ("crow", 288), ("L32", 288), ("Lw", 288), ("BO", 128),
-               ("U", 128), ("grow", 128), ("mrow", 128), ("q", 192), ("ID", 128), ("ID2", 128),
-               ("NID", 128), ("C16", 64), ("Cm", 192), ("C260", 16), ("Xb", 192), ("xr", 192), ("p15", 192), ("wb", 192),
-               ("ph", 192), ("jlrow", 192), ("C3", 192), ("c3t", 192)):
+for _n, _c in (("Xw", W), ("wk", [12, 256]), ("eq", [12, 12, 17]), ("crow", 144), ("L32", 144), ("Lw", 144), ("BO", 128), ("U", 128),
+               ("grow", 128), ("ID", 128), ("ID1", 128), ("ID2", 128), ("NID", 128), ("two", Q), ("qrow", Q), ("c3a", Q), ("c3b", Q),
+               ("C16", 68), ("Cm", P), ("C260", P), ("q", P), ("Xb", P), ("xr", P), ("p15", P), ("wb", P), ("jlrow", P), ("c3t", P)):
     _b(_n, _c, "bfloat16")
-for _n, _c in (("tk", [12, 256]), ("L64", 288)):
+for _n, _c in (("tk", [12, 256]), ("L64", 144)):
     _b(_n, _c, "float16")
-for _n, _c in (("ki", V), ("own_s", 12), ("hold_s", 12), ("wall_s", 12), ("wt_s", 1), ("ci", 8), ("KEY", 12), ("zI", 12), ("bI", 12),
-               ("sI", 24), ("uI", 24)):
+for _n, _c in (("ki", V), ("own_s", 12), ("hold_s", 12), ("wall_s", 12), ("wl1", 12), ("wl3", 12), ("wt_s", 1), ("ci", 8), ("KEY", 12),
+               ("bI", 12), ("jI", 13), ("pI", 13), ("sI", 2 * P // NJ), ("uI", 2 * P // NJ)):
     _b(_n, _c, "int32")
-for _n, _c in (("SELk", 12), ("cbu", 192), ("bU", 12), ("dkU", 12), ("dkf", 192), ("of0", 12), ("of1", 12),
-               ("wU", 12), ("EW", 12), ("rE", 12)):
+for _n, _c in (("SELk", 14), ("cbu", P), ("bU", 12), ("dkU", 12), ("dkf", P), ("of0", 12), ("of1", 12), ("wU", 12), ("EW", 12), ("rE", 12)):
     _b(_n, _c, "uint16")
 for _t in range(NS):
     _b("E%d" % _t, 12, "uint16")
     _b("EO%d" % _t, 12, "uint16")
-    _b("PR%d" % _t, 192, "bfloat16")
-    _b("PO%d" % _t, 192, "bfloat16")
-    _b("HW%d" % _t, 24, "float32")
-_b("rh", 12, "float32", "dram")
-for _n in ("ZA", "ZB", "ZC", "PP", "CN", "XB", "Y0", "Y1"):
+    _b("PR%d" % _t, P, "bfloat16")
+    _b("PO%d" % _t, P, "bfloat16")
+    _b("HW%d" % _t, 12, "float32")
+_b("rh", P // NJ, "float32", "dram")
+for _n in ("ZA", "ZB", "ZC"):
+    _b(_n, [30, 17], "float32", "psum")
+for _n in ("PP", "CN", "XB", "Y0", "Y1"):
     _b(_n, 512, "float32", "psum")
 
 SEMAPHORES = (["qV", "qS", "qT", "qG", "ls"] + ["dm%d" % i for i in range(18)]
-              + ["r%s%d" % (a, t) for a in "eph" for t in range(1, NS)] + ["rf", "rg", "rw1"])
+              + ["r%s%d" % (a, t) for a in "eph" for t in range(1, NS)] + ["rf", "rg", "rw1", "rw3"])
 
 
 def rank_program(g, core, T, topo):
@@ -192,8 +193,10 @@ def rank_program(g, core, T, topo):
         return B("ci", i, i + 1)
 
     def L(name, j):
-        o = 15 - j if j % 2 else 144 + 16 - j
-        return B(name, o, o + 128)
+        return B(name, 15 - j, 143 - j)
+
+    def convert(a, b):
+        tcopy(B("Kw", V + a, V + b), B("ki", a, b))
 
     dma("Y", B("ki", 0, HALF), ext(T.kin[:, 0:HALF]))
     dma("Y", B("own_s"), ext(T.own[:]))
@@ -206,16 +209,18 @@ def rank_program(g, core, T, topo):
 
     RB = V // 4
     iota(ci(6), [[0, 1]], 0, 1)
-    iota(B("crow"), [[-1, 2], [1, 144]], 0, 0)
-    iota(B("mrow"), [[1, 128]], 0, 0)
-    iota(B("ramp", 0, RB), [[1, RB]], 0, 0)
-    iota(B("grow"), [[1, 8], [0, 16]], 0, 0)
+    iota(B("s1"), [[16, 13]], 0, 0)
+    iota(B("crow"), [[1, 144]], 0, 0)
+    iota(B("qrow"), [[0, 12], [1, 17]], 0, 0)
     iota(B("jlrow"), [[0, 12], [1, 16]], 0, 0)
-    iota(B("s2"), [[32, 6], [16, 2]], 0, 0)
-    iota(B("s3"), [[0, 6], [1, 2]], 0, 0)
-    iota(B("dm0"), [[16, 12]], 2 * V, 0)
+    iota(B("grow"), [[1, 8], [0, 16]], 0, 0)
+    iota(B("dm0"), [[16, 12]], 2 * V + 8192, 0)
+    iota(B("ramp", 0, RB), [[1, RB]], 0, 0)
     fill(B("cb", 0, 16), 0.0)
     fill(B("cb", 208, 224), 0.0)
+    fill(B("tr", 416, 432), 0.0)
+    fill(B("C16"), 16384.0)
+    fill(R("eq", T.eq[:, :, :, 0], 0, P), 0.0)
     ts(ci(0), ci(6), 15, A.bitwise_and)
     ts(ci(1), ci(6), 4, A.logical_shift_right)
     ts(ci(2), ci(6), 1, A.bitwise_and)
@@ -223,43 +228,59 @@ def rank_program(g, core, T, topo):
     tcopy(col(9), ci(6))
     fill(B("Cm"), -32.0)
     tcopy(B("cols", 0, 4), B("ci", 0, 4))
-    fill(B("C16"), 16384.0)
-    fill(B("C260"), -260.0)
+    fill(B("RST"), -4096.0)
+    ts(B("s1"), B("s1"), col(0), A.add, Q - 1.0, A.min)
     ts(col(13), col(1), 16.0, A.mult, 15.0, A.add)
     ts(col(8), col(0), 0.0, A.is_equal, -LOW, A.mult)
+    ts(B("jI"), B("s1"), -8.0, A.add, 1.0 / 17, A.mult)
     ts(col(6), col(2), -1.0, A.mult, 1.0, A.add)
-    ts(col(10), col(3), -416.0, A.mult, 208.0, A.add)
-    ts(col(12), col(3), 208.0, A.mult, col(0), A.add)
-    ts(col(15), col(0), 1.0, A.add, 1.0 / 8192, A.mult)
+    ts(col(14), col(0), -1.0, A.mult, -1.0, A.add)
     ts(col(11), col(8), -1.0, A.mult, -BIG, A.add)
+    ts(B("pI"), B("jI"), col(3), A.add)
+    ts(B("s3"), B("jI"), 17.0, A.mult, 16.0, A.add)
+    tt(B("s2"), B("s1"), B("jI"), A.subtract)
+    ts(B("s4"), B("jI"), 416.0, A.add)
+    ts(B("pI"), B("pI"), 1, A.bitwise_and)
+    tt(B("s3"), B("s3"), B("s1"), A.is_equal)
     ts(B("L64"), B("crow"), col(13), A.is_equal, 64.0, A.mult)
+    ts(B("s1"), B("pI"), 208.0, A.mult)
+    tt(B("s4"), B("s4"), B("s3"), A.mult)
     ts(B("L32"), B("crow"), col(13), A.is_equal, -32.0, A.mult)
-    ts(B("ID"), B("mrow"), col(9), A.is_equal)
-    fill(B("RST"), -4096.0)
+    tt(B("s2"), B("s2"), B("s1"), A.add)
+    ts(B("ID"), B("crow", 0, 128), col(9), A.is_equal)
+    fill(B("RST", 0, Q, 17), 2.0 ** 26)
+    tt(B("s2"), B("s2"), B("s4"), A.max)
+    act(B("c3a"), B("qrow"), F.Abs, bias=col(14))
+    act(B("c3b"), B("qrow"), F.Abs, scale=-1.0, bias=col(0))
+    act(B("two"), B("qrow"), F.Relu, scale=-2.0, bias=2.0)
+    act(B("c3a"), B("c3a"), F.Relu, scale=-1.0, bias=1.0)
+    act(B("c3b"), B("c3b"), F.Relu, scale=-1.0, bias=1.0)
     act(B("ID2"), B("ID"), F.Identity, scale=2048.0)
     act(B("NID"), B("ID"), F.Identity, scale=-1.0)
-    act(B("IDF"), B("ID"), F.Copy)
-    fill(B("RST", 0, P, 16), 2.0 ** 26)
-    act(B("RS2"), B("RST"), F.Identity, scale=2.0)
-    for a in (RB, 2 * RB):
-        act(B("ramp", a, 2 * a), B("ramp", 0, a), F.Identity, bias=float(a))
-    tcopy(B("Kw", V, V + HALF), B("ki", 0, HALF))
-    tcopy(B("E0"), B("own_s"))
-    ts(B("BO"), B("grow"), col(1), A.is_equal, 8192.0, A.mult)
-    act(B("WKB"), B("BO"), F.Identity, scale=col(15))
+    act(B("ID1"), B("ID"), F.Identity, scale=1024.0)
+    act(B("C260"), B("Cm"), F.Identity, scale=8.125)
     ts(B("c3t"), B("jlrow"), col(0), A.is_lt, -LOW, A.mult)
     ts(B("PP", 0, P), B("jlrow"), col(0), A.is_equal, BIG, A.mult)
-    ts(B("s3"), B("s3"), col(10), A.mult, col(12), A.add)
-    tt(B("C3"), B("PP", 0, P), B("c3t"), A.add)
-    tt(B("s2"), B("s2"), B("s3"), A.add)
-    ts(B("C3", 15, P, 16), B("C3", 15, P, 16), col(8), A.add)
-    ts(B("DUM"), B("dm0"), col(0), A.add, col(11), A.subtract)
-    tcopy(B("SELk"), B("s2"))
+    tcopy(B("SELk", 0, 13), B("s2"))
+    ts(B("BO"), B("grow"), col(1), A.is_equal, -1.0, A.mult)
+    act(B("WKB"), B("BO"), F.Identity, scale=col(14))
+    tt(B("C4"), B("PP", 0, P), B("c3t"), A.add)
+    ts(B("dm0"), B("dm0"), col(0), A.add, -1.0 / 8192, A.mult)
+    mm(B("CN", 0, Q), B("ID"), B("c3a"), True, False)
+    mm(B("CN", 0, Q), B("NID"), B("c3b"), False, True)
+    act(B("C3"), B("CN", 0, Q), F.Copy)
+    act(B("cB"), B("C3", 16, Q, 17), F.Copy)
+    act(B("c15"), B("C4", 15, P, 16), F.Identity, bias=col(8))
+    act(B("C4", 15, P, 16), B("c15"), F.Copy)
+    tcopy(B("E0"), B("own_s"))
+    convert(0, HALF)
+    tt(B("cA"), B("C3", 0, Q, 17), B("dm0"), A.add)
+    act(B("ramp", RB, 2 * RB), B("ramp", 0, RB), F.Identity, bias=float(RB))
+    need("Y", B("wt_s")[1], [], False)
+    dma("Y", B("Hw", V, V + HALF), B("ramp", 0, HALF))
     op("G", lambda: g.affine_select(T.U[:], T.BO[:], [[1, 128]], A.is_gt, 0.0, 0, -1), B("U"), [B("BO")])
     iota(B("ramp", V, 2 * V), [[1, V]], V, 0)
     iota(B("Hw", 2 * V, W + 16), [[0, P + 16]], 0, 0)
-    need("Y", B("wt_s")[1], [], False)
-    dma("Y", B("Hw", V, 2 * V), B("ramp", 0, V))
 
     nxt = cores[(rank + 1) % n]
     prv = cores[(rank - 1) % n]
@@ -267,8 +288,7 @@ def rank_program(g, core, T, topo):
     away = cores[(rank + NS - 1) % n]
     XW, KW, HS = B("Xw", 0, V), B("Kw", V, 2 * V), B("Hw", V, W + 16)
 
-    SS = "CN"
-    YB = ("Y0", "Y1", "ZA", "Y0", "Y1")
+    YB = ("Y0", "Y1", "Y0", "Y1", "Y0")
 
     def sums(i):
         mm(B(YB[i]), B("WKB"), B("Kw", V + 512 * i, V + 512 * i + 512), True, True)
@@ -280,15 +300,16 @@ def rank_program(g, core, T, topo):
         return R(buf, T[buf][:, 4 * c:4 * c + 4, 16 * j:16 * j + 16], 16 * c, 16 * c + 16)
 
     def part(name, c):
-        return B(name, 64 * c, 64 * c + 64)
+        return B(name, 68 * c, 68 * c + 68)
 
-    def Z(c, i):
-        return part(("ZA", "ZB", "ZC")[c], i)
+    def Z(c, i, w=17):
+        name = ("ZA", "ZB", "ZC")[c]
+        return R(name, T[name][:, 4 * i:4 * i + 4, 0:w], 4 * i, 4 * i + 4)
 
     def linear(c):
         mm(Z(c, 0), B("ID"), B("C16"), True, False)
         for j in range(16):
-            mm(Z(c, 0), L("L32", j), moving(c, "wk", j), False, False)
+            mm(Z(c, 0, 16), L("L32", j), moving(c, "wk", j), False, False)
 
     def greater(c):
         for k in range(16):
@@ -297,13 +318,18 @@ def rank_program(g, core, T, topo):
 
     def maxima(c):
         for j in range(16):
-            mm(Z(c, 0), L("L64", j), moving(c, "tk", j), False, j == 15)
+            mm(Z(c, 0, 16), L("L64", j), moving(c, "tk", j), False, j == 15)
 
     def decode(c):
         return [lambda: ts(part("rA", c), Z(c, 0), RND, A.add, RND, A.subtract),
                 lambda: tt(Z(c, 1), Z(c, 0), part("rA", c), A.is_lt),
+                lambda: tt(part("z1", c), Z(c, 1), part("K0", c), A.add),
+                lambda: tt(part("z0", c), Z(c, 0), part("rA", c), A.is_ge),
                 lambda: tt(Z(c, 2), Z(c, 1), part("rA", c), A.mult),
-                lambda: tt(part("keys", c), Z(c, 2), part("K0", c), A.add)]
+                lambda: tt(part("keys", c), Z(c, 2), part("K1", c), A.add)]
+
+    def back(name, a, b):
+        return R(name, T[name][:, b - 1:a - 1:-1] if a else T[name][:, b - 1::-1], a, b)
 
     late = []
     for t in range(NS):
@@ -312,201 +338,216 @@ def rank_program(g, core, T, topo):
         ofn = "of%d" % (t % 2)
         EU, PR, HW, OF = "E%d" % t, "PR%d" % t, "HW%d" % t, B(ofn)
         EO, PO, HN = "EO%d" % t, "PO%d" % t, "HW%d" % (t + 1)
-        hh, wall = B(HW, 0, 12), B(HW, 12, 24)
+        hh, wall = B(HW), B("wl%d" % (t | 1))
+        SS = "CN" if last else "XB"
+        nj = NJ if last else 16
+        ws = P // nj
+        half = 0.5 if t == 2 else 0.0
         if t:
             arrive(EU, 0, 12, prv, "re%d" % t)
             arrive(PR, 0, P, prv, "rp%d" % t)
-            arrive(HW, 0, 12 if t == 1 else 24, prv, "rh%d" % t)
-            if t == 1:
-                arrive(HW, 12, 24, prv, "rw1")
+            arrive(HW, 0, 12, prv, "rh%d" % t)
+            if jub:
+                arrive("wl%d" % t, 0, 12, cores[(rank - t) % n], "rw%d" % t)
         kw = KW if t else B("ki")
         tcopy(B("cbu", 0, 64), IND(kw, B(EU, 0, 4)))
         tcopy(B("cbu", 64, P), IND(kw, B(EU, 4, 12)))
-        ts(B("eF"), B(EU), V - OFF, A.add)
         blocks = [(R("wk", T.wk[:, a, :], 4 * a, 4 * a + 4), IND(XW, B("cbu", 16 * a, 16 * a + 16))) for a in range(12)]
-        for o, i in blocks[:8 - NV] + blocks[8:]:
+        for o, i in blocks[0:2] + blocks[4:6] + blocks[8:]:
             act(o, i, F.Identity, scale=2048.0)
         if t:
             act(B("cb", 16, 208), IND(KW, B(EU)), F.Copy)
         else:
+            act(B("ramp", HALF, V), B("ramp", 0, HALF), F.Identity, bias=float(HALF))
+            dma("Y", B("Hw", V + HALF, 2 * V), B("ramp", HALF, V))
             tcopy(B("cb", 16, 208), B("cbu"))
-            tcopy(B("Kw", V + HALF, V + EARLY), B("ki", HALF, EARLY))
-            late = [lambda: tcopy(wall, B("wall_s")), lambda: send(nxt, B(HN, 12, 24), wall, "rw1")]
-        for o, i in blocks[8 - NV:8]:
+            convert(HALF, EARLY)
+            send(nxt, B("wl1"), B("wall_s"), "rw1")
+            send(away, B("wl3"), B("wall_s"), "rw3")
+        for o, i in blocks[2:4] + blocks[6:8]:
             ts(o, i, 2048.0, A.mult)
+        act(B("q"), B(PR), F.Identity, bias=129.625 - 65 * half, scale=0.25 - half / 4)
         mm(B("PP", 0, P), B("ID"), B("Cm"), True, False)
-        mm(B("PP", 0, P), B("ID2"), B(PR), False, True)
+        if half:
+            mm(B("PP", 0, P), B("ID1"), B("C260"), False, False)
+        mm(B("PP", 0, P), B("ID1" if half else "ID2"), B(PR), False, True)
         linear(0)
         linear(1)
-        for f in late[:2]:
-            f()
         greater(0)
-        for f in late[2:3]:
-            f()
         maxima(0)
         greater(1)
-        for f in late[3:]:
-            f()
         linear(2)
         maxima(1)
         greater(2)
         maxima(2)
+        if last:
+            sums_out(2)
+            sums_out(3)
         if t >= 2:
-            sums(3 * (t - 2))
-            sums(3 * (t - 2) + 1)
-        act(B("q"), B(PR), F.Identity, bias=129.625, scale=0.25)
-        act(B("ce"), B("cb", 16, 208), F.Identity, scale=col(6))
+            sums(4 * (t - 2))
         op("V", lambda: g.vector.transpose(T.tr[:, 0:192], T.cb[:, 16:208]), B("tr", 0, 192), [B("cb", 16, 208)])
         op("V", lambda: g.vector.transpose(T.tr[:, 192:416], T.cb[:, 0:224]), B("tr", 192, 416), [B("cb")])
-        act(B("K0"), IND(B("tr"), B("SELk")), F.Identity, bias=-OFF)
+        eF = B("tr", 416, 428)
+        ts(eF, B(EU), float(V), A.add)
+        act(B("K0"), IND(B("tr"), B("SELk", 0, 13)), F.Identity, scale=1.0 / 8192)
+        act(B("K1"), B("K0", 0, Q), F.Identity, scale=8192.0, bias=-OFF)
+        act(B("ce"), B("cb", 16, 208), F.Identity, scale=col(6))
         d0, d1, d2 = decode(0), decode(1), decode(2)
-        for f in (d0[0], d1[0], d0[1], d1[1], d2[0], d0[2], d1[2], d2[1], d0[3], d2[2], d1[3], d2[3]):
+        for f in (d0[0], d1[0], d0[1], d1[1], d2[0], d0[3], d1[3], d2[1], d2[3], d0[2], d1[2], d2[2], d0[4]):
             f()
-        side = []
+        side = late
         late = []
         if t == 0:
-            side = [lambda: tcopy(hh, B("hold_s")), lambda: ts(col(7), B("wt_s"), -1.0 / 32, A.mult)]
-            side += [lambda a=a: tcopy(B("Kw", V + a, V + a + 128), B("ki", a, a + 128)) for a in range(EARLY, V, 128)]
+            side = [lambda a=a: convert(a, a + 128) for a in range(EARLY, V, 128)]
         if jub:
-            side = [lambda: ts(B("nw"), wall, 2.0 * V + P, A.mult, -OFF, A.add),
-                    lambda: tt(B("hW"), hh, wall, A.mult),
-                    lambda: tt(B("nw"), B("nw"), B("eF"), A.max),
-                    lambda: ts(B("hW"), B("hW"), col(11), A.add),
-                    lambda: ts(B("EW"), B("nw"), OFF - V, A.add)]
+            side = [lambda: (ts(B("nw"), wall, 2.0 * V + P, A.mult), tt(B("th"), B("bI"), hh, A.subtract)),
+                    lambda: (tt(B("nw"), B("nw"), eF, A.max), tt(B("th"), B("th"), wall, A.mult), tt(B("hW"), hh, wall, A.mult)),
+                    lambda: ts(B("EW"), B("nw"), -float(V), A.add),
+                    lambda: (tt(B("th"), B("th"), B("wF"), A.mult), tt(B("hW"), B("hW"), B("c15"), A.add))]
 
         def fillers():
             if side:
                 side.pop(0)()
-        fillers()
-        scan(B("sz"), B("RS2"), B("keys"), A.add, A.min)
-        scan(B("sk"), B("RST"), B("keys"), A.add, A.min)
-        tt(B("zI"), B("sz", 15, P, 16), B("eF"), A.min)
-        tcopy(B("KEY"), B("sk", 15, P, 16))
-        ts(B("zI"), B("zI"), 8191, A.bitwise_and)
-        ts(B("bI"), B("KEY"), 4095, A.bitwise_and)
-        tcopy(B("dkU"), B("zI"))
-        tcopy(B("dk"), B("zI"))
-        tcopy(B("bU"), B("bI"))
+        scan(back("sz", 0, 136), back("z0", 0, 136), back("z1", 0, 136), A.add, A.min)
+        scan(back("sz", 136, Q), back("z0", 136, Q), back("z1", 136, Q), A.add, A.min)
+        d1[4]()
+        d2[4]()
+        d0[5]()
+        zf = B("sz", 0, Q, 17)
+        ts(B("dkU"), zf, 8192.0, A.mult)
+        d1[5]()
+        d2[5]()
+        tt(B("C3", 0, Q, 17), B("cA"), zf, A.add)
         tcopy(B("dkf"), IND(B("ramp"), B("dkU")))
-        fillers()
-        act(B("dkF"), IND(B("ramp"), B("dkU")), F.Copy)
-        act(B("Xb"), IND(XW, B("bU")), F.Copy)
-        act(B("bF"), IND(B("ramp", 0, V), B("bU")), F.Copy)
-        if t:
-            act(B("Fo"), IND(KW, B("bU")), F.Identity, scale=col(2))
-        mm(B("CN", 0, P), B("IDF"), B("dkF"), True, False)
+        scan(B("sk"), B("RST"), B("keys"), A.add, A.min)
+        mm(B("CN", 0, Q), B("ID"), B("two"), True, False)
         for j in range(12):
-            w = P - 16 * j
-            op("V", lambda: g.vector.tensor_scalar(T.eq[:, j, 0:w], T.dkf[:, 16 * j:P], T.dk[:, j:j + 1], None, A.is_equal),
-               (None, [("eq", 16 * j, 16 * j + 16)], []), [B("dkf"), B("dk")])
-            if j < 11:
-                mm(B("CN", 16 * j + 16, P), B("BO"), R("eq", T.eq[:, j, 16:w], 16 * j, 16 * j + 16), False, False)
+            op("V", lambda: g.vector.tensor_scalar(T.eq[:, j, 0:12 - j, 1:17], T.dkf[:, 16 * j:P], 1.0 / 8192, T.sz[:, 17 * j:17 * j + 1],
+                                                   A.mult, A.is_equal), R("eq", None, 16 * j, 16 * j + 16), [B("dkf"), zf])
             if j == 7:
-                mm(B("CN", 0, 128), B("U"), R("eq", T.eq[:, 0:8, 0:16], 0, 128), False, False)
-        mm(B("CN", 128, P), B("U"), R("eq", T.eq[:, 8:12, 0:16], 128, P), False, True)
+                tcopy(B("KEY"), B("sk", 15, Q, 17))
+            if j < 11:
+                mm(B("CN", 17 * j + 17, Q), B("BO"), R("eq", T.eq[:, j, 1:12 - j, :], 16 * j, 16 * j + 16), False, False)
+            if j == 7:
+                mm(B("CN", 0, 136), B("U"), R("eq", T.eq[:, 0:8, 0, :], 0, 128), False, False)
+        mm(B("CN", 136, Q), B("U"), R("eq", T.eq[:, 8:12, 0, :], 128, P), False, True)
+        ts(B("bI"), B("KEY"), 4095, A.bitwise_and)
+        tt(B("C3", 16, Q, 17), B("cB"), zf, A.subtract)
+        if not jub:
+            fillers()
+        tcopy(B("bU"), B("bI"))
+        act(B("bF"), IND(B("ramp", 0, V), B("bU")), F.Copy)
+        act(B("Xb"), IND(XW, B("bU")), F.Copy)
+        fillers()
+        scan(B("sc3"), B("CN", 0, Q), B("C3"), A.max, A.add)
+        h0 = hh if t else B("hold_s")
+        if t == 0:
+            tt(B("th"), B("bI"), h0, A.subtract)
+        fillers()
+        oy = B("sc3", 16, Q, 17)
+        ts(OF, oy, -1.0, A.add, -8192.0, A.mult)
+        ts(B("wU"), oy, 1.0 - V / 8192, A.is_gt)
+        ts(B("wF"), oy, 1.0 - V / 8192, A.is_gt)
+        fillers()
         mm(B("XB", 0, P), B("ID"), B("Xb"), True, False)
         mm(B("XB", 0, P), B("NID"), B("q"), False, True)
+        act(B("wb"), IND(B("ramp", 0, 16), B("wU")), F.Identity, scale=1.0 + 2 * half)
         act(B("xr"), B("XB", 0, P), F.Relu, bias=130.0)
         if t == 2:
-            sums(2)
-        if t >= 2:
-            sums_out(3 * (t - 2))
-        fillers()
-        tt(B("th"), B("bI"), hh, A.subtract)
-        if t == 0:
-            act(B("Lw"), B("L32"), F.Identity, scale=col(7))
-        scan(B("sc3"), B("CN", 0, P), B("C3"), A.max, A.add)
-        if jub:
-            tt(B("th"), B("th"), wall, A.mult)
-        fillers()
-        tt(B("oy"), B("sc3", 15, P, 16), B("DUM"), A.min)
-        fillers()
-        ts(OF, B("oy"), col(11), A.add)
-        ts(B("wU"), B("oy"), col(11), A.add, float(V), A.is_lt)
+            sums(1)
         tcopy(IND(B("Hw", 0, W), OF), B("bF"))
-        act(B("wb"), IND(B("ramp", 0, 16), B("wU")), F.Copy)
+        while side:
+            fillers()
         act(B("hm"), IND(HS, B("EW" if jub else EU)), F.Copy)
+        act(B("Fo"), IND(KW, B("bU")), F.Identity, scale=col(2))
         if last:
             dma("Y", ext(T.yh[:]), B("Hw", V, 2 * V, parts=(0, 128, 16)))
-        ts(B("wF"), B("oy"), col(11), A.add, float(V), A.is_lt)
         mm(B("PP", 0, P), B("ID"), B("wb"), True, False)
         mm(B("PP", 0, P), B("ID"), B(PR), False, True)
-        act(B("p15"), B("PP", 0, P), F.Relu, bias=15.0, scale=-1.0)
+        act(B("p15"), B("PP", 0, P), F.Relu, bias=15.0 + 260 * half, scale=half - 1.0)
         if t != 1:
             act(B("pw" if jub else PO), B("p15"), F.Identity, bias=274.5 if jub else 15.0, scale=-1.0)
-        tcopy(IND(B("Xw"), B(ofn, 0, XH)), B("xr", 0, 16 * XH))
-        tt(B("th"), B("th"), B("wF"), A.mult)
+        if t >= 2:
+            sums_out(4 * (t - 2))
         if jub:
-            for j in range(16):
-                mm(B(SS, 0, 12), L("Lw", j), B("C260", 0, 12), j == 0, False)
+            tt(B("C4", 15, P, 16), B("th"), B("hW"), A.add)
+        tcopy(IND(B("Xw"), B(ofn, 0, XH)), B("xr", 0, 16 * XH))
+        if t == 2:
+            tt(B("th"), B("bI"), h0, A.subtract)
+        elif t == 0:
+            tt(B("th"), B("th"), B("wF"), A.mult)
+        if last:
+            for j in range(nj):
+                mm(B(SS, 0, ws), L("Lw", 16 // nj * j), B("C260", 0, ws), j == 0, False)
         if t >= 2:
             yv = "yv%d" % t
-            sums_out(3 * (t - 2) + 1)
             mm(B("XB", 0, P), B("WKB"), B("Fo"), True, False)
             mm(B("XB", 0, P), B("WKB"), B("ce"), False, True)
             act(B(yv), B("XB", 0, P), F.Copy)
         if t == 2:
-            sums_out(2)
-        scan(B("sc"), B("hm"), B("C3"), A.max, A.add)
-        el = B("sc", 15, 192, 16)
-        if jub:
-            tt(B("Aw"), B("th"), B("hW"), A.add)
-            tt(B("fin"), el, B("Aw"), A.add)
-            tcopy(B(EO), B("fin"))
-        else:
-            tt(hh, B("th"), hh, A.add)
-            fillers()
-            ts(B(EO), el, col(11), A.add)
-        if last:
-            send(home, B("rE"), B(EO), "rg")
-        else:
-            send(nxt, B("E%d" % (t + 1)), B(EO), "re%d" % (t + 1))
+            sums_out(1)
+        scan(B("sc"), B("hm"), B("C4"), A.max, A.add)
+        el = B("sc", 15, P, 16)
 
         def wealth():
             tcopy(IND(B("Xw"), B(ofn, XH, 12)), B("xr", 16 * XH, P))
 
         def kin():
             tt(IND(B("Kw"), OF), B("Fo"), B("ce"), A.add)
+        if last:
+            wealth()
+        elif t == 2:
+            tt(B("th"), B("th"), B("wF"), A.mult)
+        elif t == 0:
+            tt(hh, B("th"), h0, A.add)
+        ts(B(EO), el, col(11), A.add)
+        if t == 1:
+            act(B("C4", 15, P, 16), B("c15"), F.Copy)
+        if last:
+            send(home, B("rE"), B(EO), "rg")
+        else:
+            send(nxt, B("E%d" % (t + 1)), B(EO), "re%d" % (t + 1))
         if not jub:
             send(nxt, B("PR%d" % (t + 1)), B(PO), "rp%d" % (t + 1))
-            if t == 0:
-                while side:
-                    fillers()
-                act(B("Fo"), IND(KW, B("bU")), F.Identity, scale=col(2))
-                wealth()
-                kin()
-                send(nxt, B(HN, 0, 12), hh, "rh1")
-            else:
-                kin()
-                wealth()
-                send(nxt, B(HN), B(HW), "rh%d" % (t + 1))
-        else:
+            kin()
+            if t == 2:
+                tt(hh, B("th"), h0, A.add)
+                sums(2)
+                sums(3)
             wealth()
+            send(nxt, B(HN), hh, "rh%d" % (t + 1))
+            if t == 0:
+                ts(col(7), B("wt_s"), -1.0 / 32, A.mult)
+                act(B("Lw"), B("L32"), F.Identity, scale=col(7))
+        else:
             if last:
                 dma("Y", ext(T.yx[:, 0:HALF]), B("Xw", 0, HALF))
-                tt(B("ph"), IND(XW, B(EO)), B("pw"), A.add)
+                tt(B(PO), IND(XW, B(EO)), B("pw"), A.add)
+                tcopy(IND(B("Yw"), B("of0", 0, 8)), B("yv2", 0, 128))
             else:
+                wealth()
                 kin()
                 act(B("Xb"), IND(XW, B(EO)), F.Copy)
                 mm(B("XB", 0, P), B("NID"), B("p15"), True, False)
                 mm(B("XB", 0, P), B("ID"), B("Xb"), False, True)
-                act(B("ph"), B("XB", 0, P), F.Identity, bias=274.5)
-                act(B(PO), B("ph"), F.Identity, bias=-130.0, scale=0.5)
+                act(B(PO), B("XB", 0, P), F.Identity, bias=274.5)
                 send(nxt, B("PR%d" % (t + 1)), B(PO), "rp%d" % (t + 1))
-            for j in range(16):
-                rhs = B("ph", 12 * j, 12 * j + 12) if last else B("ph", j, P, 16)
-                mm(B(SS, 0, 12), L("Lw", j), rhs, False, j == 15)
-            late = [lambda: ts(B("sI", 0, 12), B(SS, 0, 12), 0.5, A.mult),
-                    lambda: ts(B("sI", 12, 24), B(SS, 0, 12), 0.5, A.mult, -float(V), A.add),
-                    lambda: ts(B("uI"), B("sI"), 4095, A.bitwise_and)]
+                for j in range(16):
+                    mm(B(SS, 0, 12), L("Lw", j), B("C260", 0, 12), j == 0, False)
+            for j in range(nj):
+                rhs = B(PO, ws * j, ws * j + ws) if last else B(PO, j, P, 16)
+                mm(B(SS, 0, ws), L("Lw", 16 // nj * j), rhs, False, j == nj - 1)
+            late = [lambda SS=SS, ws=ws: ts(B("sI", 0, ws), B(SS, 0, ws), 0.5, A.mult),
+                    lambda SS=SS, ws=ws: ts(B("sI", ws, 2 * ws), B(SS, 0, ws), 0.5, A.mult, -float(V), A.add),
+                    lambda ws=ws: ts(B("uI", 0, 2 * ws), B("sI", 0, 2 * ws), 4095, A.bitwise_and)]
             if last:
                 for f in late:
                     f()
-                tt(B("hh"), B("uI", 0, 12), B("uI", 12, 24), A.min)
+                tt(B("hh"), B("uI", 0, ws), B("uI", ws, 2 * ws), A.min)
                 send(home, B("rh"), B("hh"), "rf")
                 need("Y", B("hh")[1], [], False)
                 dma("Y", ext(T.yx[:, HALF:V]), B("Xw", HALF, V))
-                tcopy(IND(B("Yw"), B("of0")), B("yv2"))
+                tcopy(IND(B("Yw"), B("of0", 8, 12)), B("yv2", 128, P))
                 tcopy(IND(B("Yw"), OF), B("yv3"))
                 dma("Y", ext(T.yk[:]), B("Yw", V, 2 * V, parts=(0, 128, 16)))
             else:
@@ -514,11 +555,10 @@ def rank_program(g, core, T, topo):
     arrive("rE", 0, 12, away, "rg")
     act(B("outf"), IND(B("ramp", 0, V), B("rE")), F.Copy)
     dma("S", ext(T.yo[:]), B("outf", 0, P, parts=(0, 128, 16)))
-    arrive("rh", 0, 12, away, "rf")
-    dma("Y", ext(T.yt[:]), B("rh"))
+    arrive("rh", 0, P // NJ, away, "rf")
+    dma("Y", ext(T.yt[:]), B("rh", parts=(0, 128, 16 // NJ)))
+    for q in "GTVS":
+        g.wait_ge(T.sem["q" + q], cnt[q])
     g.wait_ge(T.sem["ls"], sent[0])
     for i in range(ndma[0]):
         g.wait_ge(T.sem["dm%d" % i], 16)
-    for q in "VST":
-        g.wait_ge(T.sem["q" + q], cnt[q])
-    g.wait_ge(T.sem["qG"], cnt["G"])

from concourse.mybir import dt, AluOpType, AxisListType, ActivationFunctionType

V, P, NS = 2560, 192, 4
W = 2 * V + P
Q = 12 * 17
BIG, LOW = 2.0 ** 21, 2.0 ** 23
OFF = 240.0 * 65536
RND = 1.5 * 2.0 ** 39
HALF = V // 2
NJ = 8
EARLY = HALF + 512
XH = 6
A = AluOpType
F = ActivationFunctionType

SCRATCH = {}


def _b(name, cols, d, where="sbuf"):
    SCRATCH[name] = (where, [128] + (cols if isinstance(cols, list) else [cols]), d)


for _n, _c in (("Kw", W), ("Hw", W + 16), ("Yw", W), ("ramp", 2 * V), ("cb", 224), ("tr", 432), ("K0", 208), ("K1", Q), ("keys", Q),
               ("rA", Q), ("RST", Q), ("sk", Q), ("sz", Q), ("z0", Q), ("z1", Q), ("C3", Q), ("sc3", Q), ("C4", P), ("sc", P),
               ("bF", P), ("pw", P), ("Fo", P), ("ce", P), ("hm", P), ("outf", P), ("yv2", P), ("yv3", P), ("WKB", 128), ("cols", 16),
               ("cA", 12), ("cB", 12), ("c15", 12), ("dm0", 12), ("wF", 12), ("th", 12), ("hW", 12), ("nw", 12), ("hh", P // NJ),
               ("s1", 13), ("s2", 13), ("s3", 13), ("s4", 13)):
    _b(_n, _c, "float32")
for _n, _c in (("Xw", W), ("wk", [12, 256]), ("eq", [12, 12, 17]), ("crow", 144), ("L32", 144), ("Lw", 144), ("BO", 128), ("U", 128),
               ("grow", 128), ("ID", 128), ("ID1", 128), ("ID2", 128), ("NID", 128), ("two", Q), ("qrow", Q), ("c3a", Q), ("c3b", Q),
               ("C16", 68), ("Cm", P), ("C260", P), ("q", P), ("Xb", P), ("xr", P), ("p15", P), ("wb", P), ("jlrow", P), ("c3t", P)):
    _b(_n, _c, "bfloat16")
for _n, _c in (("tk", [12, 256]), ("L64", 144)):
    _b(_n, _c, "float16")
for _n, _c in (("ki", V), ("own_s", 12), ("hold_s", 12), ("wall_s", 12), ("wl1", 12), ("wl3", 12), ("wt_s", 1), ("ci", 8), ("KEY", 12),
               ("bI", 12), ("jI", 13), ("pI", 13), ("sI", 2 * P // NJ), ("uI", 2 * P // NJ)):
    _b(_n, _c, "int32")
for _n, _c in (("SELk", 14), ("cbu", P), ("bU", 12), ("dkU", 12), ("dkf", P), ("of0", 12), ("of1", 12), ("wU", 12), ("EW", 12), ("rE", 12)):
    _b(_n, _c, "uint16")
for _t in range(NS):
    _b("E%d" % _t, 12, "uint16")
    _b("EO%d" % _t, 12, "uint16")
    _b("PR%d" % _t, P, "bfloat16")
    _b("PO%d" % _t, P, "bfloat16")
    _b("HW%d" % _t, 12, "float32")
_b("rh", P // NJ, "float32", "dram")
for _n in ("ZA", "ZB", "ZC"):
    _b(_n, [30, 17], "float32", "psum")
for _n in ("PP", "CN", "XB", "Y0", "Y1"):
    _b(_n, 512, "float32", "psum")

SEMAPHORES = (["qV", "qS", "qT", "qG", "ls"] + ["dm%d" % i for i in range(18)]
              + ["r%s%d" % (a, t) for a in "eph" for t in range(1, NS)] + ["rf", "rg", "rw1", "rw3"])


def rank_program(g, core, T, topo):
    rank = T.rank_of(core)
    if rank is None:
        return
    cores = T.cores
    n = len(cores)
    eng = {"V": g.vector, "S": g.scalar, "T": g.tensor, "G": g, "Y": g.sync}
    cnt = {"V": 0, "S": 0, "T": 0, "G": 0}
    log = {}
    known = {q: {} for q in "VSTGY"}
    clock = {}
    ndma = [0]
    psum = ("ZA", "ZB", "ZC", "PP", "CN", "XB", "Y0", "Y1")

    def B(name, lo=0, hi=None, step=1, parts=None):
        t = T[name]
        if hi is None:
            hi = SCRATCH[name][1][1]
        if parts is None:
            ap = t[:, lo:hi] if step == 1 else t[:, lo:hi:step]
        else:
            ap = t[parts[0]:parts[1]:parts[2], lo:hi]
        return (ap, [(name, lo, hi)], [])

    def R(name, ap, lo, hi):
        return (ap, [(name, lo, hi)], [])

    def IND(win, off):
        return (win[0].indirect(off[0]), win[1], off[1])

    def ext(ap):
        return (ap, [], [])

    def need(q, reads, writes, acc):
        want = {}
        for regs, wr in ((reads, False), (writes, True)):
            for nm, lo, hi in regs:
                for e in log.get(nm, []):
                    if (e[0] < hi and lo < e[1] and (wr or e[3])) or (nm in psum and e[4] != q):
                        if e[4] == q and acc:
                            continue
                        s, v = e[2]
                        if want.get(s, 0) < v:
                            want[s] = v
        for s in sorted(want):
            v = want[s]
            if known[q].get(s, 0) >= v:
                continue
            eng[q].wait_ge(T.sem[s], v)
            for k, w in clock.get((s, v), {}).items():
                if known[q].get(k, 0) < w:
                    known[q][k] = w
            known[q][s] = max(known[q].get(s, 0), v)

    def note(q, tok, reads, writes):
        clock[tok] = dict(known[q])
        for regs, wr in ((reads, False), (writes, True)):
            for nm, lo, hi in regs:
                lst = log.get(nm, [])
                if wr:
                    lst = [e for e in lst if not (lo <= e[0] and e[1] <= hi)]
                else:
                    lst = [e for e in lst if not (e[4] == q and not e[3] and lo <= e[0] and e[1] <= hi)]
                lst.append([lo, hi, tok, wr, q])
                log[nm] = lst

    def op(q, fn, out, ins, acc=False, done=True):
        reads = list(out[2])
        for i in ins:
            reads += i[1] + i[2]
        need(q, reads, out[1], acc)
        inst = fn()
        s = "q" + q
        if done:
            cnt[q] += 1
            inst.then_inc(T.sem[s], 1)
            note(q, (s, cnt[q]), reads, out[1])
        else:
            note(q, (s, cnt[q] + 1), reads, out[1])

    def dma(q, out, in_):
        need(q, in_[1], out[1], False)
        s = "dm%d" % ndma[0]
        ndma[0] += 1
        eng[q].dma_start(out[0], in_[0]).then_inc(T.sem[s], 16)
        known[s] = dict(known[q])
        note(s, (s, 16), in_[1], out[1])

    sent = [0]

    def send(dst, out, in_, sem):
        need("G", in_[1], [], False)
        rid, pid, _ = topo.addr(dst)
        g.remote_dma(out[0], in_[0], T.sem[sem], T.sem["ls"], pid, rid, topo.mask(core, dst))
        sent[0] += len(topo.engines(core, dst))

    def arrive(name, lo, hi, src, sem):
        known[sem] = {}
        note(sem, (sem, len(topo.engines(src, core))), [], [(name, lo, hi)])

    def val(x):
        return x[0] if isinstance(x, tuple) else x

    def opnds(*xs):
        return [x for x in xs if isinstance(x, tuple)]

    def tcopy(out, in_):
        op("V", lambda: g.vector.tensor_copy(out[0], in_[0]), out, [in_])

    def tt(out, a, b, o):
        op("V", lambda: g.vector.tensor_tensor(out[0], a[0], b[0], o), out, [a, b])

    def ts(out, a, s1, o1, s2=None, o2=None):
        if o2 is None:
            op("V", lambda: g.vector.tensor_scalar(out[0], a[0], val(s1), None, o1), out, [a] + opnds(s1))
        else:
            op("V", lambda: g.vector.tensor_scalar(out[0], a[0], val(s1), val(s2), o1, o2), out, [a] + opnds(s1, s2))

    def scan(out, a, b, o1, o2):
        op("V", lambda: g.vector.tensor_tensor_scan(out[0], a[0], b[0], 0.0, o1, o2), out, [a, b])

    def fill(out, c):
        op("V", lambda: g.vector.memset(out[0], c), out, [])

    def act(out, in_, f, bias=0.0, scale=1.0):
        op("S", lambda: g.scalar.activation(out[0], in_[0], f, bias=val(bias), scale=val(scale)), out, [in_] + opnds(bias, scale))

    def mm(out, l, r, st, sp):
        op("T", lambda: g.tensor.matmul(out[0], l[0], r[0], st, sp), out, [l, r], acc=not st, done=sp)

    def iota(out, pat, base, cm):
        op("G", lambda: g.iota(out[0], pat, base, cm, allow_small_or_imprecise_dtypes=True), out, [])

    def col(i):
        return B("cols", i, i + 1)

    def ci(i):
        return B("ci", i, i + 1)

    def L(name, j):
        return B(name, 15 - j, 143 - j)

    def convert(a, b):
        tcopy(B("Kw", V + a, V + b), B("ki", a, b))

    dma("Y", B("ki", 0, HALF), ext(T.kin[:, 0:HALF]))
    dma("Y", B("own_s"), ext(T.own[:]))
    dma("Y", B("ki", HALF, V), ext(T.kin[:, HALF:V]))
    dma("Y", B("Xw", 0, V), ext(T.x[:]))
    dma("Y", B("PR0"), ext(T.price[:]))
    dma("Y", B("wall_s"), ext(T.wall[:]))
    dma("Y", B("hold_s"), ext(T.hold[:]))
    dma("Y", B("wt_s"), ext(T.wt[:]))

    RB = V // 4
    iota(ci(6), [[0, 1]], 0, 1)
    iota(B("s1"), [[16, 13]], 0, 0)
    iota(B("crow"), [[1, 144]], 0, 0)
    iota(B("qrow"), [[0, 12], [1, 17]], 0, 0)
    iota(B("jlrow"), [[0, 12], [1, 16]], 0, 0)
    iota(B("grow"), [[1, 8], [0, 16]], 0, 0)
    iota(B("dm0"), [[16, 12]], 2 * V + 8192, 0)
    iota(B("ramp", 0, RB), [[1, RB]], 0, 0)
    fill(B("cb", 0, 16), 0.0)
    fill(B("cb", 208, 224), 0.0)
    fill(B("tr", 416, 432), 0.0)
    fill(B("C16"), 16384.0)
    fill(R("eq", T.eq[:, :, :, 0], 0, P), 0.0)
    ts(ci(0), ci(6), 15, A.bitwise_and)
    ts(ci(1), ci(6), 4, A.logical_shift_right)
    ts(ci(2), ci(6), 1, A.bitwise_and)
    ts(ci(3), ci(6), 4, A.logical_shift_right, 1, A.bitwise_and)
    tcopy(col(9), ci(6))
    fill(B("Cm"), -32.0)
    tcopy(B("cols", 0, 4), B("ci", 0, 4))
    fill(B("RST"), -4096.0)
    ts(B("s1"), B("s1"), col(0), A.add, Q - 1.0, A.min)
    ts(col(13), col(1), 16.0, A.mult, 15.0, A.add)
    ts(col(8), col(0), 0.0, A.is_equal, -LOW, A.mult)
    ts(B("jI"), B("s1"), -8.0, A.add, 1.0 / 17, A.mult)
    ts(col(6), col(2), -1.0, A.mult, 1.0, A.add)
    ts(col(14), col(0), -1.0, A.mult, -1.0, A.add)
    ts(col(11), col(8), -1.0, A.mult, -BIG, A.add)
    ts(B("pI"), B("jI"), col(3), A.add)
    ts(B("s3"), B("jI"), 17.0, A.mult, 16.0, A.add)
    tt(B("s2"), B("s1"), B("jI"), A.subtract)
    ts(B("s4"), B("jI"), 416.0, A.add)
    ts(B("pI"), B("pI"), 1, A.bitwise_and)
    tt(B("s3"), B("s3"), B("s1"), A.is_equal)
    ts(B("L64"), B("crow"), col(13), A.is_equal, 64.0, A.mult)
    ts(B("s1"), B("pI"), 208.0, A.mult)
    tt(B("s4"), B("s4"), B("s3"), A.mult)
    ts(B("L32"), B("crow"), col(13), A.is_equal, -32.0, A.mult)
    tt(B("s2"), B("s2"), B("s1"), A.add)
    ts(B("ID"), B("crow", 0, 128), col(9), A.is_equal)
    fill(B("RST", 0, Q, 17), 2.0 ** 26)
    tt(B("s2"), B("s2"), B("s4"), A.max)
    act(B("c3a"), B("qrow"), F.Abs, bias=col(14))
    act(B("c3b"), B("qrow"), F.Abs, scale=-1.0, bias=col(0))
    act(B("two"), B("qrow"), F.Relu, scale=-2.0, bias=2.0)
    act(B("c3a"), B("c3a"), F.Relu, scale=-1.0, bias=1.0)
    act(B("c3b"), B("c3b"), F.Relu, scale=-1.0, bias=1.0)
    act(B("ID2"), B("ID"), F.Identity, scale=2048.0)
    act(B("NID"), B("ID"), F.Identity, scale=-1.0)
    act(B("ID1"), B("ID"), F.Identity, scale=1024.0)
    act(B("C260"), B("Cm"), F.Identity, scale=8.125)
    ts(B("c3t"), B("jlrow"), col(0), A.is_lt, -LOW, A.mult)
    ts(B("PP", 0, P), B("jlrow"), col(0), A.is_equal, BIG, A.mult)
    tcopy(B("SELk", 0, 13), B("s2"))
    ts(B("BO"), B("grow"), col(1), A.is_equal, -1.0, A.mult)
    act(B("WKB"), B("BO"), F.Identity, scale=col(14))
    tt(B("C4"), B("PP", 0, P), B("c3t"), A.add)
    ts(B("dm0"), B("dm0"), col(0), A.add, -1.0 / 8192, A.mult)
    mm(B("CN", 0, Q), B("ID"), B("c3a"), True, False)
    mm(B("CN", 0, Q), B("NID"), B("c3b"), False, True)
    act(B("C3"), B("CN", 0, Q), F.Copy)
    act(B("cB"), B("C3", 16, Q, 17), F.Copy)
    act(B("c15"), B("C4", 15, P, 16), F.Identity, bias=col(8))
    act(B("C4", 15, P, 16), B("c15"), F.Copy)
    tcopy(B("E0"), B("own_s"))
    convert(0, HALF)
    tt(B("cA"), B("C3", 0, Q, 17), B("dm0"), A.add)
    act(B("ramp", RB, 2 * RB), B("ramp", 0, RB), F.Identity, bias=float(RB))
    need("Y", B("wt_s")[1], [], False)
    dma("Y", B("Hw", V, V + HALF), B("ramp", 0, HALF))
    op("G", lambda: g.affine_select(T.U[:], T.BO[:], [[1, 128]], A.is_gt, 0.0, 0, -1), B("U"), [B("BO")])
    iota(B("ramp", V, 2 * V), [[1, V]], V, 0)
    iota(B("Hw", 2 * V, W + 16), [[0, P + 16]], 0, 0)

    nxt = cores[(rank + 1) % n]
    prv = cores[(rank - 1) % n]
    home = cores[(rank - (NS - 1)) % n]
    away = cores[(rank + NS - 1) % n]
    XW, KW, HS = B("Xw", 0, V), B("Kw", V, 2 * V), B("Hw", V, W + 16)

    YB = ("Y0", "Y1", "Y0", "Y1", "Y0")

    def sums(i):
        mm(B(YB[i]), B("WKB"), B("Kw", V + 512 * i, V + 512 * i + 512), True, True)

    def sums_out(i):
        act(B("Yw", V + 512 * i, V + 512 * i + 512), B(YB[i]), F.Copy)

    def moving(c, buf, j):
        return R(buf, T[buf][:, 4 * c:4 * c + 4, 16 * j:16 * j + 16], 16 * c, 16 * c + 16)

    def part(name, c):
        return B(name, 68 * c, 68 * c + 68)

    def Z(c, i, w=17):
        name = ("ZA", "ZB", "ZC")[c]
        return R(name, T[name][:, 4 * i:4 * i + 4, 0:w], 4 * i, 4 * i + 4)

    def linear(c):
        mm(Z(c, 0), B("ID"), B("C16"), True, False)
        for j in range(16):
            mm(Z(c, 0, 16), L("L32", j), moving(c, "wk", j), False, False)

    def greater(c):
        for k in range(16):
            tt(R("tk", T.tk[:, 4 * c:4 * c + 4, k::16], 16 * c + k, 16 * c + k + 1),
               R("wk", T.wk[:, 4 * c:4 * c + 4, k::16], 16 * c, 16 * c + 16), B("PP", 64 * c, 64 * c + 64), A.max)

    def maxima(c):
        for j in range(16):
            mm(Z(c, 0, 16), L("L64", j), moving(c, "tk", j), False, j == 15)

    def decode(c):
        return [lambda: ts(part("rA", c), Z(c, 0), RND, A.add, RND, A.subtract),
                lambda: tt(Z(c, 1), Z(c, 0), part("rA", c), A.is_lt),
                lambda: tt(part("z1", c), Z(c, 1), part("K0", c), A.add),
                lambda: tt(part("z0", c), Z(c, 0), part("rA", c), A.is_ge),
                lambda: tt(Z(c, 2), Z(c, 1), part("rA", c), A.mult),
                lambda: tt(part("keys", c), Z(c, 2), part("K1", c), A.add)]

    def back(name, a, b):
        return R(name, T[name][:, b - 1:a - 1:-1] if a else T[name][:, b - 1::-1], a, b)

    late = []
    for t in range(NS):
        jub = t % 2 == 1
        last = t == NS - 1
        ofn = "of%d" % (t % 2)
        EU, PR, HW, OF = "E%d" % t, "PR%d" % t, "HW%d" % t, B(ofn)
        EO, PO, HN = "EO%d" % t, "PO%d" % t, "HW%d" % (t + 1)
        hh, wall = B(HW), B("wl%d" % (t | 1))
        SS = "CN" if last else "XB"
        nj = NJ if last else 16
        ws = P // nj
        half = 0.5 if t == 2 else 0.0
        if t:
            arrive(EU, 0, 12, prv, "re%d" % t)
            arrive(PR, 0, P, prv, "rp%d" % t)
            arrive(HW, 0, 12, prv, "rh%d" % t)
            if jub:
                arrive("wl%d" % t, 0, 12, cores[(rank - t) % n], "rw%d" % t)
        kw = KW if t else B("ki")
        tcopy(B("cbu", 0, 64), IND(kw, B(EU, 0, 4)))
        tcopy(B("cbu", 64, P), IND(kw, B(EU, 4, 12)))
        blocks = [(R("wk", T.wk[:, a, :], 4 * a, 4 * a + 4), IND(XW, B("cbu", 16 * a, 16 * a + 16))) for a in range(12)]
        for o, i in blocks[0:2] + blocks[4:6] + blocks[8:]:
            act(o, i, F.Identity, scale=2048.0)
        if t:
            act(B("cb", 16, 208), IND(KW, B(EU)), F.Copy)
        else:
            act(B("ramp", HALF, V), B("ramp", 0, HALF), F.Identity, bias=float(HALF))
            dma("Y", B("Hw", V + HALF, 2 * V), B("ramp", HALF, V))
            tcopy(B("cb", 16, 208), B("cbu"))
            convert(HALF, EARLY)
            send(nxt, B("wl1"), B("wall_s"), "rw1")
            send(away, B("wl3"), B("wall_s"), "rw3")
        for o, i in blocks[2:4] + blocks[6:8]:
            ts(o, i, 2048.0, A.mult)
        act(B("q"), B(PR), F.Identity, bias=129.625 - 65 * half, scale=0.25 - half / 4)
        mm(B("PP", 0, P), B("ID"), B("Cm"), True, False)
        if half:
            mm(B("PP", 0, P), B("ID1"), B("C260"), False, False)
        mm(B("PP", 0, P), B("ID1" if half else "ID2"), B(PR), False, True)
        linear(0)
        linear(1)
        greater(0)
        maxima(0)
        greater(1)
        linear(2)
        maxima(1)
        greater(2)
        maxima(2)
        if last:
            sums_out(2)
            sums_out(3)
        if t >= 2:
            sums(4 * (t - 2))
        op("V", lambda: g.vector.transpose(T.tr[:, 0:192], T.cb[:, 16:208]), B("tr", 0, 192), [B("cb", 16, 208)])
        op("V", lambda: g.vector.transpose(T.tr[:, 192:416], T.cb[:, 0:224]), B("tr", 192, 416), [B("cb")])
        eF = B("tr", 416, 428)
        ts(eF, B(EU), float(V), A.add)
        act(B("K0"), IND(B("tr"), B("SELk", 0, 13)), F.Identity, scale=1.0 / 8192)
        act(B("K1"), B("K0", 0, Q), F.Identity, scale=8192.0, bias=-OFF)
        act(B("ce"), B("cb", 16, 208), F.Identity, scale=col(6))
        d0, d1, d2 = decode(0), decode(1), decode(2)
        for f in (d0[0], d1[0], d0[1], d1[1], d2[0], d0[3], d1[3], d2[1], d2[3], d0[2], d1[2], d2[2], d0[4]):
            f()
        side = late
        late = []
        if t == 0:
            side = [lambda a=a: convert(a, a + 128) for a in range(EARLY, V, 128)]
        if jub:
            side = [lambda: (ts(B("nw"), wall, 2.0 * V + P, A.mult), tt(B("th"), B("bI"), hh, A.subtract)),
                    lambda: (tt(B("nw"), B("nw"), eF, A.max), tt(B("th"), B("th"), wall, A.mult), tt(B("hW"), hh, wall, A.mult)),
                    lambda: ts(B("EW"), B("nw"), -float(V), A.add),
                    lambda: (tt(B("th"), B("th"), B("wF"), A.mult), tt(B("hW"), B("hW"), B("c15"), A.add))]

        def fillers():
            if side:
                side.pop(0)()
        scan(back("sz", 0, 136), back("z0", 0, 136), back("z1", 0, 136), A.add, A.min)
        scan(back("sz", 136, Q), back("z0", 136, Q), back("z1", 136, Q), A.add, A.min)
        d1[4]()
        d2[4]()
        d0[5]()
        zf = B("sz", 0, Q, 17)
        ts(B("dkU"), zf, 8192.0, A.mult)
        d1[5]()
        d2[5]()
        tt(B("C3", 0, Q, 17), B("cA"), zf, A.add)
        tcopy(B("dkf"), IND(B("ramp"), B("dkU")))
        scan(B("sk"), B("RST"), B("keys"), A.add, A.min)
        mm(B("CN", 0, Q), B("ID"), B("two"), True, False)
        for j in range(12):
            op("V", lambda: g.vector.tensor_scalar(T.eq[:, j, 0:12 - j, 1:17], T.dkf[:, 16 * j:P], 1.0 / 8192, T.sz[:, 17 * j:17 * j + 1],
                                                   A.mult, A.is_equal), R("eq", None, 16 * j, 16 * j + 16), [B("dkf"), zf])
            if j == 7:
                tcopy(B("KEY"), B("sk", 15, Q, 17))
            if j < 11:
                mm(B("CN", 17 * j + 17, Q), B("BO"), R("eq", T.eq[:, j, 1:12 - j, :], 16 * j, 16 * j + 16), False, False)
            if j == 7:
                mm(B("CN", 0, 136), B("U"), R("eq", T.eq[:, 0:8, 0, :], 0, 128), False, False)
        mm(B("CN", 136, Q), B("U"), R("eq", T.eq[:, 8:12, 0, :], 128, P), False, True)
        ts(B("bI"), B("KEY"), 4095, A.bitwise_and)
        tt(B("C3", 16, Q, 17), B("cB"), zf, A.subtract)
        if not jub:
            fillers()
        tcopy(B("bU"), B("bI"))
        act(B("bF"), IND(B("ramp", 0, V), B("bU")), F.Copy)
        act(B("Xb"), IND(XW, B("bU")), F.Copy)
        fillers()
        scan(B("sc3"), B("CN", 0, Q), B("C3"), A.max, A.add)
        h0 = hh if t else B("hold_s")
        if t == 0:
            tt(B("th"), B("bI"), h0, A.subtract)
        fillers()
        oy = B("sc3", 16, Q, 17)
        ts(OF, oy, -1.0, A.add, -8192.0, A.mult)
        ts(B("wU"), oy, 1.0 - V / 8192, A.is_gt)
        ts(B("wF"), oy, 1.0 - V / 8192, A.is_gt)
        fillers()
        mm(B("XB", 0, P), B("ID"), B("Xb"), True, False)
        mm(B("XB", 0, P), B("NID"), B("q"), False, True)
        act(B("wb"), IND(B("ramp", 0, 16), B("wU")), F.Identity, scale=1.0 + 2 * half)
        act(B("xr"), B("XB", 0, P), F.Relu, bias=130.0)
        if t == 2:
            sums(1)
        tcopy(IND(B("Hw", 0, W), OF), B("bF"))
        while side:
            fillers()
        act(B("hm"), IND(HS, B("EW" if jub else EU)), F.Copy)
        act(B("Fo"), IND(KW, B("bU")), F.Identity, scale=col(2))
        if last:
            dma("Y", ext(T.yh[:]), B("Hw", V, 2 * V, parts=(0, 128, 16)))
        mm(B("PP", 0, P), B("ID"), B("wb"), True, False)
        mm(B("PP", 0, P), B("ID"), B(PR), False, True)
        act(B("p15"), B("PP", 0, P), F.Relu, bias=15.0 + 260 * half, scale=half - 1.0)
        if t != 1:
            act(B("pw" if jub else PO), B("p15"), F.Identity, bias=274.5 if jub else 15.0, scale=-1.0)
        if t >= 2:
            sums_out(4 * (t - 2))
        if jub:
            tt(B("C4", 15, P, 16), B("th"), B("hW"), A.add)
        tcopy(IND(B("Xw"), B(ofn, 0, XH)), B("xr", 0, 16 * XH))
        if t == 2:
            tt(B("th"), B("bI"), h0, A.subtract)
        elif t == 0:
            tt(B("th"), B("th"), B("wF"), A.mult)
        if last:
            for j in range(nj):
                mm(B(SS, 0, ws), L("Lw", 16 // nj * j), B("C260", 0, ws), j == 0, False)
        if t >= 2:
            yv = "yv%d" % t
            mm(B("XB", 0, P), B("WKB"), B("Fo"), True, False)
            mm(B("XB", 0, P), B("WKB"), B("ce"), False, True)
            act(B(yv), B("XB", 0, P), F.Copy)
        if t == 2:
            sums_out(1)
        scan(B("sc"), B("hm"), B("C4"), A.max, A.add)
        el = B("sc", 15, P, 16)

        def wealth():
            tcopy(IND(B("Xw"), B(ofn, XH, 12)), B("xr", 16 * XH, P))

        def kin():
            tt(IND(B("Kw"), OF), B("Fo"), B("ce"), A.add)
        if last:
            wealth()
        elif t == 2:
            tt(B("th"), B("th"), B("wF"), A.mult)
        elif t == 0:
            tt(hh, B("th"), h0, A.add)
        ts(B(EO), el, col(11), A.add)
        if t == 1:
            act(B("C4", 15, P, 16), B("c15"), F.Copy)
        if last:
            send(home, B("rE"), B(EO), "rg")
        else:
            send(nxt, B("E%d" % (t + 1)), B(EO), "re%d" % (t + 1))
        if not jub:
            send(nxt, B("PR%d" % (t + 1)), B(PO), "rp%d" % (t + 1))
            kin()
            if t == 2:
                tt(hh, B("th"), h0, A.add)
                sums(2)
                sums(3)
            wealth()
            send(nxt, B(HN), hh, "rh%d" % (t + 1))
            if t == 0:
                ts(col(7), B("wt_s"), -1.0 / 32, A.mult)
                act(B("Lw"), B("L32"), F.Identity, scale=col(7))
        else:
            if last:
                dma("Y", ext(T.yx[:, 0:HALF]), B("Xw", 0, HALF))
                tt(B(PO), IND(XW, B(EO)), B("pw"), A.add)
                tcopy(IND(B("Yw"), B("of0", 0, 8)), B("yv2", 0, 128))
            else:
                wealth()
                kin()
                act(B("Xb"), IND(XW, B(EO)), F.Copy)
                mm(B("XB", 0, P), B("NID"), B("p15"), True, False)
                mm(B("XB", 0, P), B("ID"), B("Xb"), False, True)
                act(B(PO), B("XB", 0, P), F.Identity, bias=274.5)
                send(nxt, B("PR%d" % (t + 1)), B(PO), "rp%d" % (t + 1))
                for j in range(16):
                    mm(B(SS, 0, 12), L("Lw", j), B("C260", 0, 12), j == 0, False)
            for j in range(nj):
                rhs = B(PO, ws * j, ws * j + ws) if last else B(PO, j, P, 16)
                mm(B(SS, 0, ws), L("Lw", 16 // nj * j), rhs, False, j == nj - 1)
            late = [lambda SS=SS, ws=ws: ts(B("sI", 0, ws), B(SS, 0, ws), 0.5, A.mult),
                    lambda SS=SS, ws=ws: ts(B("sI", ws, 2 * ws), B(SS, 0, ws), 0.5, A.mult, -float(V), A.add),
                    lambda ws=ws: ts(B("uI", 0, 2 * ws), B("sI", 0, 2 * ws), 4095, A.bitwise_and)]
            if last:
                for f in late:
                    f()
                tt(B("hh"), B("uI", 0, ws), B("uI", ws, 2 * ws), A.min)
                send(home, B("rh"), B("hh"), "rf")
                need("Y", B("hh")[1], [], False)
                dma("Y", ext(T.yx[:, HALF:V]), B("Xw", HALF, V))
                tcopy(IND(B("Yw"), B("of0", 8, 12)), B("yv2", 128, P))
                tcopy(IND(B("Yw"), OF), B("yv3"))
                dma("Y", ext(T.yk[:]), B("Yw", V, 2 * V, parts=(0, 128, 16)))
            else:
                late += [lambda hh=hh, HN=HN, HW=HW: (tt(hh, B("uI", 0, 12), B("uI", 12, 24), A.min), send(nxt, B(HN), B(HW), "rh2"))]
    arrive("rE", 0, 12, away, "rg")
    act(B("outf"), IND(B("ramp", 0, V), B("rE")), F.Copy)
    dma("S", ext(T.yo[:]), B("outf", 0, P, parts=(0, 128, 16)))
    arrive("rh", 0, P // NJ, away, "rf")
    dma("Y", ext(T.yt[:]), B("rh", parts=(0, 128, 16 // NJ)))
    for q in "GTVS":
        g.wait_ge(T.sem["q" + q], cnt[q])
    g.wait_ge(T.sem["ls"], sent[0])
    for i in range(ndma[0]):
        g.wait_ge(T.sem["dm%d" % i], 16)
